import numpy as np
import ml_dtypes


def mxq(x, axis, fmt="e4m3"):
    dtype, down = {"e4m3": (ml_dtypes.float8_e4m3fn, 7), "e5m2": (ml_dtypes.float8_e5m2, 14)}[fmt]
    v = np.moveaxis(np.asarray(x, np.float32).astype(ml_dtypes.bfloat16).astype(np.float64), axis, -1)
    blocks = v.reshape(v.shape[:-1] + (-1, 32))
    amax = np.abs(blocks).max(-1, keepdims=True)
    byte = np.maximum(np.where(amax > 0, np.frexp(amax)[1] - 1 + 127, 0) - down, 1)
    scale = np.exp2(byte - 127.0)
    codes = (blocks / scale).astype(np.float32).astype(dtype).astype(np.float64)
    return np.moveaxis((codes * scale).reshape(v.shape), -1, axis)


WIDE = False


def mx_kscale(k):
    if not WIDE:
        return np.ones(k)
    levels = np.array([10, -10, 5, -5, 0])
    if k % 512:
        return np.exp2(np.random.permutation(np.resize(levels, k // 32))).repeat(32)
    a = np.empty((k // 512, 16))
    for p in range(k // 512):
        a[p, :8] = np.random.permutation(np.resize(levels, 8))
        for g in range(8):
            far = levels[np.abs(levels - a[p, g]) >= 10]
            a[p, g + 8] = far[np.random.randint(len(far))]
    return np.exp2(a.ravel()).repeat(32)


def f64(x):
    return np.asarray(x).astype(np.float64)


def striped(idx):
    return np.tile(idx.reshape(-1, 16).T, (8, 1)).astype(np.uint16)


def unstriped(offs):
    return offs[:16].T.reshape(-1).astype(np.int64)


def striped8(idx):
    return np.concatenate([x.reshape(-1, 16).T for x in idx]).astype(np.uint16)


def runs(offs, k):
    lists = np.stack([offs[16 * r : 16 * r + 16].T.reshape(-1) for r in range(8)]).astype(np.int64)
    return lists[np.arange(k) % 512 // 64]


def pack_weight(w):
    k, n = w.shape
    w = f64(np.asarray(w, np.float32).astype(ml_dtypes.bfloat16)).reshape(k // 32, 32, n)
    amax = np.abs(w).max(1)
    byte = np.clip(np.where(amax > 0, np.frexp(amax)[1] - 1 + 127 - 7, 1), 1, 254)
    scaled = (w * np.exp2(127.0 - byte)[:, None, :]).reshape(k, n).astype(np.float32)
    words = np.ascontiguousarray(scaled.reshape(k // 512, 128, 4, n).transpose(0, 1, 3, 2)).astype(ml_dtypes.float8_e4m3fn).view(np.uint8)
    return words, np.ascontiguousarray(byte.astype(np.uint8).reshape(k // 512, 16, n))


def unpack_weight(words, scales):
    g, p, n, _ = words.shape
    vals = np.ascontiguousarray(words).view(ml_dtypes.float8_e4m3fn).astype(np.float64) * np.repeat(np.exp2(scales.astype(np.float64) - 127.0), 8, axis=1)[..., None]
    return vals.transpose(0, 1, 3, 2).reshape(g * 512, n)

def planes(y):
    n, m = y.shape
    v = y.astype(np.float32).astype(ml_dtypes.bfloat16).astype(np.float64).reshape(n // 32, 32, m)
    top = np.abs(v).max(1)
    byte = np.clip(np.where(top > 0, np.frexp(top)[1] - 1 + 127 - 7, 1), 1, 254)
    codes = (v * np.exp2(127.0 - byte)[:, None, :]).reshape(n, m).astype(np.float32).astype(ml_dtypes.float8_e4m3fn).view(np.uint8)
    words = codes.reshape(n // 512, 128, 4, m).transpose(0, 1, 3, 2)
    return np.ascontiguousarray(words), np.ascontiguousarray(byte.astype(np.uint8).reshape(n // 512, 16, m))


K, T, S, N, U = 512, 2048, 512, 512, 1024


def setup_inputs():
    n = np.random.standard_normal
    s = mx_kscale(K)[:, None]
    packed_xT = pack_weight(n((K, T)) * s)
    return {
        "x_words": packed_xT[0],
        "x_scales": packed_xT[1],
        "w1": (n((K, N)) / np.sqrt(K) / s).astype(np.float32),
        "par": n((N, U)).astype(np.float32),
        "sec": np.random.uniform(0.5, 2.0, (N, U)).astype(np.float32),
        "vmax": np.random.uniform(0.5, 2.5, (N, U)).astype(np.float32),
        "offs": striped(np.random.permutation(T)[:S]),
        "ent": striped8(np.stack([np.random.permutation(U)[:S] for _ in range(8)])),
    }


def reference(x_words, x_scales, w1, par, sec, vmax, offs, ent):
    xq = unpack_weight(x_words, x_scales)[:, unstriped(offs)]
    y = mxq(f64(w1), 0, "e4m3").T @ xq
    b = 0.875 * (f64(sec)[np.arange(N)[:, None], runs(ent, N)]) + 0.125 * ((y) ** 2)
    mx = np.maximum(b, f64(vmax)[np.arange(N)[:, None], runs(ent, N)])
    pn = f64(par)[np.arange(N)[:, None], runs(ent, N)] - (0.5 * (y / np.sqrt(mx)))
    out = f64(par).copy()
    out[np.arange(N)[:, None], runs(ent, N)] = pn
    return (out,) + planes(out)

@@ -1,0 +1,197 @@
+import math
+from contextlib import ExitStack
+
+import concourse.mybir as mybir
+
+F32 = mybir.dt.float32
+BF16 = mybir.dt.bfloat16
+I32 = mybir.dt.int32
+U32 = mybir.dt.uint32
+U16 = mybir.dt.uint16
+U8 = mybir.dt.uint8
+FP8X4 = mybir.dt.float8_e4m3fn_x4
+ALU = mybir.AluOpType
+ACT = mybir.ActivationFunctionType
+
+P = 128
+PACK = 4
+K, T, S, N, U = 512, 2048, 512, 512, 1024
+FLOPS = 2 * K * S * N
+CHUNK = 256
+W_SPLIT = 80
+PLANE_ORDER = (2, 0, 1, 3)
+
+
+def tile_picked_amsg8_none_po_kernel(
+    tc, x_words, x_scales, w1, par, sec, vmax, offs, ent, out_0, out_1, out_2
+):
+    nc = tc.nc
+    with ExitStack() as ctx:
+        lists = ctx.enter_context(tc.tile_pool(name="lists", bufs=1))
+        keep = ctx.enter_context(tc.tile_pool(name="keep", bufs=1))
+        psum = ctx.enter_context(tc.psum_pool(name="psum", bufs=1))
+
+        offs_sb = lists.tile([P, S // 16], U16, name="offs_sb")
+        ent_sb = lists.tile([P, S // 16], U16, name="ent_sb")
+        w_raw = keep.tile([P, PACK, N], F32, name="w_raw")
+        x_table = keep.tile([P, T], I32, name="x_table")
+        xs_table = keep.tile([P, T], U8, name="xs_table")
+        warm_in = keep.tile([P, 1], F32, name="warm_in")
+        warm_out = keep.tile([P, 1], F32, name="warm_out")
+
+        nc.gpsimd.memset(xs_table[:].bitcast(I32), 0)
+        nc.gpsimd.memset(warm_in[:], 1.0)
+        nc.sync.dma_start(offs_sb[:], offs)
+        nc.sync.dma_start(w_raw[:], w1.rearrange("(p j) c -> p j c", j=PACK))
+        for q in range(4):
+            nc.sync.dma_start(
+                xs_table[32 * q : 32 * q + 4, :].bitcast(I32),
+                x_scales[0, 4 * q : 4 * q + 4, :].bitcast(I32),
+            )
+        nc.scalar.activation(warm_out[:], warm_in[:], ACT.Abs_reciprocal_sqrt)
+        nc.sync.dma_start(x_table[:], x_words[0].rearrange("p c r -> p (c r)").bitcast(I32))
+        nc.sync.dma_start(ent_sb[:], ent)
+
+        par_rows = par.rearrange("(p t) u -> p t u", t=PACK)
+        sec_rows = sec.rearrange("(p t) u -> p t u", t=PACK)
+        vmax_rows = vmax.rearrange("(p t) u -> p t u", t=PACK)
+        out_rows = out_0.rearrange("(p t) u -> p t u", t=PACK)
+        par_sb, sec_sb, vmax_sb = {}, {}, {}
+        for t in PLANE_ORDER:
+            vmax_sb[t] = keep.tile([P, U], F32, name="vmax%d" % t)
+            sec_sb[t] = keep.tile([P, U], F32, name="sec%d" % t)
+            par_sb[t] = keep.tile([P, U], F32, name="par%d" % t)
+        a, b, c, d = PLANE_ORDER
+        for tiles, rows, t in (
+            (vmax_sb, vmax_rows, a),
+            (vmax_sb, vmax_rows, b),
+            (sec_sb, sec_rows, a),
+            (sec_sb, sec_rows, b),
+            (par_sb, par_rows, a),
+            (vmax_sb, vmax_rows, c),
+            (sec_sb, sec_rows, c),
+            (par_sb, par_rows, b),
+            (vmax_sb, vmax_rows, d),
+            (sec_sb, sec_rows, d),
+            (par_sb, par_rows, c),
+            (par_sb, par_rows, d),
+        ):
+            nc.sync.dma_start(tiles[t][:], rows[:, t, :])
+
+        xs_picked = keep.tile([P, S], U8, name="xs_picked", align_bytes=64)
+        nc.vector.tensor_copy(xs_picked[:], xs_table[:].indirect(offs_sb[:]))
+
+        w_grouped = keep.tile([P, N * PACK], BF16, name="w_grouped", align_bytes=64)
+        w_dealt = w_grouped[:].rearrange("p (t m j) -> p m j t", t=PACK, j=PACK)
+        w_rows = w_raw[:].rearrange("p j (m t) -> p m j t", t=PACK)
+        nc.vector.tensor_copy(w_dealt[:, :W_SPLIT], w_rows[:, :W_SPLIT])
+        nc.scalar.copy(w_dealt[:, W_SPLIT:], w_rows[:, W_SPLIT:])
+        w_codes = keep.tile([P, N], U32, name="w_codes", align_bytes=64)
+        w_scales = keep.tile([P, N], U8, name="w_scales", align_bytes=64)
+        nc.vector.quantize_mx(out=w_codes[:].bitcast(FP8X4), scales=w_scales[:], in_=w_grouped[:])
+
+        x_picked = keep.tile([P, S], U32, name="x_picked", align_bytes=64)
+        nc.vector.tensor_copy(x_picked[:], x_table[:].bitcast(U32).indirect(offs_sb[:]))
+
+        y, y_sq = {}, {}
+        for t in PLANE_ORDER:
+            y[t] = psum.tile([P, S], F32, name="y%d" % t)
+            cols = slice(t * P, (t + 1) * P)
+            nc.tensor.matmul_mx(
+                out=y[t][:],
+                lhsT=w_codes[:, cols].bitcast(FP8X4),
+                lhsT_scale=w_scales[:, cols],
+                rhs=x_picked[:].bitcast(FP8X4),
+                rhs_scale=xs_picked[:],
+                start=True,
+                stop=True,
+            )
+            y_sq[t] = keep.tile([P, S], F32, name="y_sq%d" % t)
+            nc.scalar.activation(y_sq[t][:], y[t][:], ACT.Square, scale=math.sqrt(0.125 / 0.875))
+
+        grouped = keep.tile([P, U * PACK], BF16, name="grouped", align_bytes=64)
+        grouped_t = grouped[:].rearrange("p (c t) -> p c t", t=PACK)
+        halves = [(slice(h * S // 2, (h + 1) * S // 2), slice(h * S // 32, (h + 1) * S // 32)) for h in range(2)]
+        vmax_g, moment, largest, rate, step, new = {}, {}, {}, {}, {}, {}
+
+        def gather_vmax(t):
+            vmax_g[t] = keep.tile([P, S], F32, name="vmax_g%d" % t)
+            nc.vector.tensor_copy(vmax_g[t][:], vmax_sb[t][:].indirect(ent_sb[:]))
+
+        def gather_sec(t):
+            moment[t] = keep.tile([P, S], F32, name="moment%d" % t)
+            for cols, part in halves:
+                nc.vector.tensor_tensor(moment[t][:, cols], sec_sb[t][:].indirect(ent_sb[:, part]), y_sq[t][:, cols], ALU.add)
+
+        def take_largest(t):
+            largest[t] = keep.tile([P, S], F32, name="largest%d" % t)
+            rate[t] = keep.tile([P, S], F32, name="rate%d" % t)
+            for cols, part in halves:
+                nc.vector.scalar_tensor_tensor(
+                    largest[t][:, cols], moment[t][:, cols], 0.875, vmax_g[t][:, cols], ALU.mult, ALU.max
+                )
+                nc.scalar.activation(rate[t][:, cols], largest[t][:, cols], ACT.Abs_reciprocal_sqrt, scale=4.0)
+
+        def make_step(t):
+            step[t] = keep.tile([P, S], F32, name="step%d" % t)
+            for cols, part in halves:
+                nc.vector.tensor_tensor(step[t][:, cols], y[t][:, cols], rate[t][:, cols], ALU.mult)
+
+        def gather_par(t):
+            new[t] = keep.tile([P, S], F32, name="new%d" % t)
+            nc.vector.tensor_tensor(new[t][:], par_sb[t][:].indirect(ent_sb[:]), step[t][:], ALU.subtract)
+
+        def scatter(t, last):
+            nc.vector.tensor_copy(par_sb[t][:].indirect(ent_sb[:]), new[t][:])
+            nc.sync.dma_start(out_rows[:, t, :], par_sb[t][:])
+            if not last:
+                nc.scalar.copy(grouped_t[:, :, t], par_sb[t][:])
+
+        gather_vmax(a)
+        gather_vmax(b)
+        gather_sec(a)
+        take_largest(a)
+        gather_sec(b)
+        make_step(a)
+        take_largest(b)
+        gather_par(a)
+        make_step(b)
+        scatter(a, False)
+        gather_vmax(c)
+        gather_sec(c)
+        take_largest(c)
+        gather_par(b)
+        make_step(c)
+        scatter(b, False)
+        gather_vmax(d)
+        gather_sec(d)
+        take_largest(d)
+        gather_par(c)
+        make_step(d)
+        scatter(c, False)
+        gather_par(d)
+        scatter(d, True)
+
+        out_codes = keep.tile([P, U], U32, name="out_codes", align_bytes=64)
+        out_scales = keep.tile([P, U], U8, name="out_scales", align_bytes=64)
+        chunks = [slice(i * CHUNK, (i + 1) * CHUNK) for i in range(U // CHUNK)]
+        for cols in chunks[:2]:
+            nc.vector.tensor_copy(grouped_t[:, cols, d], par_sb[d][:, cols])
+        for cols in chunks[2:]:
+            nc.scalar.copy(grouped_t[:, cols, d], par_sb[d][:, cols])
+        words_out = out_1[0].rearrange("p c r -> p (c r)").bitcast(I32)
+        for i, cols in enumerate(chunks):
+            nc.vector.quantize_mx(
+                out=out_codes[:, cols].bitcast(FP8X4),
+                scales=out_scales[:, cols],
+                in_=grouped[:, cols.start * PACK : cols.stop * PACK],
+            )
+            if i % 2 == 1:
+                half = slice(cols.start - CHUNK, cols.stop)
+                nc.sync.dma_start(words_out[:, half], out_codes[:, half].bitcast(I32))
+        for q in range(4):
+            queue = nc.scalar if q % 2 == 0 else nc.sync
+            queue.dma_start(
+                out_2[0, 4 * q : 4 * q + 4, :].bitcast(I32),
+                out_scales[32 * q : 32 * q + 4, :].bitcast(I32),
+            )

@@ -42,14 +42,14 @@ def tile_picked_amsg8_none_po_kernel(
         nc.gpsimd.memset(xs_table[:].bitcast(I32), 0)
         nc.gpsimd.memset(warm_in[:], 1.0)
         nc.sync.dma_start(offs_sb[:], offs)
-        nc.sync.dma_start(w_raw[:], w1.rearrange("(p j) c -> p j c", j=PACK))
+        nc.sync.dma_start(x_table[:], x_words[0].rearrange("p c r -> p (c r)").bitcast(I32))
         for q in range(4):
             nc.sync.dma_start(
                 xs_table[32 * q : 32 * q + 4, :].bitcast(I32),
                 x_scales[0, 4 * q : 4 * q + 4, :].bitcast(I32),
             )
         nc.scalar.activation(warm_out[:], warm_in[:], ACT.Abs_reciprocal_sqrt)
-        nc.sync.dma_start(x_table[:], x_words[0].rearrange("p c r -> p (c r)").bitcast(I32))
+        nc.sync.dma_start(w_raw[:], w1.rearrange("(p j) c -> p j c", j=PACK))
         nc.sync.dma_start(ent_sb[:], ent)
 
         par_rows = par.rearrange("(p t) u -> p t u", t=PACK)
@@ -67,17 +67,19 @@ def tile_picked_amsg8_none_po_kernel(
             (vmax_sb, vmax_rows, b),
             (sec_sb, sec_rows, a),
             (sec_sb, sec_rows, b),
-            (par_sb, par_rows, a),
             (vmax_sb, vmax_rows, c),
+            (par_sb, par_rows, a),
             (sec_sb, sec_rows, c),
-            (par_sb, par_rows, b),
             (vmax_sb, vmax_rows, d),
+            (par_sb, par_rows, b),
             (sec_sb, sec_rows, d),
-            (par_sb, par_rows, c),
             (par_sb, par_rows, d),
+            (par_sb, par_rows, c),
         ):
             nc.sync.dma_start(tiles[t][:], rows[:, t, :])
 
+        x_picked = keep.tile([P, S], U32, name="x_picked", align_bytes=64)
+        nc.vector.tensor_copy(x_picked[:], x_table[:].bitcast(U32).indirect(offs_sb[:]))
         xs_picked = keep.tile([P, S], U8, name="xs_picked", align_bytes=64)
         nc.vector.tensor_copy(xs_picked[:], xs_table[:].indirect(offs_sb[:]))
 
@@ -89,9 +91,6 @@ def tile_picked_amsg8_none_po_kernel(
         w_codes = keep.tile([P, N], U32, name="w_codes", align_bytes=64)
         w_scales = keep.tile([P, N], U8, name="w_scales", align_bytes=64)
         nc.vector.quantize_mx(out=w_codes[:].bitcast(FP8X4), scales=w_scales[:], in_=w_grouped[:])
-
-        x_picked = keep.tile([P, S], U32, name="x_picked", align_bytes=64)
-        nc.vector.tensor_copy(x_picked[:], x_table[:].bitcast(U32).indirect(offs_sb[:]))
 
         y, y_sq = {}, {}
         for t in PLANE_ORDER:
@@ -109,14 +108,25 @@ def tile_picked_amsg8_none_po_kernel(
             y_sq[t] = keep.tile([P, S], F32, name="y_sq%d" % t)
             nc.scalar.activation(y_sq[t][:], y[t][:], ACT.Square, scale=math.sqrt(0.125 / 0.875))
 
+        y_sb = {}
+        for t in PLANE_ORDER[1:]:
+            y_sb[t] = keep.tile([P, S], F32, name="y_sb%d" % t)
+            nc.scalar.activation(y_sb[t][:], y[t][:], ACT.Copy, scale=-1.0)
+
         grouped = keep.tile([P, U * PACK], BF16, name="grouped", align_bytes=64)
         grouped_t = grouped[:].rearrange("p (c t) -> p c t", t=PACK)
         halves = [(slice(h * S // 2, (h + 1) * S // 2), slice(h * S // 32, (h + 1) * S // 32)) for h in range(2)]
-        vmax_g, moment, largest, rate, step, new = {}, {}, {}, {}, {}, {}
+        half = S // 2
+        strip = keep.tile([P, 6 * half], F32, name="strip")
+        step = {t: strip[:, (i + 1) * half : (i + 3) * half] for i, t in enumerate(PLANE_ORDER)}
+        vmax_g = {c: strip[:, 0 : 2 * half], d: strip[:, half : 3 * half]}
+        for t in (a, b):
+            vmax_g[t] = keep.tile([P, S], F32, name="vmax_g%d" % t)[:]
+        par_g = strip[:, 2 * half : 4 * half]
+        moment, largest, rate, new = {}, {}, {}, {}
 
         def gather_vmax(t):
-            vmax_g[t] = keep.tile([P, S], F32, name="vmax_g%d" % t)
-            nc.vector.tensor_copy(vmax_g[t][:], vmax_sb[t][:].indirect(ent_sb[:]))
+            nc.vector.tensor_copy(vmax_g[t], vmax_sb[t][:].indirect(ent_sb[:]))
 
         def gather_sec(t):
             moment[t] = keep.tile([P, S], F32, name="moment%d" % t)
@@ -133,19 +143,20 @@ def tile_picked_amsg8_none_po_kernel(
                 nc.scalar.activation(rate[t][:, cols], largest[t][:, cols], ACT.Abs_reciprocal_sqrt, scale=4.0)
 
         def make_step(t):
-            step[t] = keep.tile([P, S], F32, name="step%d" % t)
-            for cols, part in halves:
-                nc.vector.tensor_tensor(step[t][:, cols], y[t][:, cols], rate[t][:, cols], ALU.mult)
+            if t in y_sb:
+                nc.gpsimd.tensor_tensor(step[t], y_sb[t][:], rate[t][:], ALU.mult)
+            else:
+                nc.vector.scalar_tensor_tensor(step[t], y[t][:], -1.0, rate[t][:], ALU.mult, ALU.mult)
 
         def gather_par(t):
             new[t] = keep.tile([P, S], F32, name="new%d" % t)
-            nc.vector.tensor_tensor(new[t][:], par_sb[t][:].indirect(ent_sb[:]), step[t][:], ALU.subtract)
+            for cols, part in halves:
+                nc.vector.tensor_tensor(new[t][:, cols], par_sb[t][:].indirect(ent_sb[:, part]), step[t][:, cols], ALU.add)
 
-        def scatter(t, last):
+        def scatter(t):
             nc.vector.tensor_copy(par_sb[t][:].indirect(ent_sb[:]), new[t][:])
             nc.sync.dma_start(out_rows[:, t, :], par_sb[t][:])
-            if not last:
-                nc.scalar.copy(grouped_t[:, :, t], par_sb[t][:])
+            nc.scalar.copy(grouped_t[:, :, t], par_sb[t][:])
 
         gather_vmax(a)
         gather_vmax(b)
@@ -156,21 +167,22 @@ def tile_picked_amsg8_none_po_kernel(
         take_largest(b)
         gather_par(a)
         make_step(b)
-        scatter(a, False)
         gather_vmax(c)
+        scatter(a)
         gather_sec(c)
         take_largest(c)
         gather_par(b)
         make_step(c)
-        scatter(b, False)
         gather_vmax(d)
+        scatter(b)
         gather_sec(d)
         take_largest(d)
         gather_par(c)
         make_step(d)
-        scatter(c, False)
-        gather_par(d)
-        scatter(d, True)
+        nc.vector.tensor_copy(par_g, par_sb[d][:].indirect(ent_sb[:]))
+        scatter(c)
+        nc.vector.tensor_tensor(par_sb[d][:].indirect(ent_sb[:]), par_g, step[d], ALU.add)
+        nc.sync.dma_start(out_rows[:, d, :], par_sb[d][:])
 
         out_codes = keep.tile([P, U], U32, name="out_codes", align_bytes=64)
         out_scales = keep.tile([P, U], U8, name="out_scales", align_bytes=64)
@@ -187,8 +199,8 @@ def tile_picked_amsg8_none_po_kernel(
                 in_=grouped[:, cols.start * PACK : cols.stop * PACK],
             )
             if i % 2 == 1:
-                half = slice(cols.start - CHUNK, cols.stop)
-                nc.sync.dma_start(words_out[:, half], out_codes[:, half].bitcast(I32))
+                pair = slice(cols.start - CHUNK, cols.stop)
+                nc.sync.dma_start(words_out[:, pair], out_codes[:, pair].bitcast(I32))
         for q in range(4):
             queue = nc.scalar if q % 2 == 0 else nc.sync
             queue.dma_start(

@@ -18,7 +18,6 @@ PACK = 4
 K, T, S, N, U = 512, 2048, 512, 512, 1024
 FLOPS = 2 * K * S * N
 CHUNK = 256
-W_SPLIT = 80
 PLANE_ORDER = (2, 0, 1, 3)
 
 
@@ -42,14 +41,15 @@ def tile_picked_amsg8_none_po_kernel(
         nc.gpsimd.memset(xs_table[:].bitcast(I32), 0)
         nc.gpsimd.memset(warm_in[:], 1.0)
         nc.sync.dma_start(offs_sb[:], offs)
-        nc.sync.dma_start(x_table[:], x_words[0].rearrange("p c r -> p (c r)").bitcast(I32))
+        nc.sync.dma_start(w_raw[:], w1.rearrange("(p j) c -> p j c", j=PACK))
         for q in range(4):
-            nc.sync.dma_start(
+            queue = nc.sync if q < 2 else nc.scalar
+            queue.dma_start(
                 xs_table[32 * q : 32 * q + 4, :].bitcast(I32),
                 x_scales[0, 4 * q : 4 * q + 4, :].bitcast(I32),
             )
         nc.scalar.activation(warm_out[:], warm_in[:], ACT.Abs_reciprocal_sqrt)
-        nc.sync.dma_start(w_raw[:], w1.rearrange("(p j) c -> p j c", j=PACK))
+        nc.sync.dma_start(x_table[:], x_words[0].rearrange("p c r -> p (c r)").bitcast(I32))
         nc.sync.dma_start(ent_sb[:], ent)
 
         par_rows = par.rearrange("(p t) u -> p t u", t=PACK)
@@ -64,9 +64,9 @@ def tile_picked_amsg8_none_po_kernel(
         a, b, c, d = PLANE_ORDER
         for tiles, rows, t in (
             (vmax_sb, vmax_rows, a),
-            (vmax_sb, vmax_rows, b),
             (sec_sb, sec_rows, a),
             (sec_sb, sec_rows, b),
+            (vmax_sb, vmax_rows, b),
             (vmax_sb, vmax_rows, c),
             (par_sb, par_rows, a),
             (sec_sb, sec_rows, c),
@@ -78,19 +78,20 @@ def tile_picked_amsg8_none_po_kernel(
         ):
             nc.sync.dma_start(tiles[t][:], rows[:, t, :])
 
-        x_picked = keep.tile([P, S], U32, name="x_picked", align_bytes=64)
-        nc.vector.tensor_copy(x_picked[:], x_table[:].bitcast(U32).indirect(offs_sb[:]))
-        xs_picked = keep.tile([P, S], U8, name="xs_picked", align_bytes=64)
-        nc.vector.tensor_copy(xs_picked[:], xs_table[:].indirect(offs_sb[:]))
-
-        w_grouped = keep.tile([P, N * PACK], BF16, name="w_grouped", align_bytes=64)
-        w_dealt = w_grouped[:].rearrange("p (t m j) -> p m j t", t=PACK, j=PACK)
         w_rows = w_raw[:].rearrange("p j (m t) -> p m j t", t=PACK)
-        nc.vector.tensor_copy(w_dealt[:, :W_SPLIT], w_rows[:, :W_SPLIT])
-        nc.scalar.copy(w_dealt[:, W_SPLIT:], w_rows[:, W_SPLIT:])
         w_codes = keep.tile([P, N], U32, name="w_codes", align_bytes=64)
         w_scales = keep.tile([P, N], U8, name="w_scales", align_bytes=64)
-        nc.vector.quantize_mx(out=w_codes[:].bitcast(FP8X4), scales=w_scales[:], in_=w_grouped[:])
+        w_grouped = [keep.tile([P, N * 2], BF16, name="w_grouped%d" % i, align_bytes=64) for i in range(2)]
+        w_dealt = [g[:].rearrange("p (t m j) -> p m j t", t=2, j=PACK) for g in w_grouped]
+        nc.vector.tensor_copy(w_dealt[1], w_rows[:, :, :, 2:4])
+        nc.scalar.copy(w_dealt[0], w_rows[:, :, :, 0:2])
+        xs_picked = keep.tile([P, S], U8, name="xs_picked", align_bytes=64)
+        nc.vector.tensor_copy(xs_picked[:], xs_table[:].indirect(offs_sb[:]))
+        for i in (1, 0):
+            cols = slice(i * 2 * P, (i + 1) * 2 * P)
+            nc.vector.quantize_mx(out=w_codes[:, cols].bitcast(FP8X4), scales=w_scales[:, cols], in_=w_grouped[i][:])
+        x_picked = keep.tile([P, S], U32, name="x_picked", align_bytes=64)
+        nc.vector.tensor_copy(x_picked[:], x_table[:].bitcast(U32).indirect(offs_sb[:]))
 
         y, y_sq = {}, {}
         for t in PLANE_ORDER:
@@ -105,16 +106,24 @@ def tile_picked_amsg8_none_po_kernel(
                 start=True,
                 stop=True,
             )
-            y_sq[t] = keep.tile([P, S], F32, name="y_sq%d" % t)
-            nc.scalar.activation(y_sq[t][:], y[t][:], ACT.Square, scale=math.sqrt(0.125 / 0.875))
 
         y_sb = {}
-        for t in PLANE_ORDER[1:]:
-            y_sb[t] = keep.tile([P, S], F32, name="y_sb%d" % t)
-            nc.scalar.activation(y_sb[t][:], y[t][:], ACT.Copy, scale=-1.0)
 
-        grouped = keep.tile([P, U * PACK], BF16, name="grouped", align_bytes=64)
-        grouped_t = grouped[:].rearrange("p (c t) -> p c t", t=PACK)
+        def square(t, into):
+            y_sq[t] = into
+            nc.scalar.activation(into[:], y[t][:], ACT.Square, scale=math.sqrt(0.125 / 0.875))
+
+        def negate(t, into):
+            y_sb[t] = into
+            nc.scalar.activation(into[:], y[t][:], ACT.Copy, scale=-1.0)
+
+        for t in (a, b):
+            square(t, keep.tile([P, S], F32, name="y_sq%d" % t))
+        for t in (a, b):
+            negate(t, keep.tile([P, S], F32, name="y_sb%d" % t))
+
+        grouped = [keep.tile([P, 2 * CHUNK * PACK], BF16, name="grouped%d" % i, align_bytes=64) for i in range(2)]
+        grouped_t = [g[:].rearrange("p (c t) -> p c t", t=PACK) for g in grouped]
         halves = [(slice(h * S // 2, (h + 1) * S // 2), slice(h * S // 32, (h + 1) * S // 32)) for h in range(2)]
         half = S // 2
         strip = keep.tile([P, 6 * half], F32, name="strip")
@@ -125,12 +134,15 @@ def tile_picked_amsg8_none_po_kernel(
         par_g = strip[:, 2 * half : 4 * half]
         moment, largest, rate, new = {}, {}, {}, {}
 
-        def gather_vmax(t):
-            nc.vector.tensor_copy(vmax_g[t], vmax_sb[t][:].indirect(ent_sb[:]))
+        whole = [(slice(0, S), slice(0, S // 16))]
 
-        def gather_sec(t):
+        def gather_vmax(t, parts=whole):
+            for cols, part in parts:
+                nc.vector.tensor_copy(vmax_g[t][:, cols], vmax_sb[t][:].indirect(ent_sb[:, part]))
+
+        def gather_sec(t, parts=halves):
             moment[t] = keep.tile([P, S], F32, name="moment%d" % t)
-            for cols, part in halves:
+            for cols, part in parts:
                 nc.vector.tensor_tensor(moment[t][:, cols], sec_sb[t][:].indirect(ent_sb[:, part]), y_sq[t][:, cols], ALU.add)
 
         def take_largest(t):
@@ -143,10 +155,7 @@ def tile_picked_amsg8_none_po_kernel(
                 nc.scalar.activation(rate[t][:, cols], largest[t][:, cols], ACT.Abs_reciprocal_sqrt, scale=4.0)
 
         def make_step(t):
-            if t in y_sb:
-                nc.gpsimd.tensor_tensor(step[t], y_sb[t][:], rate[t][:], ALU.mult)
-            else:
-                nc.vector.scalar_tensor_tensor(step[t], y[t][:], -1.0, rate[t][:], ALU.mult, ALU.mult)
+            nc.gpsimd.tensor_tensor(step[t], y_sb[t][:], rate[t][:], ALU.mult)
 
         def gather_par(t):
             new[t] = keep.tile([P, S], F32, name="new%d" % t)
@@ -156,15 +165,20 @@ def tile_picked_amsg8_none_po_kernel(
         def scatter(t):
             nc.vector.tensor_copy(par_sb[t][:].indirect(ent_sb[:]), new[t][:])
             nc.sync.dma_start(out_rows[:, t, :], par_sb[t][:])
-            nc.scalar.copy(grouped_t[:, :, t], par_sb[t][:])
+            for i in range(2):
+                nc.scalar.copy(grouped_t[i][:, :, t], par_sb[t][:, 2 * i * CHUNK : 2 * (i + 1) * CHUNK])
 
         gather_vmax(a)
-        gather_vmax(b)
         gather_sec(a)
         take_largest(a)
-        gather_sec(b)
+        square(c, moment[a])
+        negate(c, largest[a])
+        gather_sec(b, whole)
         make_step(a)
+        gather_vmax(b, halves)
         take_largest(b)
+        square(d, moment[b])
+        negate(d, largest[b])
         gather_par(a)
         make_step(b)
         gather_vmax(c)
@@ -187,20 +201,22 @@ def tile_picked_amsg8_none_po_kernel(
         out_codes = keep.tile([P, U], U32, name="out_codes", align_bytes=64)
         out_scales = keep.tile([P, U], U8, name="out_scales", align_bytes=64)
         chunks = [slice(i * CHUNK, (i + 1) * CHUNK) for i in range(U // CHUNK)]
-        for cols in chunks[:2]:
-            nc.vector.tensor_copy(grouped_t[:, cols, d], par_sb[d][:, cols])
-        for cols in chunks[2:]:
-            nc.scalar.copy(grouped_t[:, cols, d], par_sb[d][:, cols])
+        for i, cols in enumerate(chunks):
+            into = grouped_t[i // 2][:, chunks[i % 2], d]
+            if i < 2:
+                nc.vector.tensor_copy(into, par_sb[d][:, cols])
+            else:
+                nc.scalar.copy(into, par_sb[d][:, cols])
         words_out = out_1[0].rearrange("p c r -> p (c r)").bitcast(I32)
         for i, cols in enumerate(chunks):
             nc.vector.quantize_mx(
                 out=out_codes[:, cols].bitcast(FP8X4),
                 scales=out_scales[:, cols],
-                in_=grouped[:, cols.start * PACK : cols.stop * PACK],
+                in_=grouped[i // 2][:, (i % 2) * CHUNK * PACK : (i % 2 + 1) * CHUNK * PACK],
             )
-            if i % 2 == 1:
-                pair = slice(cols.start - CHUNK, cols.stop)
-                nc.sync.dma_start(words_out[:, pair], out_codes[:, pair].bitcast(I32))
+            if i > 0:
+                ready = slice(0 if i == 1 else cols.start, cols.stop)
+                nc.sync.dma_start(words_out[:, ready], out_codes[:, ready].bitcast(I32))
         for q in range(4):
             queue = nc.scalar if q % 2 == 0 else nc.sync
             queue.dma_start(

@@ -67,11 +67,11 @@ def tile_picked_amsg8_none_po_kernel(
             (sec_sb, sec_rows, a),
             (sec_sb, sec_rows, b),
             (vmax_sb, vmax_rows, b),
-            (vmax_sb, vmax_rows, c),
             (par_sb, par_rows, a),
+            (vmax_sb, vmax_rows, c),
             (sec_sb, sec_rows, c),
-            (vmax_sb, vmax_rows, d),
             (par_sb, par_rows, b),
+            (vmax_sb, vmax_rows, d),
             (sec_sb, sec_rows, d),
             (par_sb, par_rows, d),
             (par_sb, par_rows, c),
@@ -119,36 +119,34 @@ def tile_picked_amsg8_none_po_kernel(
 
         for t in (a, b):
             square(t, keep.tile([P, S], F32, name="y_sq%d" % t))
-        for t in (a, b):
-            negate(t, keep.tile([P, S], F32, name="y_sb%d" % t))
+        negate(b, keep.tile([P, S], F32, name="y_sb%d" % b))
 
         grouped = [keep.tile([P, 2 * CHUNK * PACK], BF16, name="grouped%d" % i, align_bytes=64) for i in range(2)]
         grouped_t = [g[:].rearrange("p (c t) -> p c t", t=PACK) for g in grouped]
         halves = [(slice(h * S // 2, (h + 1) * S // 2), slice(h * S // 32, (h + 1) * S // 32)) for h in range(2)]
         half = S // 2
-        strip = keep.tile([P, 6 * half], F32, name="strip")
-        step = {t: strip[:, (i + 1) * half : (i + 3) * half] for i, t in enumerate(PLANE_ORDER)}
-        vmax_g = {c: strip[:, 0 : 2 * half], d: strip[:, half : 3 * half]}
-        for t in (a, b):
-            vmax_g[t] = keep.tile([P, S], F32, name="vmax_g%d" % t)[:]
-        par_g = strip[:, 2 * half : 4 * half]
-        moment, largest, rate, new = {}, {}, {}, {}
-
         whole = [(slice(0, S), slice(0, S // 16))]
+        step, largest = {}, {}
+        largest[a] = keep.tile([P, S], F32, name="largest_first")[:]
+        for t, following in ((a, b), (b, c), (c, d)):
+            shared = keep.tile([P, 3 * half], F32, name="shared%d" % t)
+            largest[following] = shared[:, 0 : 2 * half]
+            step[t] = shared[:, half : 3 * half]
+        step[d] = keep.tile([P, S], F32, name="step_last")[:]
+        vmax_g, moment, rate, new = {}, {}, {}, {}
 
-        def gather_vmax(t, parts=whole):
-            for cols, part in parts:
-                nc.vector.tensor_copy(vmax_g[t][:, cols], vmax_sb[t][:].indirect(ent_sb[:, part]))
+        def gather_vmax(t):
+            vmax_g[t] = keep.tile([P, S], F32, name="vmax_g%d" % t)
+            nc.vector.tensor_copy(vmax_g[t][:], vmax_sb[t][:].indirect(ent_sb[:]))
 
-        def gather_sec(t, parts=halves):
+        def gather_sec(t, parts):
             moment[t] = keep.tile([P, S], F32, name="moment%d" % t)
             for cols, part in parts:
                 nc.vector.tensor_tensor(moment[t][:, cols], sec_sb[t][:].indirect(ent_sb[:, part]), y_sq[t][:, cols], ALU.add)
 
-        def take_largest(t):
-            largest[t] = keep.tile([P, S], F32, name="largest%d" % t)
+        def take_largest(t, parts):
             rate[t] = keep.tile([P, S], F32, name="rate%d" % t)
-            for cols, part in halves:
+            for cols, part in parts:
                 nc.vector.scalar_tensor_tensor(
                     largest[t][:, cols], moment[t][:, cols], 0.875, vmax_g[t][:, cols], ALU.mult, ALU.max
                 )
@@ -169,33 +167,34 @@ def tile_picked_amsg8_none_po_kernel(
                 nc.scalar.copy(grouped_t[i][:, :, t], par_sb[t][:, 2 * i * CHUNK : 2 * (i + 1) * CHUNK])
 
         gather_vmax(a)
-        gather_sec(a)
-        take_largest(a)
+        gather_sec(a, halves)
+        take_largest(a, halves)
         square(c, moment[a])
         negate(c, largest[a])
         gather_sec(b, whole)
-        make_step(a)
-        gather_vmax(b, halves)
-        take_largest(b)
-        square(d, moment[b])
-        negate(d, largest[b])
+        nc.vector.scalar_tensor_tensor(step[a], y[a][:], -1.0, rate[a][:], ALU.mult, ALU.mult)
+        gather_vmax(b)
         gather_par(a)
+        take_largest(b, whole)
         make_step(b)
-        gather_vmax(c)
+        square(d, moment[b])
+        negate(d, rate[a])
         scatter(a)
-        gather_sec(c)
-        take_largest(c)
+        gather_vmax(c)
+        gather_sec(c, whole)
         gather_par(b)
+        take_largest(c, whole)
         make_step(c)
-        gather_vmax(d)
         scatter(b)
-        gather_sec(d)
-        take_largest(d)
+        gather_vmax(d)
+        gather_sec(d, whole)
+        par_g = keep.tile([P, S], F32, name="par_g")
+        nc.vector.tensor_copy(par_g[:], par_sb[d][:].indirect(ent_sb[:]))
         gather_par(c)
+        take_largest(d, whole)
         make_step(d)
-        nc.vector.tensor_copy(par_g, par_sb[d][:].indirect(ent_sb[:]))
         scatter(c)
-        nc.vector.tensor_tensor(par_sb[d][:].indirect(ent_sb[:]), par_g, step[d], ALU.add)
+        nc.vector.tensor_tensor(par_sb[d][:].indirect(ent_sb[:]), par_g[:], step[d], ALU.add)
         nc.sync.dma_start(out_rows[:, d, :], par_sb[d][:])
 
         out_codes = keep.tile([P, U], U32, name="out_codes", align_bytes=64)

@@ -2,6 +2,7 @@ import math
 from contextlib import ExitStack
 
 import concourse.mybir as mybir
+from concourse.masks import make_identity
 
 F32 = mybir.dt.float32
 BF16 = mybir.dt.bfloat16
@@ -40,18 +41,8 @@ def tile_picked_amsg8_none_po_kernel(
 
         nc.gpsimd.memset(xs_table[:].bitcast(I32), 0)
         nc.gpsimd.memset(warm_in[:], 1.0)
-        nc.sync.dma_start(offs_sb[:], offs)
-        nc.sync.dma_start(w_raw[:], w1.rearrange("(p j) c -> p j c", j=PACK))
-        for q in range(4):
-            queue = nc.sync if q < 2 else nc.scalar
-            queue.dma_start(
-                xs_table[32 * q : 32 * q + 4, :].bitcast(I32),
-                x_scales[0, 4 * q : 4 * q + 4, :].bitcast(I32),
-            )
-        nc.scalar.activation(warm_out[:], warm_in[:], ACT.Abs_reciprocal_sqrt)
-        nc.sync.dma_start(x_table[:], x_words[0].rearrange("p c r -> p (c r)").bitcast(I32))
-        nc.sync.dma_start(ent_sb[:], ent)
-
+        identity = keep.tile([P, P], F32, name="identity")
+        make_identity(nc, identity[:])
         par_rows = par.rearrange("(p t) u -> p t u", t=PACK)
         sec_rows = sec.rearrange("(p t) u -> p t u", t=PACK)
         vmax_rows = vmax.rearrange("(p t) u -> p t u", t=PACK)
@@ -62,18 +53,29 @@ def tile_picked_amsg8_none_po_kernel(
             sec_sb[t] = keep.tile([P, U], F32, name="sec%d" % t)
             par_sb[t] = keep.tile([P, U], F32, name="par%d" % t)
         a, b, c, d = PLANE_ORDER
+        nc.sync.dma_start(ent_sb[:], ent)
+        nc.sync.dma_start(vmax_sb[a][:], vmax_rows[:, a, :])
+        nc.sync.dma_start(offs_sb[:], offs)
+        for q in range(4):
+            queue = nc.sync if q < 2 else nc.scalar
+            queue.dma_start(
+                xs_table[32 * q : 32 * q + 4, :].bitcast(I32),
+                x_scales[0, 4 * q : 4 * q + 4, :].bitcast(I32),
+            )
+        nc.scalar.activation(warm_out[:], warm_in[:], ACT.Abs_reciprocal_sqrt)
+        nc.sync.dma_start(w_raw[:], w1.rearrange("(p j) c -> p j c", j=PACK))
+        nc.sync.dma_start(par_sb[d][:], par_rows[:, d, :])
+        nc.sync.dma_start(x_table[:], x_words[0].rearrange("p c r -> p (c r)").bitcast(I32))
         for tiles, rows, t in (
-            (vmax_sb, vmax_rows, a),
+            (vmax_sb, vmax_rows, b),
             (sec_sb, sec_rows, a),
             (sec_sb, sec_rows, b),
-            (vmax_sb, vmax_rows, b),
-            (par_sb, par_rows, a),
             (vmax_sb, vmax_rows, c),
             (sec_sb, sec_rows, c),
+            (par_sb, par_rows, a),
+            (sec_sb, sec_rows, d),
             (par_sb, par_rows, b),
             (vmax_sb, vmax_rows, d),
-            (sec_sb, sec_rows, d),
-            (par_sb, par_rows, d),
             (par_sb, par_rows, c),
         ):
             nc.sync.dma_start(tiles[t][:], rows[:, t, :])
@@ -107,53 +109,74 @@ def tile_picked_amsg8_none_po_kernel(
                 stop=True,
             )
 
+        half = S // 2
         y_sb = {}
 
         def square(t, into):
             y_sq[t] = into
-            nc.scalar.activation(into[:], y[t][:], ACT.Square, scale=math.sqrt(0.125 / 0.875))
+            nc.scalar.activation(into, y[t][:], ACT.Square, scale=math.sqrt(0.125 / 0.875))
 
         def negate(t, into):
             y_sb[t] = into
-            nc.scalar.activation(into[:], y[t][:], ACT.Copy, scale=-1.0)
+            nc.scalar.activation(into, y[t][:], ACT.Copy, scale=-1.0)
 
         for t in (a, b):
-            square(t, keep.tile([P, S], F32, name="y_sq%d" % t))
-        negate(b, keep.tile([P, S], F32, name="y_sb%d" % b))
+            square(t, keep.tile([P, S], F32, name="y_sq%d" % t)[:])
+        negate(b, keep.tile([P, S], F32, name="y_second")[:])
 
-        grouped = [keep.tile([P, 2 * CHUNK * PACK], BF16, name="grouped%d" % i, align_bytes=64) for i in range(2)]
-        grouped_t = [g[:].rearrange("p (c t) -> p c t", t=PACK) for g in grouped]
-        halves = [(slice(h * S // 2, (h + 1) * S // 2), slice(h * S // 32, (h + 1) * S // 32)) for h in range(2)]
-        half = S // 2
-        whole = [(slice(0, S), slice(0, S // 16))]
-        step, largest = {}, {}
-        largest[a] = keep.tile([P, S], F32, name="largest_first")[:]
-        for t, following in ((a, b), (b, c), (c, d)):
-            shared = keep.tile([P, 3 * half], F32, name="shared%d" % t)
-            largest[following] = shared[:, 0 : 2 * half]
-            step[t] = shared[:, half : 3 * half]
+        grouped_all = keep.tile([P, 3, 2 * CHUNK * PACK], BF16, name="grouped_all", align_bytes=64)
+        grouped = [grouped_all[:, 0, :], grouped_all[:, 2, :]]
+        grouped_t = [g.rearrange("p (c t) -> p c t", t=PACK) for g in grouped]
+        grouped_both = grouped_all[:, 0:3:2, :].rearrange("p h (c t) -> p h c t", t=PACK)
+        clipped = grouped_all[:, 1, :].bitcast(F32)[:, 0:S]
+        halves = [(slice(h * half, (h + 1) * half), slice(h * S // 32, (h + 1) * S // 32)) for h in range(2)]
+        blocks = [slice(k * P, (k + 1) * P) for k in range(S // P)]
+        vmax_strip = keep.tile([P, 3 * half], F32, name="vmax_strip")
+        moment_strip = keep.tile([P, 3 * half], F32, name="moment_strip")
+        vmax_first = vmax_strip[:, half : 3 * half]
+        moment_first = moment_strip[:, half : 3 * half]
+        largest_first = keep.tile([P, S], F32, name="largest_first")
+        rate_first = keep.tile([P, S], F32, name="rate_first")
+        strip_first = keep.tile([P, 3 * half], F32, name="strip_first")
+        step = {a: strip_first[:, half : 3 * half], b: moment_first, c: vmax_first}
         step[d] = keep.tile([P, S], F32, name="step_last")[:]
-        vmax_g, moment, rate, new = {}, {}, {}, {}
+        moment = {b: keep.tile([P, S], F32, name="moment_second")[:], c: strip_first[:, 0:S]}
+        new, vmax_neg, rate, excess, largest, vmax_turned = {}, {}, {}, {}, {}, {}
+
+        def turn(bank, values, start, stop):
+            for k, block in enumerate(blocks):
+                nc.tensor.matmul(
+                    bank[:, block],
+                    values[:, block],
+                    identity[:],
+                    start=start and k == 0,
+                    stop=stop and k == len(blocks) - 1,
+                    is_transpose=True,
+                )
 
         def gather_vmax(t):
-            vmax_g[t] = keep.tile([P, S], F32, name="vmax_g%d" % t)
-            nc.vector.tensor_copy(vmax_g[t][:], vmax_sb[t][:].indirect(ent_sb[:]))
+            vmax_neg[t] = keep.tile([P, S], F32, name="vmax_neg%d" % t)
+            vmax_turned[t] = keep.tile([P, S], F32, name="vmax_turned%d" % t)
+            excess[t] = psum.tile([P, S], F32, name="excess%d" % t)
+            largest[t] = psum.tile([P, S], F32, name="largest%d" % t)
+            nc.vector.tensor_scalar(vmax_neg[t][:], vmax_sb[t][:].indirect(ent_sb[:]), -1.0 / 0.875, 0.0, ALU.mult, ALU.add)
+            turn(largest[t], vmax_neg[t], True, True)
+            turn(excess[t], vmax_neg[t], True, False)
+            nc.scalar.activation(vmax_turned[t][:], largest[t][:], ACT.Copy, scale=-1.0)
+            turn(largest[t], vmax_turned[t], True, False)
 
-        def gather_sec(t, parts):
-            moment[t] = keep.tile([P, S], F32, name="moment%d" % t)
-            for cols, part in parts:
-                nc.vector.tensor_tensor(moment[t][:, cols], sec_sb[t][:].indirect(ent_sb[:, part]), y_sq[t][:, cols], ALU.add)
+        def gather_sec(t):
+            nc.vector.tensor_tensor(moment[t], sec_sb[t][:].indirect(ent_sb[:]), y_sq[t], ALU.add)
 
-        def take_largest(t, parts):
-            rate[t] = keep.tile([P, S], F32, name="rate%d" % t)
-            for cols, part in parts:
-                nc.vector.scalar_tensor_tensor(
-                    largest[t][:, cols], moment[t][:, cols], 0.875, vmax_g[t][:, cols], ALU.mult, ALU.max
-                )
-                nc.scalar.activation(rate[t][:, cols], largest[t][:, cols], ACT.Abs_reciprocal_sqrt, scale=4.0)
+        def make_rate(t):
+            rate[t] = keep.tile([P, S], F32, name="rate%d" % t)[:]
+            turn(excess[t], moment[t], False, True)
+            nc.scalar.activation(clipped, excess[t][:], ACT.Relu)
+            turn(largest[t], clipped, False, True)
+            nc.scalar.activation(rate[t], largest[t][:], ACT.Abs_reciprocal_sqrt, scale=4.0 * 0.875)
 
         def make_step(t):
-            nc.gpsimd.tensor_tensor(step[t], y_sb[t][:], rate[t][:], ALU.mult)
+            nc.gpsimd.tensor_tensor(step[t], y_sb[t], rate[t], ALU.mult)
 
         def gather_par(t):
             new[t] = keep.tile([P, S], F32, name="new%d" % t)
@@ -163,37 +186,54 @@ def tile_picked_amsg8_none_po_kernel(
         def scatter(t):
             nc.vector.tensor_copy(par_sb[t][:].indirect(ent_sb[:]), new[t][:])
             nc.sync.dma_start(out_rows[:, t, :], par_sb[t][:])
-            for i in range(2):
-                nc.scalar.copy(grouped_t[i][:, :, t], par_sb[t][:, 2 * i * CHUNK : 2 * (i + 1) * CHUNK])
 
-        gather_vmax(a)
-        gather_sec(a, halves)
-        take_largest(a, halves)
-        square(c, moment[a])
-        negate(c, largest[a])
-        gather_sec(b, whole)
-        nc.vector.scalar_tensor_tensor(step[a], y[a][:], -1.0, rate[a][:], ALU.mult, ALU.mult)
-        gather_vmax(b)
-        gather_par(a)
-        take_largest(b, whole)
-        make_step(b)
-        square(d, moment[b])
-        negate(d, rate[a])
-        scatter(a)
-        gather_vmax(c)
-        gather_sec(c, whole)
-        gather_par(b)
-        take_largest(c, whole)
-        make_step(c)
-        scatter(b)
-        gather_vmax(d)
-        gather_sec(d, whole)
+        def round_plane(t):
+            both = par_sb[t][:].rearrange("p (h c) -> p h c", h=2)
+            for i in range(4):
+                cols = slice(i * P, (i + 1) * P)
+                nc.scalar.copy(grouped_both[:, :, cols, t], both[:, :, cols])
+
+        nc.vector.tensor_copy(vmax_first, vmax_sb[a][:].indirect(ent_sb[:]))
         par_g = keep.tile([P, S], F32, name="par_g")
         nc.vector.tensor_copy(par_g[:], par_sb[d][:].indirect(ent_sb[:]))
+        gather_vmax(b)
+        for cols, part in halves:
+            nc.vector.tensor_tensor(moment_first[:, cols], sec_sb[a][:].indirect(ent_sb[:, part]), y_sq[a][:, cols], ALU.add)
+        for cols, part in halves:
+            nc.vector.scalar_tensor_tensor(
+                largest_first[:, cols], moment_first[:, cols], 0.875, vmax_first[:, cols], ALU.mult, ALU.max
+            )
+            nc.scalar.activation(rate_first[:, cols], largest_first[:, cols], ACT.Abs_reciprocal_sqrt, scale=4.0)
+        gather_sec(b)
+        make_rate(b)
+        nc.vector.scalar_tensor_tensor(step[a], y[a][:], -1.0, rate_first[:], ALU.mult, ALU.mult)
+        square(c, moment_first)
+        gather_vmax(c)
+        negate(c, largest_first[:])
+        square(d, vmax_first)
+        negate(d, rate_first[:])
+        gather_par(a)
+        gather_sec(c)
+        make_step(b)
+        make_rate(c)
+        scatter(a)
+        round_plane(a)
+        gather_par(b)
+        moment[d] = moment_strip[:, 0:S]
+        gather_sec(d)
+        make_step(c)
+        scatter(b)
+        vmax_last = rate[c]
+        nc.vector.tensor_copy(vmax_last, vmax_sb[d][:].indirect(ent_sb[:]))
         gather_par(c)
-        take_largest(d, whole)
+        largest_last = vmax_strip[:, 0:S]
+        nc.vector.scalar_tensor_tensor(largest_last, moment[d], 0.875, vmax_last, ALU.mult, ALU.max)
+        rate[d] = keep.tile([P, S], F32, name="rate_last")[:]
+        nc.scalar.activation(rate[d], largest_last, ACT.Abs_reciprocal_sqrt, scale=4.0)
         make_step(d)
+        round_plane(b)
         scatter(c)
+        round_plane(c)
         nc.vector.tensor_tensor(par_sb[d][:].indirect(ent_sb[:]), par_g[:], step[d], ALU.add)
         nc.sync.dma_start(out_rows[:, d, :], par_sb[d][:])
 

@@ -33,7 +33,7 @@ def tile_picked_amsg8_none_po_kernel(
 
         offs_sb = lists.tile([P, S // 16], U16, name="offs_sb")
         ent_sb = lists.tile([P, S // 16], U16, name="ent_sb")
-        w_raw = keep.tile([P, PACK, N], F32, name="w_raw")
+        w_raw = [keep.tile([P, 2, N], F32, name="w_raw%d" % i) for i in range(2)]
         x_table = keep.tile([P, T], I32, name="x_table")
         xs_table = keep.tile([P, T], U8, name="xs_table")
         warm_in = keep.tile([P, 1], F32, name="warm_in")
@@ -63,10 +63,11 @@ def tile_picked_amsg8_none_po_kernel(
                 x_scales[0, 4 * q : 4 * q + 4, :].bitcast(I32),
             )
         nc.scalar.activation(warm_out[:], warm_in[:], ACT.Abs_reciprocal_sqrt)
-        nc.sync.dma_start(w_raw[:], w1.rearrange("(p j) c -> p j c", j=PACK))
-        nc.sync.dma_start(par_sb[d][:], par_rows[:, d, :])
         nc.sync.dma_start(x_table[:], x_words[0].rearrange("p c r -> p (c r)").bitcast(I32))
+        for i in range(2):
+            nc.sync.dma_start(w_raw[i][:], w1.rearrange("(p j) c -> p j c", j=PACK)[:, 2 * i : 2 * i + 2, :])
         for tiles, rows, t in (
+            (par_sb, par_rows, d),
             (vmax_sb, vmax_rows, b),
             (sec_sb, sec_rows, a),
             (sec_sb, sec_rows, b),
@@ -80,20 +81,21 @@ def tile_picked_amsg8_none_po_kernel(
         ):
             nc.sync.dma_start(tiles[t][:], rows[:, t, :])
 
-        w_rows = w_raw[:].rearrange("p j (m t) -> p m j t", t=PACK)
+        x_picked = keep.tile([P, S], U32, name="x_picked", align_bytes=64)
+        nc.vector.tensor_copy(x_picked[:], x_table[:].bitcast(U32).indirect(offs_sb[:]))
+        xs_picked = keep.tile([P, S], U8, name="xs_picked", align_bytes=64)
+        nc.vector.tensor_copy(xs_picked[:], xs_table[:].indirect(offs_sb[:]))
         w_codes = keep.tile([P, N], U32, name="w_codes", align_bytes=64)
         w_scales = keep.tile([P, N], U8, name="w_scales", align_bytes=64)
         w_grouped = [keep.tile([P, N * 2], BF16, name="w_grouped%d" % i, align_bytes=64) for i in range(2)]
         w_dealt = [g[:].rearrange("p (t m j) -> p m j t", t=2, j=PACK) for g in w_grouped]
-        nc.vector.tensor_copy(w_dealt[1], w_rows[:, :, :, 2:4])
-        nc.scalar.copy(w_dealt[0], w_rows[:, :, :, 0:2])
-        xs_picked = keep.tile([P, S], U8, name="xs_picked", align_bytes=64)
-        nc.vector.tensor_copy(xs_picked[:], xs_table[:].indirect(offs_sb[:]))
+        for i in range(2):
+            w_rows = w_raw[i][:].rearrange("p j (m t) -> p m j t", t=PACK)
+            nc.vector.tensor_copy(w_dealt[1][:, :, 2 * i : 2 * i + 2, :], w_rows[:, :, :, 2:4])
+            nc.scalar.copy(w_dealt[0][:, :, 2 * i : 2 * i + 2, :], w_rows[:, :, :, 0:2])
         for i in (1, 0):
             cols = slice(i * 2 * P, (i + 1) * 2 * P)
             nc.vector.quantize_mx(out=w_codes[:, cols].bitcast(FP8X4), scales=w_scales[:, cols], in_=w_grouped[i][:])
-        x_picked = keep.tile([P, S], U32, name="x_picked", align_bytes=64)
-        nc.vector.tensor_copy(x_picked[:], x_table[:].bitcast(U32).indirect(offs_sb[:]))
 
         y, y_sq = {}, {}
         for t in PLANE_ORDER:

@@ -67,17 +67,17 @@ def tile_picked_amsg8_none_po_kernel(
         for i in range(2):
             nc.sync.dma_start(w_raw[i][:], w1.rearrange("(p j) c -> p j c", j=PACK)[:, 2 * i : 2 * i + 2, :])
         for tiles, rows, t in (
-            (par_sb, par_rows, d),
             (vmax_sb, vmax_rows, b),
             (sec_sb, sec_rows, a),
             (sec_sb, sec_rows, b),
             (vmax_sb, vmax_rows, c),
             (sec_sb, sec_rows, c),
-            (par_sb, par_rows, a),
-            (sec_sb, sec_rows, d),
-            (par_sb, par_rows, b),
             (vmax_sb, vmax_rows, d),
+            (sec_sb, sec_rows, d),
+            (par_sb, par_rows, a),
+            (par_sb, par_rows, b),
             (par_sb, par_rows, c),
+            (par_sb, par_rows, d),
         ):
             nc.sync.dma_start(tiles[t][:], rows[:, t, :])
 
@@ -133,17 +133,26 @@ def tile_picked_amsg8_none_po_kernel(
         clipped = grouped_all[:, 1, :].bitcast(F32)[:, 0:S]
         halves = [(slice(h * half, (h + 1) * half), slice(h * S // 32, (h + 1) * S // 32)) for h in range(2)]
         blocks = [slice(k * P, (k + 1) * P) for k in range(S // P)]
-        vmax_strip = keep.tile([P, 3 * half], F32, name="vmax_strip")
-        moment_strip = keep.tile([P, 3 * half], F32, name="moment_strip")
-        vmax_first = vmax_strip[:, half : 3 * half]
-        moment_first = moment_strip[:, half : 3 * half]
-        largest_first = keep.tile([P, S], F32, name="largest_first")
-        rate_first = keep.tile([P, S], F32, name="rate_first")
+        strip = keep.tile([P, 6 * half], F32, name="strip")
         strip_first = keep.tile([P, 3 * half], F32, name="strip_first")
-        step = {a: strip_first[:, half : 3 * half], b: moment_first, c: vmax_first}
-        step[d] = keep.tile([P, S], F32, name="step_last")[:]
-        moment = {b: keep.tile([P, S], F32, name="moment_second")[:], c: strip_first[:, 0:S]}
-        new, vmax_neg, rate, excess, largest, vmax_turned = {}, {}, {}, {}, {}, {}
+        vmax_first = strip[:, 2 * half : 4 * half]
+        moment_first = keep.tile([P, S], F32, name="moment_first")[:]
+        largest_first = keep.tile([P, S], F32, name="largest_first")[:]
+        rate_first = keep.tile([P, S], F32, name="rate_first")[:]
+        step = {
+            a: strip_first[:, half : 3 * half],
+            b: strip[:, 3 * half : 5 * half],
+            c: strip[:, half : 3 * half],
+            d: strip[:, 0 : 2 * half],
+        }
+        moment = {t: keep.tile([P, S], F32, name="moment%d" % t)[:] for t in (b, c)}
+        moment[d] = strip_first[:, 0:S]
+        rate = {t: keep.tile([P, S], F32, name="rate%d" % t)[:] for t in (b, c)}
+        rate[d] = strip[:, 4 * half : 6 * half]
+        new, vmax_neg, vmax_turned = {}, {}, {}
+        banks = [psum.tile([P, S], F32, name="bank%d" % i) for i in range(4)]
+        excess = {b: banks[0], c: banks[2], d: banks[2]}
+        largest = {b: banks[1], c: banks[3], d: banks[3]}
 
         def turn(bank, values, start, stop):
             for k, block in enumerate(blocks):
@@ -159,8 +168,6 @@ def tile_picked_amsg8_none_po_kernel(
         def gather_vmax(t):
             vmax_neg[t] = keep.tile([P, S], F32, name="vmax_neg%d" % t)
             vmax_turned[t] = keep.tile([P, S], F32, name="vmax_turned%d" % t)
-            excess[t] = psum.tile([P, S], F32, name="excess%d" % t)
-            largest[t] = psum.tile([P, S], F32, name="largest%d" % t)
             nc.vector.tensor_scalar(vmax_neg[t][:], vmax_sb[t][:].indirect(ent_sb[:]), -1.0 / 0.875, 0.0, ALU.mult, ALU.add)
             turn(largest[t], vmax_neg[t], True, True)
             turn(excess[t], vmax_neg[t], True, False)
@@ -170,34 +177,36 @@ def tile_picked_amsg8_none_po_kernel(
         def gather_sec(t):
             nc.vector.tensor_tensor(moment[t], sec_sb[t][:].indirect(ent_sb[:]), y_sq[t], ALU.add)
 
-        def make_rate(t):
-            rate[t] = keep.tile([P, S], F32, name="rate%d" % t)[:]
+        def make_largest(t):
             turn(excess[t], moment[t], False, True)
             nc.scalar.activation(clipped, excess[t][:], ACT.Relu)
             turn(largest[t], clipped, False, True)
+
+        def make_rate(t):
             nc.scalar.activation(rate[t], largest[t][:], ACT.Abs_reciprocal_sqrt, scale=4.0 * 0.875)
 
         def make_step(t):
             nc.gpsimd.tensor_tensor(step[t], y_sb[t], rate[t], ALU.mult)
 
-        def gather_par(t):
-            new[t] = keep.tile([P, S], F32, name="new%d" % t)
-            for cols, part in halves:
-                nc.vector.tensor_tensor(new[t][:, cols], par_sb[t][:].indirect(ent_sb[:, part]), step[t][:, cols], ALU.add)
+        def gather_par(t, h):
+            cols, part = halves[h]
+            nc.vector.tensor_tensor(new[t][:, cols], par_sb[t][:].indirect(ent_sb[:, part]), step[t][:, cols], ALU.add)
 
         def scatter(t):
-            nc.vector.tensor_copy(par_sb[t][:].indirect(ent_sb[:]), new[t][:])
+            nc.vector.tensor_copy(par_sb[t][:].indirect(ent_sb[:]), new[t])
             nc.sync.dma_start(out_rows[:, t, :], par_sb[t][:])
 
-        def round_plane(t):
+        def round_first(t):
             both = par_sb[t][:].rearrange("p (h c) -> p h c", h=2)
             for i in range(4):
                 cols = slice(i * P, (i + 1) * P)
                 nc.scalar.copy(grouped_both[:, :, cols, t], both[:, :, cols])
 
+        def round_plane(t):
+            for h in range(2):
+                nc.scalar.copy(grouped_t[h][:, :, t], par_sb[t][:, h * U // 2 : (h + 1) * U // 2])
+
         nc.vector.tensor_copy(vmax_first, vmax_sb[a][:].indirect(ent_sb[:]))
-        par_g = keep.tile([P, S], F32, name="par_g")
-        nc.vector.tensor_copy(par_g[:], par_sb[d][:].indirect(ent_sb[:]))
         gather_vmax(b)
         for cols, part in halves:
             nc.vector.tensor_tensor(moment_first[:, cols], sec_sb[a][:].indirect(ent_sb[:, part]), y_sq[a][:, cols], ALU.add)
@@ -207,37 +216,42 @@ def tile_picked_amsg8_none_po_kernel(
             )
             nc.scalar.activation(rate_first[:, cols], largest_first[:, cols], ACT.Abs_reciprocal_sqrt, scale=4.0)
         gather_sec(b)
+        make_largest(b)
         make_rate(b)
-        nc.vector.scalar_tensor_tensor(step[a], y[a][:], -1.0, rate_first[:], ALU.mult, ALU.mult)
+        nc.vector.scalar_tensor_tensor(step[a], y[a][:], -1.0, rate_first, ALU.mult, ALU.mult)
         square(c, moment_first)
         gather_vmax(c)
-        negate(c, largest_first[:])
-        square(d, vmax_first)
-        negate(d, rate_first[:])
-        gather_par(a)
         gather_sec(c)
-        make_step(b)
+        make_largest(c)
         make_rate(c)
-        scatter(a)
-        round_plane(a)
-        gather_par(b)
-        moment[d] = moment_strip[:, 0:S]
+        negate(c, largest_first)
+        gather_vmax(d)
+        square(d, vmax_first)
+        negate(d, rate_first)
+        new[a] = keep.tile([P, S], F32, name="new_first")[:]
+        new[b] = y_sb[c]
+        gather_par(a, 0)
+        gather_par(a, 1)
         gather_sec(d)
+        make_step(b)
         make_step(c)
-        scatter(b)
-        vmax_last = rate[c]
-        nc.vector.tensor_copy(vmax_last, vmax_sb[d][:].indirect(ent_sb[:]))
-        gather_par(c)
-        largest_last = vmax_strip[:, 0:S]
-        nc.vector.scalar_tensor_tensor(largest_last, moment[d], 0.875, vmax_last, ALU.mult, ALU.max)
-        rate[d] = keep.tile([P, S], F32, name="rate_last")[:]
-        nc.scalar.activation(rate[d], largest_last, ACT.Abs_reciprocal_sqrt, scale=4.0)
+        make_largest(d)
+        scatter(a)
+        gather_par(b, 0)
+        gather_par(b, 1)
+        make_rate(d)
+        round_first(a)
+        new[c] = step[b]
+        gather_par(c, 0)
         make_step(d)
+        scatter(b)
         round_plane(b)
+        gather_par(c, 1)
+        new[d] = clipped
+        nc.vector.tensor_tensor(new[d], par_sb[d][:].indirect(ent_sb[:]), step[d], ALU.add)
         scatter(c)
         round_plane(c)
-        nc.vector.tensor_tensor(par_sb[d][:].indirect(ent_sb[:]), par_g[:], step[d], ALU.add)
-        nc.sync.dma_start(out_rows[:, d, :], par_sb[d][:])
+        scatter(d)
 
         out_codes = keep.tile([P, U], U32, name="out_codes", align_bytes=64)
         out_scales = keep.tile([P, U], U8, name="out_scales", align_bytes=64)

@@ -68,9 +68,9 @@ def tile_picked_amsg8_none_po_kernel(
             nc.sync.dma_start(w_raw[i][:], w1.rearrange("(p j) c -> p j c", j=PACK)[:, 2 * i : 2 * i + 2, :])
         for tiles, rows, t in (
             (vmax_sb, vmax_rows, b),
+            (vmax_sb, vmax_rows, c),
             (sec_sb, sec_rows, a),
             (sec_sb, sec_rows, b),
-            (vmax_sb, vmax_rows, c),
             (sec_sb, sec_rows, c),
             (vmax_sb, vmax_rows, d),
             (sec_sb, sec_rows, d),
@@ -99,7 +99,7 @@ def tile_picked_amsg8_none_po_kernel(
 
         y, y_sq = {}, {}
         for t in PLANE_ORDER:
-            y[t] = psum.tile([P, S], F32, name="y%d" % t)
+            y[t] = psum.tile([P, S], F32, name="y%d" % t, tag="y%d" % t)
             cols = slice(t * P, (t + 1) * P)
             nc.tensor.matmul_mx(
                 out=y[t][:],
@@ -130,29 +130,33 @@ def tile_picked_amsg8_none_po_kernel(
         grouped = [grouped_all[:, 0, :], grouped_all[:, 2, :]]
         grouped_t = [g.rearrange("p (c t) -> p c t", t=PACK) for g in grouped]
         grouped_both = grouped_all[:, 0:3:2, :].rearrange("p h (c t) -> p h c t", t=PACK)
-        clipped = grouped_all[:, 1, :].bitcast(F32)[:, 0:S]
+        gap = grouped_all[:, 1, :].bitcast(F32)[:, 0:S]
         halves = [(slice(h * half, (h + 1) * half), slice(h * S // 32, (h + 1) * S // 32)) for h in range(2)]
         blocks = [slice(k * P, (k + 1) * P) for k in range(S // P)]
         strip = keep.tile([P, 6 * half], F32, name="strip")
         strip_first = keep.tile([P, 3 * half], F32, name="strip_first")
-        vmax_first = strip[:, 2 * half : 4 * half]
+        vmax_first = strip[:, 3 * half : 5 * half]
         moment_first = keep.tile([P, S], F32, name="moment_first")[:]
-        largest_first = keep.tile([P, S], F32, name="largest_first")[:]
-        rate_first = keep.tile([P, S], F32, name="rate_first")[:]
+        strip_third = keep.tile([P, 3 * half], F32, name="strip_third")
+        largest_first = strip_third[:, 0:S]
+        strip_last = keep.tile([P, 3 * half], F32, name="strip_last")
+        rate_first = strip[:, half : 3 * half]
+        step_second = strip[:].rearrange("p (k c) -> p k c", c=half)[:, 0:4:3, :]
         step = {
             a: strip_first[:, half : 3 * half],
-            b: strip[:, 3 * half : 5 * half],
-            c: strip[:, half : 3 * half],
-            d: strip[:, 0 : 2 * half],
+            d: strip_last[:, 0:S],
         }
+        step_third = (strip[:, 9 * half // 2 : 11 * half // 2], strip[:, 4 * half : 5 * half])
         moment = {t: keep.tile([P, S], F32, name="moment%d" % t)[:] for t in (b, c)}
         moment[d] = strip_first[:, 0:S]
-        rate = {t: keep.tile([P, S], F32, name="rate%d" % t)[:] for t in (b, c)}
-        rate[d] = strip[:, 4 * half : 6 * half]
+        rate = {b: keep.tile([P, S], F32, name="rate_second")[:], c: strip_last[:, half : 3 * half]}
+        rate[d] = keep.tile([P, S], F32, name="rate_last")[:]
         new, vmax_neg, vmax_turned = {}, {}, {}
+        clipped = {t: keep.tile([P, S], F32, name="clipped%d" % t)[:] for t in (b, c)}
+        clipped[d] = gap
         banks = [psum.tile([P, S], F32, name="bank%d" % i) for i in range(4)]
-        excess = {b: banks[0], c: banks[2], d: banks[2]}
-        largest = {b: banks[1], c: banks[3], d: banks[3]}
+        excess = {b: banks[0], c: banks[2]}
+        largest = {b: banks[1], c: banks[3]}
 
         def turn(bank, values, start, stop):
             for k, block in enumerate(blocks):
@@ -165,10 +169,10 @@ def tile_picked_amsg8_none_po_kernel(
                     is_transpose=True,
                 )
 
-        def gather_vmax(t):
-            vmax_neg[t] = keep.tile([P, S], F32, name="vmax_neg%d" % t)
+        def gather_vmax(t, into):
+            vmax_neg[t] = into
             vmax_turned[t] = keep.tile([P, S], F32, name="vmax_turned%d" % t)
-            nc.vector.tensor_scalar(vmax_neg[t][:], vmax_sb[t][:].indirect(ent_sb[:]), -1.0 / 0.875, 0.0, ALU.mult, ALU.add)
+            nc.vector.tensor_scalar(vmax_neg[t], vmax_sb[t][:].indirect(ent_sb[:]), -1.0 / 0.875, 0.0, ALU.mult, ALU.add)
             turn(largest[t], vmax_neg[t], True, True)
             turn(excess[t], vmax_neg[t], True, False)
             nc.scalar.activation(vmax_turned[t][:], largest[t][:], ACT.Copy, scale=-1.0)
@@ -179,8 +183,8 @@ def tile_picked_amsg8_none_po_kernel(
 
         def make_largest(t):
             turn(excess[t], moment[t], False, True)
-            nc.scalar.activation(clipped, excess[t][:], ACT.Relu)
-            turn(largest[t], clipped, False, True)
+            nc.scalar.activation(clipped[t], excess[t][:], ACT.Relu)
+            turn(largest[t], clipped[t], False, True)
 
         def make_rate(t):
             nc.scalar.activation(rate[t], largest[t][:], ACT.Abs_reciprocal_sqrt, scale=4.0 * 0.875)
@@ -207,7 +211,8 @@ def tile_picked_amsg8_none_po_kernel(
                 nc.scalar.copy(grouped_t[h][:, :, t], par_sb[t][:, h * U // 2 : (h + 1) * U // 2])
 
         nc.vector.tensor_copy(vmax_first, vmax_sb[a][:].indirect(ent_sb[:]))
-        gather_vmax(b)
+        for t in (b, c):
+            gather_vmax(t, keep.tile([P, S], F32, name="vmax_neg%d" % t)[:])
         for cols, part in halves:
             nc.vector.tensor_tensor(moment_first[:, cols], sec_sb[a][:].indirect(ent_sb[:, part]), y_sq[a][:, cols], ALU.add)
         for cols, part in halves:
@@ -215,39 +220,44 @@ def tile_picked_amsg8_none_po_kernel(
                 largest_first[:, cols], moment_first[:, cols], 0.875, vmax_first[:, cols], ALU.mult, ALU.max
             )
             nc.scalar.activation(rate_first[:, cols], largest_first[:, cols], ACT.Abs_reciprocal_sqrt, scale=4.0)
+        square(c, moment_first)
         gather_sec(b)
         make_largest(b)
+        square(d, vmax_first)
         make_rate(b)
         nc.vector.scalar_tensor_tensor(step[a], y[a][:], -1.0, rate_first, ALU.mult, ALU.mult)
-        square(c, moment_first)
-        gather_vmax(c)
         gather_sec(c)
         make_largest(c)
         make_rate(c)
         negate(c, largest_first)
-        gather_vmax(d)
-        square(d, vmax_first)
+        excess[d] = psum.tile([P, S], F32, name="excess_last", tag="y%d" % a)
+        largest[d] = psum.tile([P, S], F32, name="largest_last", tag="y%d" % b)
+        gather_vmax(d, keep.tile([P, S], F32, name="vmax_neg_last")[:])
         negate(d, rate_first)
         new[a] = keep.tile([P, S], F32, name="new_first")[:]
-        new[b] = y_sb[c]
+        new[b] = strip_third[:, half : 3 * half]
         gather_par(a, 0)
         gather_par(a, 1)
         gather_sec(d)
-        make_step(b)
-        make_step(c)
+        nc.gpsimd.tensor_tensor(
+            step_second, y_sb[b].rearrange("p (k c) -> p k c", k=2), rate[b].rearrange("p (k c) -> p k c", k=2), ALU.mult
+        )
+        nc.gpsimd.tensor_tensor(step_third[1], y_sb[c][:, halves[1][0]], rate[c][:, halves[1][0]], ALU.mult)
         make_largest(d)
-        scatter(a)
-        gather_par(b, 0)
-        gather_par(b, 1)
         make_rate(d)
+        scatter(a)
+        for h in (1, 0):
+            cols, part = halves[h]
+            nc.vector.tensor_tensor(new[b][:, cols], par_sb[b][:].indirect(ent_sb[:, part]), step_second[:, h, :], ALU.add)
         round_first(a)
-        new[c] = step[b]
-        gather_par(c, 0)
+        new[c] = strip[:, 2 * half : 4 * half]
+        nc.vector.tensor_tensor(new[c][:, halves[1][0]], par_sb[c][:].indirect(ent_sb[:, halves[1][1]]), step_third[1], ALU.add)
+        nc.gpsimd.tensor_tensor(step_third[0], y_sb[c][:, halves[0][0]], rate[c][:, halves[0][0]], ALU.mult)
         make_step(d)
         scatter(b)
         round_plane(b)
-        gather_par(c, 1)
-        new[d] = clipped
+        nc.vector.tensor_tensor(new[c][:, halves[0][0]], par_sb[c][:].indirect(ent_sb[:, halves[0][1]]), step_third[0], ALU.add)
+        new[d] = gap
         nc.vector.tensor_tensor(new[d], par_sb[d][:].indirect(ent_sb[:]), step[d], ALU.add)
         scatter(c)
         round_plane(c)

@@ -33,7 +33,7 @@ def tile_picked_amsg8_none_po_kernel(
 
         offs_sb = lists.tile([P, S // 16], U16, name="offs_sb")
         ent_sb = lists.tile([P, S // 16], U16, name="ent_sb")
-        w_raw = [keep.tile([P, 2, N], F32, name="w_raw%d" % i) for i in range(2)]
+        w_raw = [keep.tile([P, 2, N], F32, name="w_raw%d" % i, tag="w_raw%d" % i) for i in range(2)]
         x_table = keep.tile([P, T], I32, name="x_table")
         xs_table = keep.tile([P, T], U8, name="xs_table")
         warm_in = keep.tile([P, 1], F32, name="warm_in")
@@ -49,7 +49,7 @@ def tile_picked_amsg8_none_po_kernel(
         out_rows = out_0.rearrange("(p t) u -> p t u", t=PACK)
         par_sb, sec_sb, vmax_sb = {}, {}, {}
         for t in PLANE_ORDER:
-            vmax_sb[t] = keep.tile([P, U], F32, name="vmax%d" % t)
+            vmax_sb[t] = keep.tile([P, U], F32, name="vmax%d" % t, tag="vmax%d" % t)
             sec_sb[t] = keep.tile([P, U], F32, name="sec%d" % t)
             par_sb[t] = keep.tile([P, U], F32, name="par%d" % t)
         a, b, c, d = PLANE_ORDER
@@ -75,16 +75,16 @@ def tile_picked_amsg8_none_po_kernel(
             (vmax_sb, vmax_rows, d),
             (sec_sb, sec_rows, d),
             (par_sb, par_rows, a),
-            (par_sb, par_rows, b),
             (par_sb, par_rows, c),
+            (par_sb, par_rows, b),
             (par_sb, par_rows, d),
         ):
             nc.sync.dma_start(tiles[t][:], rows[:, t, :])
 
         x_picked = keep.tile([P, S], U32, name="x_picked", align_bytes=64)
-        nc.vector.tensor_copy(x_picked[:], x_table[:].bitcast(U32).indirect(offs_sb[:]))
         xs_picked = keep.tile([P, S], U8, name="xs_picked", align_bytes=64)
         nc.vector.tensor_copy(xs_picked[:], xs_table[:].indirect(offs_sb[:]))
+        nc.vector.tensor_copy(x_picked[:], x_table[:].bitcast(U32).indirect(offs_sb[:]))
         w_codes = keep.tile([P, N], U32, name="w_codes", align_bytes=64)
         w_scales = keep.tile([P, N], U8, name="w_scales", align_bytes=64)
         w_grouped = [keep.tile([P, N * 2], BF16, name="w_grouped%d" % i, align_bytes=64) for i in range(2)]
@@ -122,10 +122,6 @@ def tile_picked_amsg8_none_po_kernel(
             y_sb[t] = into
             nc.scalar.activation(into, y[t][:], ACT.Copy, scale=-1.0)
 
-        for t in (a, b):
-            square(t, keep.tile([P, S], F32, name="y_sq%d" % t)[:])
-        negate(b, keep.tile([P, S], F32, name="y_second")[:])
-
         grouped_all = keep.tile([P, 3, 2 * CHUNK * PACK], BF16, name="grouped_all", align_bytes=64)
         grouped = [grouped_all[:, 0, :], grouped_all[:, 2, :]]
         grouped_t = [g.rearrange("p (c t) -> p c t", t=PACK) for g in grouped]
@@ -133,30 +129,20 @@ def tile_picked_amsg8_none_po_kernel(
         gap = grouped_all[:, 1, :].bitcast(F32)[:, 0:S]
         halves = [(slice(h * half, (h + 1) * half), slice(h * S // 32, (h + 1) * S // 32)) for h in range(2)]
         blocks = [slice(k * P, (k + 1) * P) for k in range(S // P)]
-        strip = keep.tile([P, 6 * half], F32, name="strip")
         strip_first = keep.tile([P, 3 * half], F32, name="strip_first")
-        vmax_first = strip[:, 3 * half : 5 * half]
-        moment_first = keep.tile([P, S], F32, name="moment_first")[:]
-        strip_third = keep.tile([P, 3 * half], F32, name="strip_third")
-        largest_first = strip_third[:, 0:S]
+        strip_third = keep.tile([P, 5 * half], F32, name="strip_third")
         strip_last = keep.tile([P, 3 * half], F32, name="strip_last")
-        rate_first = strip[:, half : 3 * half]
-        step_second = strip[:].rearrange("p (k c) -> p k c", c=half)[:, 0:4:3, :]
-        step = {
-            a: strip_first[:, half : 3 * half],
-            d: strip_last[:, 0:S],
-        }
-        step_third = (strip[:, 9 * half // 2 : 11 * half // 2], strip[:, 4 * half : 5 * half])
-        moment = {t: keep.tile([P, S], F32, name="moment%d" % t)[:] for t in (b, c)}
-        moment[d] = strip_first[:, 0:S]
-        rate = {b: keep.tile([P, S], F32, name="rate_second")[:], c: strip_last[:, half : 3 * half]}
-        rate[d] = keep.tile([P, S], F32, name="rate_last")[:]
-        new, vmax_neg, vmax_turned = {}, {}, {}
-        clipped = {t: keep.tile([P, S], F32, name="clipped%d" % t)[:] for t in (b, c)}
+        step = {a: strip_first[:, 0:S], d: strip_last[:, 0:S]}
+        moment = {t: keep.tile([P, S], F32, name="moment%d" % t)[:] for t in PLANE_ORDER}
+        rate = {t: keep.tile([P, S], F32, name="rate%d" % t)[:] for t in (b, d)}
+        rate[a] = strip_third[:, half : 3 * half]
+        vmax_neg = {t: keep.tile([P, S], F32, name="vmax_neg%d" % t)[:] for t in (a, b, c)}
+        vmax_neg[d] = strip_first[:, half : 3 * half]
+        rate[c] = strip_last[:, half : 3 * half]
+        new, vmax_turned = {}, {}
+        clipped = {t: keep.tile([P, S], F32, name="clipped%d" % t)[:] for t in (a, b, c)}
         clipped[d] = gap
-        banks = [psum.tile([P, S], F32, name="bank%d" % i) for i in range(4)]
-        excess = {b: banks[0], c: banks[2]}
-        largest = {b: banks[1], c: banks[3]}
+        excess, largest = {}, {}
 
         def turn(bank, values, start, stop):
             for k, block in enumerate(blocks):
@@ -169,21 +155,35 @@ def tile_picked_amsg8_none_po_kernel(
                     is_transpose=True,
                 )
 
-        def gather_vmax(t, into):
-            vmax_neg[t] = into
-            vmax_turned[t] = keep.tile([P, S], F32, name="vmax_turned%d" % t)
-            nc.vector.tensor_scalar(vmax_neg[t], vmax_sb[t][:].indirect(ent_sb[:]), -1.0 / 0.875, 0.0, ALU.mult, ALU.add)
+        def add_to_excess(t, values, tag):
+            first = t not in excess
+            if first:
+                excess[t] = psum.tile([P, S], F32, name="excess%d" % t, tag=tag)
+            turn(excess[t], values, first, not first)
+
+        def gather_vmax(t, cols=slice(0, S), part=slice(0, S // 16)):
+            nc.vector.tensor_scalar(
+                vmax_neg[t][:, cols], vmax_sb[t][:].indirect(ent_sb[:, part]), -1.0 / 0.875, 0.0, ALU.mult, ALU.add
+            )
+
+        def turn_vmax(t, excess_tag, largest_tag):
+            largest[t] = psum.tile([P, S], F32, name="largest%d" % t, tag=largest_tag)
+            vmax_turned[t] = keep.tile([P, S], F32, name="vmax_turned%d" % t, tag="w_raw1" if t == a else "vmax_turned%d" % t)
             turn(largest[t], vmax_neg[t], True, True)
-            turn(excess[t], vmax_neg[t], True, False)
+            add_to_excess(t, vmax_neg[t], excess_tag)
             nc.scalar.activation(vmax_turned[t][:], largest[t][:], ACT.Copy, scale=-1.0)
+
+        def gather_sec(t, excess_tag):
+            nc.vector.tensor_tensor(moment[t], sec_sb[t][:].indirect(ent_sb[:]), y_sq[t], ALU.add)
+            add_to_excess(t, moment[t], excess_tag)
+
+        def open_largest(t):
             turn(largest[t], vmax_turned[t], True, False)
 
-        def gather_sec(t):
-            nc.vector.tensor_tensor(moment[t], sec_sb[t][:].indirect(ent_sb[:]), y_sq[t], ALU.add)
-
         def make_largest(t):
-            turn(excess[t], moment[t], False, True)
             nc.scalar.activation(clipped[t], excess[t][:], ACT.Relu)
+            if t != a:
+                open_largest(t)
             turn(largest[t], clipped[t], False, True)
 
         def make_rate(t):
@@ -210,39 +210,50 @@ def tile_picked_amsg8_none_po_kernel(
             for h in range(2):
                 nc.scalar.copy(grouped_t[h][:, :, t], par_sb[t][:, h * U // 2 : (h + 1) * U // 2])
 
-        nc.vector.tensor_copy(vmax_first, vmax_sb[a][:].indirect(ent_sb[:]))
-        for t in (b, c):
-            gather_vmax(t, keep.tile([P, S], F32, name="vmax_neg%d" % t)[:])
-        for cols, part in halves:
-            nc.vector.tensor_tensor(moment_first[:, cols], sec_sb[a][:].indirect(ent_sb[:, part]), y_sq[a][:, cols], ALU.add)
-        for cols, part in halves:
-            nc.vector.scalar_tensor_tensor(
-                largest_first[:, cols], moment_first[:, cols], 0.875, vmax_first[:, cols], ALU.mult, ALU.max
-            )
-            nc.scalar.activation(rate_first[:, cols], largest_first[:, cols], ACT.Abs_reciprocal_sqrt, scale=4.0)
-        square(c, moment_first)
-        gather_sec(b)
+        gather_vmax(a)
+        turn_vmax(a, "bank0", "bank1")
+        open_largest(a)
+        for t in (a, b):
+            square(t, keep.tile([P, S], F32, name="y_sq%d" % t)[:])
+        gather_vmax(b)
+        turn_vmax(b, "bank3", "bank2")
+        gather_sec(a, "bank0")
+        make_largest(a)
+        make_rate(a)
+        square(c, keep.tile([P, S], F32, name="y_sq_third")[:])
+        square(d, step[a])
+        gather_sec(b, "bank3")
         make_largest(b)
-        square(d, vmax_first)
         make_rate(b)
-        nc.vector.scalar_tensor_tensor(step[a], y[a][:], -1.0, rate_first, ALU.mult, ALU.mult)
-        gather_sec(c)
+        gather_vmax(c)
+        turn_vmax(c, "bank1", "bank0")
+        gather_sec(c, "bank1")
+        gather_vmax(d, *halves[1])
+        for h in (1, 0):
+            cols, part = halves[h]
+            nc.vector.tensor_tensor(moment[d][:, cols], sec_sb[d][:].indirect(ent_sb[:, part]), y_sq[d][:, cols], ALU.add)
+        for h in (1, 0):
+            cols = halves[h][0]
+            nc.vector.scalar_tensor_tensor(step[a][:, cols], y[a][:, cols], -1.0, rate[a][:, cols], ALU.mult, ALU.mult)
+        negate(b, strip_third[:, 0:S])
+        negate(c, strip_third[:, S : 2 * S])
         make_largest(c)
         make_rate(c)
-        negate(c, largest_first)
-        excess[d] = psum.tile([P, S], F32, name="excess_last", tag="y%d" % a)
-        largest[d] = psum.tile([P, S], F32, name="largest_last", tag="y%d" % b)
-        gather_vmax(d, keep.tile([P, S], F32, name="vmax_neg_last")[:])
-        negate(d, rate_first)
+        add_to_excess(d, moment[d], "bank3")
         new[a] = keep.tile([P, S], F32, name="new_first")[:]
-        new[b] = strip_third[:, half : 3 * half]
-        gather_par(a, 0)
+        new[b] = strip_third[:, 3 * half : 5 * half]
         gather_par(a, 1)
-        gather_sec(d)
+        gather_par(a, 0)
+        gather_vmax(d, *halves[0])
+        strip = keep.tile([P, 6 * half], F32, name="strip", tag="vmax%d" % d)
+        step_second = strip[:].rearrange("p (k c) -> p k c", c=half)[:, 0:4:3, :]
+        step_third = (strip[:, 9 * half // 2 : 11 * half // 2], strip[:, 4 * half : 5 * half])
+        turn_vmax(d, "bank3", "bank2")
         nc.gpsimd.tensor_tensor(
             step_second, y_sb[b].rearrange("p (k c) -> p k c", k=2), rate[b].rearrange("p (k c) -> p k c", k=2), ALU.mult
         )
         nc.gpsimd.tensor_tensor(step_third[1], y_sb[c][:, halves[1][0]], rate[c][:, halves[1][0]], ALU.mult)
+        negate(d, strip[:, half : 3 * half])
         make_largest(d)
         make_rate(d)
         scatter(a)

@@ -49,7 +49,7 @@ def tile_picked_amsg8_none_po_kernel(
         out_rows = out_0.rearrange("(p t) u -> p t u", t=PACK)
         par_sb, sec_sb, vmax_sb = {}, {}, {}
         for t in PLANE_ORDER:
-            vmax_sb[t] = keep.tile([P, U], F32, name="vmax%d" % t, tag="vmax%d" % t)
+            vmax_sb[t] = keep.tile([P, U], F32, name="vmax%d" % t)
             sec_sb[t] = keep.tile([P, U], F32, name="sec%d" % t)
             par_sb[t] = keep.tile([P, U], F32, name="par%d" % t)
         a, b, c, d = PLANE_ORDER
@@ -71,9 +71,9 @@ def tile_picked_amsg8_none_po_kernel(
             (vmax_sb, vmax_rows, c),
             (sec_sb, sec_rows, a),
             (sec_sb, sec_rows, b),
-            (sec_sb, sec_rows, c),
             (vmax_sb, vmax_rows, d),
             (sec_sb, sec_rows, d),
+            (sec_sb, sec_rows, c),
             (par_sb, par_rows, a),
             (par_sb, par_rows, c),
             (par_sb, par_rows, b),
@@ -91,11 +91,17 @@ def tile_picked_amsg8_none_po_kernel(
         w_dealt = [g[:].rearrange("p (t m j) -> p m j t", t=2, j=PACK) for g in w_grouped]
         for i in range(2):
             w_rows = w_raw[i][:].rearrange("p j (m t) -> p m j t", t=PACK)
-            nc.vector.tensor_copy(w_dealt[1][:, :, 2 * i : 2 * i + 2, :], w_rows[:, :, :, 2:4])
-            nc.scalar.copy(w_dealt[0][:, :, 2 * i : 2 * i + 2, :], w_rows[:, :, :, 0:2])
-        for i in (1, 0):
-            cols = slice(i * 2 * P, (i + 1) * 2 * P)
-            nc.vector.quantize_mx(out=w_codes[:, cols].bitcast(FP8X4), scales=w_scales[:, cols], in_=w_grouped[i][:])
+            for lo, hi in ((0, 2),) if i == 0 else ((0, 1), (1, 2)):
+                nc.vector.tensor_copy(w_dealt[1][:, :, 2 * i : 2 * i + 2, lo:hi], w_rows[:, :, :, 2 + lo : 2 + hi])
+            if i == 0:
+                nc.scalar.copy(w_dealt[0][:, :, 0:2, :], w_rows[:, :, :, 0:2])
+            else:
+                nc.scalar.copy(w_dealt[0][:, 0:96, 2:4, :], w_rows[:, 0:96, :, 0:2])
+                nc.vector.tensor_copy(w_dealt[0][:, 96:P, 2:4, :], w_rows[:, 96:P, :, 0:2])
+        for lo, hi in ((2, 3), (3, 4), (0, 2)):
+            cols = slice(lo * P, hi * P)
+            rounded = w_grouped[lo // 2][:, (lo % 2) * P * PACK : (hi - lo // 2 * 2) * P * PACK]
+            nc.vector.quantize_mx(out=w_codes[:, cols].bitcast(FP8X4), scales=w_scales[:, cols], in_=rounded)
 
         y, y_sq = {}, {}
         for t in PLANE_ORDER:
@@ -131,14 +137,17 @@ def tile_picked_amsg8_none_po_kernel(
         blocks = [slice(k * P, (k + 1) * P) for k in range(S // P)]
         strip_first = keep.tile([P, 3 * half], F32, name="strip_first")
         strip_third = keep.tile([P, 5 * half], F32, name="strip_third")
-        strip_last = keep.tile([P, 3 * half], F32, name="strip_last")
-        step = {a: strip_first[:, 0:S], d: strip_last[:, 0:S]}
-        moment = {t: keep.tile([P, S], F32, name="moment%d" % t)[:] for t in PLANE_ORDER}
-        rate = {t: keep.tile([P, S], F32, name="rate%d" % t)[:] for t in (b, d)}
+        strip = keep.tile([P, 2816], F32, name="strip")
+        step_second = strip[:, 0:2176].rearrange("p (k c) -> p k c", k=2)[:, :, 0:half]
+        step_third = (strip[:, 1216:1472], strip[:, 1408:1664])
+        square_last = strip[:, 1280:2816].rearrange("p (k c) -> p k c", k=2)[:, :, 0:half]
+        step = {a: strip_first[:, 0:S], d: strip[:, 1536:2048]}
+        moment = {t: keep.tile([P, S], F32, name="moment%d" % t)[:] for t in (a, b, c)}
+        moment[d] = strip_first[:, half : 3 * half]
+        rate = {b: keep.tile([P, S], F32, name="rate_second")[:]}
         rate[a] = strip_third[:, half : 3 * half]
-        vmax_neg = {t: keep.tile([P, S], F32, name="vmax_neg%d" % t)[:] for t in (a, b, c)}
-        vmax_neg[d] = strip_first[:, half : 3 * half]
-        rate[c] = strip_last[:, half : 3 * half]
+        vmax_neg = {t: keep.tile([P, S], F32, name="vmax_neg%d" % t)[:] for t in PLANE_ORDER}
+        rate[c] = keep.tile([P, S], F32, name="rate_third")[:]
         new, vmax_turned = {}, {}
         clipped = {t: keep.tile([P, S], F32, name="clipped%d" % t)[:] for t in (a, b, c)}
         clipped[d] = gap
@@ -161,16 +170,17 @@ def tile_picked_amsg8_none_po_kernel(
                 excess[t] = psum.tile([P, S], F32, name="excess%d" % t, tag=tag)
             turn(excess[t], values, first, not first)
 
-        def gather_vmax(t, cols=slice(0, S), part=slice(0, S // 16)):
-            nc.vector.tensor_scalar(
-                vmax_neg[t][:, cols], vmax_sb[t][:].indirect(ent_sb[:, part]), -1.0 / 0.875, 0.0, ALU.mult, ALU.add
-            )
+        def gather_vmax(t):
+            nc.vector.tensor_scalar(vmax_neg[t], vmax_sb[t][:].indirect(ent_sb[:]), -1.0 / 0.875, 0.0, ALU.mult, ALU.add)
 
-        def turn_vmax(t, excess_tag, largest_tag):
+        def gather_sec_half(t, h, squares):
+            cols, part = halves[h]
+            nc.vector.tensor_tensor(moment[t][:, cols], sec_sb[t][:].indirect(ent_sb[:, part]), squares, ALU.add)
+
+        def turn_vmax(t, largest_tag):
             largest[t] = psum.tile([P, S], F32, name="largest%d" % t, tag=largest_tag)
             vmax_turned[t] = keep.tile([P, S], F32, name="vmax_turned%d" % t, tag="w_raw1" if t == a else "vmax_turned%d" % t)
             turn(largest[t], vmax_neg[t], True, True)
-            add_to_excess(t, vmax_neg[t], excess_tag)
             nc.scalar.activation(vmax_turned[t][:], largest[t][:], ACT.Copy, scale=-1.0)
 
         def gather_sec(t, excess_tag):
@@ -211,49 +221,53 @@ def tile_picked_amsg8_none_po_kernel(
                 nc.scalar.copy(grouped_t[h][:, :, t], par_sb[t][:, h * U // 2 : (h + 1) * U // 2])
 
         gather_vmax(a)
-        turn_vmax(a, "bank0", "bank1")
+        turn_vmax(a, "bank1")
+        add_to_excess(a, vmax_neg[a], "bank0")
         open_largest(a)
         for t in (a, b):
             square(t, keep.tile([P, S], F32, name="y_sq%d" % t)[:])
         gather_vmax(b)
-        turn_vmax(b, "bank3", "bank2")
+        turn_vmax(b, "bank2")
         gather_sec(a, "bank0")
         make_largest(a)
         make_rate(a)
-        square(c, keep.tile([P, S], F32, name="y_sq_third")[:])
-        square(d, step[a])
-        gather_sec(b, "bank3")
+        negate(b, clipped[a])
+        square(c, step[a])
+        nc.scalar.activation(
+            square_last, y[d][:].rearrange("p (k c) -> p k c", k=2), ACT.Square, scale=math.sqrt(0.125 / 0.875)
+        )
+        negate(d, keep.tile([P, S], F32, name="y_last")[:])
+        gather_sec(b, "bank0")
+        add_to_excess(b, vmax_neg[b], "bank0")
         make_largest(b)
         make_rate(b)
         gather_vmax(c)
-        turn_vmax(c, "bank1", "bank0")
-        gather_sec(c, "bank1")
-        gather_vmax(d, *halves[1])
+        turn_vmax(c, "bank3")
+        add_to_excess(c, vmax_neg[c], "bank1")
+        gather_vmax(d)
+        gather_sec_half(d, 1, square_last[:, 1, :])
         for h in (1, 0):
-            cols, part = halves[h]
-            nc.vector.tensor_tensor(moment[d][:, cols], sec_sb[d][:].indirect(ent_sb[:, part]), y_sq[d][:, cols], ALU.add)
+            gather_sec_half(c, h, y_sq[c][:, halves[h][0]])
+        add_to_excess(c, moment[c], "bank1")
         for h in (1, 0):
             cols = halves[h][0]
             nc.vector.scalar_tensor_tensor(step[a][:, cols], y[a][:, cols], -1.0, rate[a][:, cols], ALU.mult, ALU.mult)
-        negate(b, strip_third[:, 0:S])
         negate(c, strip_third[:, S : 2 * S])
         make_largest(c)
         make_rate(c)
-        add_to_excess(d, moment[d], "bank3")
+        turn_vmax(d, "bank2")
+        add_to_excess(d, vmax_neg[d], "bank0")
         new[a] = keep.tile([P, S], F32, name="new_first")[:]
         new[b] = strip_third[:, 3 * half : 5 * half]
         gather_par(a, 1)
         gather_par(a, 0)
-        gather_vmax(d, *halves[0])
-        strip = keep.tile([P, 6 * half], F32, name="strip", tag="vmax%d" % d)
-        step_second = strip[:].rearrange("p (k c) -> p k c", c=half)[:, 0:4:3, :]
-        step_third = (strip[:, 9 * half // 2 : 11 * half // 2], strip[:, 4 * half : 5 * half])
-        turn_vmax(d, "bank3", "bank2")
+        gather_sec_half(d, 0, square_last[:, 0, :])
+        add_to_excess(d, moment[d], "bank0")
         nc.gpsimd.tensor_tensor(
             step_second, y_sb[b].rearrange("p (k c) -> p k c", k=2), rate[b].rearrange("p (k c) -> p k c", k=2), ALU.mult
         )
         nc.gpsimd.tensor_tensor(step_third[1], y_sb[c][:, halves[1][0]], rate[c][:, halves[1][0]], ALU.mult)
-        negate(d, strip[:, half : 3 * half])
+        rate[d] = strip[:, 256:768]
         make_largest(d)
         make_rate(d)
         scatter(a)
@@ -261,7 +275,7 @@ def tile_picked_amsg8_none_po_kernel(
             cols, part = halves[h]
             nc.vector.tensor_tensor(new[b][:, cols], par_sb[b][:].indirect(ent_sb[:, part]), step_second[:, h, :], ALU.add)
         round_first(a)
-        new[c] = strip[:, 2 * half : 4 * half]
+        new[c] = strip[:, 640:1152]
         nc.vector.tensor_tensor(new[c][:, halves[1][0]], par_sb[c][:].indirect(ent_sb[:, halves[1][1]]), step_third[1], ALU.add)
         nc.gpsimd.tensor_tensor(step_third[0], y_sb[c][:, halves[0][0]], rate[c][:, halves[0][0]], ALU.mult)
         make_step(d)

@@ -36,11 +36,8 @@ def tile_picked_amsg8_none_po_kernel(
         w_raw = [keep.tile([P, 2, N], F32, name="w_raw%d" % i, tag="w_raw%d" % i) for i in range(2)]
         x_table = keep.tile([P, T], I32, name="x_table")
         xs_table = keep.tile([P, T], U8, name="xs_table")
-        warm_in = keep.tile([P, 1], F32, name="warm_in")
-        warm_out = keep.tile([P, 1], F32, name="warm_out")
 
         nc.gpsimd.memset(xs_table[:].bitcast(I32), 0)
-        nc.gpsimd.memset(warm_in[:], 1.0)
         identity = keep.tile([P, P], F32, name="identity")
         make_identity(nc, identity[:])
         par_rows = par.rearrange("(p t) u -> p t u", t=PACK)
@@ -62,7 +59,6 @@ def tile_picked_amsg8_none_po_kernel(
                 xs_table[32 * q : 32 * q + 4, :].bitcast(I32),
                 x_scales[0, 4 * q : 4 * q + 4, :].bitcast(I32),
             )
-        nc.scalar.activation(warm_out[:], warm_in[:], ACT.Abs_reciprocal_sqrt)
         nc.sync.dma_start(x_table[:], x_words[0].rearrange("p c r -> p (c r)").bitcast(I32))
         for i in range(2):
             nc.sync.dma_start(w_raw[i][:], w1.rearrange("(p j) c -> p j c", j=PACK)[:, 2 * i : 2 * i + 2, :])

@@ -2,7 +2,6 @@ import math
 from contextlib import ExitStack
 
 import concourse.mybir as mybir
-from concourse.masks import make_identity
 
 F32 = mybir.dt.float32
 BF16 = mybir.dt.bfloat16
@@ -29,77 +28,77 @@ def tile_picked_amsg8_none_po_kernel(
     with ExitStack() as ctx:
         lists = ctx.enter_context(tc.tile_pool(name="lists", bufs=1))
         keep = ctx.enter_context(tc.tile_pool(name="keep", bufs=1))
+        late = ctx.enter_context(tc.tile_pool(name="late", bufs=1))
         psum = ctx.enter_context(tc.psum_pool(name="psum", bufs=1))
+
+        def place(name, shape, dtype, tag=None):
+            if name == "moment3":
+                return late.tile(shape, dtype, name=name, offset=1024)
+            if tag == "vmax_at":
+                return late.tile(shape, dtype, name=name, tag=tag, offset=5120)
+            return keep.tile(shape, dtype, name=name, tag=tag or name, align_bytes=64)
 
         offs_sb = lists.tile([P, S // 16], U16, name="offs_sb")
         ent_sb = lists.tile([P, S // 16], U16, name="ent_sb")
-        w_raw = [keep.tile([P, 2, N], F32, name="w_raw%d" % i, tag="w_raw%d" % i) for i in range(2)]
-        x_table = keep.tile([P, T], I32, name="x_table")
-        xs_table = keep.tile([P, T], U8, name="xs_table")
-
+        w_raw = [place("w_raw%d" % i, [P, 2, N], F32) for i in range(2)]
+        x_table = place("x_table", [P, T], I32)
+        xs_table = place("xs_table", [P, T], U8)
         nc.gpsimd.memset(xs_table[:].bitcast(I32), 0)
-        identity = keep.tile([P, P], F32, name="identity")
-        make_identity(nc, identity[:])
-        par_rows = par.rearrange("(p t) u -> p t u", t=PACK)
-        sec_rows = sec.rearrange("(p t) u -> p t u", t=PACK)
-        vmax_rows = vmax.rearrange("(p t) u -> p t u", t=PACK)
+
+        one = place("one", [P, 2], F32)
+        nc.gpsimd.memset(one[:, 0:1], 1.0)
+        nc.scalar.activation(one[:, 1:2], one[:, 0:1], ACT.Abs_reciprocal_sqrt)
+
+        rows = {name: ap.rearrange("(p t) u -> p t u", t=PACK) for name, ap in (("par", par), ("sec", sec), ("vmax", vmax))}
         out_rows = out_0.rearrange("(p t) u -> p t u", t=PACK)
-        par_sb, sec_sb, vmax_sb = {}, {}, {}
-        for t in PLANE_ORDER:
-            vmax_sb[t] = keep.tile([P, U], F32, name="vmax%d" % t)
-            sec_sb[t] = keep.tile([P, U], F32, name="sec%d" % t)
-            par_sb[t] = keep.tile([P, U], F32, name="par%d" % t)
-        a, b, c, d = PLANE_ORDER
-        nc.sync.dma_start(ent_sb[:], ent)
-        nc.sync.dma_start(vmax_sb[a][:], vmax_rows[:, a, :])
+        table = {(name, t): place("%s%d" % (name, t), [P, U], F32) for name in rows for t in range(PACK)}
+
         nc.sync.dma_start(offs_sb[:], offs)
+        w_halves = w1.rearrange("(p i j) c -> i p j c", i=2, j=2)
+        nc.sync.dma_start(w_raw[0][:], w_halves[0])
         for q in range(4):
-            queue = nc.sync if q < 2 else nc.scalar
-            queue.dma_start(
+            nc.sync.dma_start(
                 xs_table[32 * q : 32 * q + 4, :].bitcast(I32),
                 x_scales[0, 4 * q : 4 * q + 4, :].bitcast(I32),
             )
         nc.sync.dma_start(x_table[:], x_words[0].rearrange("p c r -> p (c r)").bitcast(I32))
-        for i in range(2):
-            nc.sync.dma_start(w_raw[i][:], w1.rearrange("(p j) c -> p j c", j=PACK)[:, 2 * i : 2 * i + 2, :])
-        for tiles, rows, t in (
-            (vmax_sb, vmax_rows, b),
-            (vmax_sb, vmax_rows, c),
-            (sec_sb, sec_rows, a),
-            (sec_sb, sec_rows, b),
-            (vmax_sb, vmax_rows, d),
-            (sec_sb, sec_rows, d),
-            (sec_sb, sec_rows, c),
-            (par_sb, par_rows, a),
-            (par_sb, par_rows, c),
-            (par_sb, par_rows, b),
-            (par_sb, par_rows, d),
-        ):
-            nc.sync.dma_start(tiles[t][:], rows[:, t, :])
+        nc.sync.dma_start(w_raw[1][:], w_halves[1])
+        nc.sync.dma_start(ent_sb[:], ent)
+        a, b, c, d = PLANE_ORDER
+        order = [("vmax", a), ("sec", a), ("vmax", b), ("sec", b), ("par", a)]
+        for before, t in ((b, c), (c, d)):
+            order.extend([("sec", t), ("vmax", t), ("par", before)])
+        order.append(("par", d))
+        for name, t in order:
+            nc.sync.dma_start(table[name, t][:], rows[name][:, t, :])
 
-        x_picked = keep.tile([P, S], U32, name="x_picked", align_bytes=64)
-        xs_picked = keep.tile([P, S], U8, name="xs_picked", align_bytes=64)
+        x_picked = place("x_picked", [P, S], U32)
+        xs_picked = place("xs_picked", [P, S], U8)
+        w_codes = place("w_codes", [P, N], U32)
+        w_scales = place("w_scales", [P, N], U8)
+        w_rows = [raw[:].rearrange("p j (m t) -> p m j t", t=PACK) for raw in w_raw]
+        rounded = [place("w_rounded%d" % h, [P, 2 * N], BF16) for h in range(2)]
+        dealt = [r[:].rearrange("p (t m j) -> p m j t", t=2, j=PACK) for r in rounded]
+
+        def quantise_w(t):
+            cols = slice(t * P, (t + 1) * P)
+            nc.vector.quantize_mx(
+                out=w_codes[:, cols].bitcast(FP8X4), scales=w_scales[:, cols], in_=rounded[t // 2][:, (t % 2) * N : (t % 2 + 1) * N]
+            )
+
+        nc.vector.tensor_copy(dealt[1][:, :, 0:2, :], w_rows[0][:, :, :, 2:4])
+        nc.scalar.copy(dealt[0][:, :, 0:2, :], w_rows[0][:, :, :, 0:2])
         nc.vector.tensor_copy(xs_picked[:], xs_table[:].indirect(offs_sb[:]))
         nc.vector.tensor_copy(x_picked[:], x_table[:].bitcast(U32).indirect(offs_sb[:]))
-        w_codes = keep.tile([P, N], U32, name="w_codes", align_bytes=64)
-        w_scales = keep.tile([P, N], U8, name="w_scales", align_bytes=64)
-        w_grouped = [keep.tile([P, N * 2], BF16, name="w_grouped%d" % i, align_bytes=64) for i in range(2)]
-        w_dealt = [g[:].rearrange("p (t m j) -> p m j t", t=2, j=PACK) for g in w_grouped]
-        for i in range(2):
-            w_rows = w_raw[i][:].rearrange("p j (m t) -> p m j t", t=PACK)
-            for lo, hi in ((0, 2),) if i == 0 else ((0, 1), (1, 2)):
-                nc.vector.tensor_copy(w_dealt[1][:, :, 2 * i : 2 * i + 2, lo:hi], w_rows[:, :, :, 2 + lo : 2 + hi])
-            if i == 0:
-                nc.scalar.copy(w_dealt[0][:, :, 0:2, :], w_rows[:, :, :, 0:2])
-            else:
-                nc.scalar.copy(w_dealt[0][:, 0:96, 2:4, :], w_rows[:, 0:96, :, 0:2])
-                nc.vector.tensor_copy(w_dealt[0][:, 96:P, 2:4, :], w_rows[:, 96:P, :, 0:2])
-        for lo, hi in ((2, 3), (3, 4), (0, 2)):
-            cols = slice(lo * P, hi * P)
-            rounded = w_grouped[lo // 2][:, (lo % 2) * P * PACK : (hi - lo // 2 * 2) * P * PACK]
-            nc.vector.quantize_mx(out=w_codes[:, cols].bitcast(FP8X4), scales=w_scales[:, cols], in_=rounded)
+        nc.vector.tensor_copy(dealt[1][:, :, 2:4, 0:1], w_rows[1][:, :, :, 2:3])
+        nc.scalar.copy(dealt[0][:, :, 2:4, 0:1], w_rows[1][:, :, :, 0:1])
+        quantise_w(a)
+        nc.vector.tensor_copy(dealt[1][:, :, 2:4, 1:2], w_rows[1][:, :, :, 3:4])
+        nc.vector.tensor_copy(dealt[0][:, :, 2:4, 1:2], w_rows[1][:, :, :, 1:2])
+        for t in (b, d, c):
+            quantise_w(t)
 
-        y, y_sq = {}, {}
+        y = {}
         for t in PLANE_ORDER:
             y[t] = psum.tile([P, S], F32, name="y%d" % t, tag="y%d" % t)
             cols = slice(t * P, (t + 1) * P)
@@ -113,193 +112,90 @@ def tile_picked_amsg8_none_po_kernel(
                 stop=True,
             )
 
-        half = S // 2
-        y_sb = {}
+        square, moment, largest, rate, vmax_at, par_at, step = {}, {}, {}, {}, {}, {}, {}
 
-        def square(t, into):
-            y_sq[t] = into
+        def fetch(name, t, scale, tag):
+            picked = place("%s_at%d" % (name, t), [P, S], F32, tag=tag)
+            nc.scalar.activation(picked[:], table[name, t][:].indirect(ent_sb[:]), ACT.Copy, scale=scale)
+            return picked[:]
+
+        def make_square(t, into):
+            square[t] = into
             nc.scalar.activation(into, y[t][:], ACT.Square, scale=math.sqrt(0.125 / 0.875))
 
-        def negate(t, into):
-            y_sb[t] = into
-            nc.scalar.activation(into, y[t][:], ACT.Copy, scale=-1.0)
-
-        grouped_all = keep.tile([P, 3, 2 * CHUNK * PACK], BF16, name="grouped_all", align_bytes=64)
-        grouped = [grouped_all[:, 0, :], grouped_all[:, 2, :]]
-        grouped_t = [g.rearrange("p (c t) -> p c t", t=PACK) for g in grouped]
-        grouped_both = grouped_all[:, 0:3:2, :].rearrange("p h (c t) -> p h c t", t=PACK)
-        gap = grouped_all[:, 1, :].bitcast(F32)[:, 0:S]
-        halves = [(slice(h * half, (h + 1) * half), slice(h * S // 32, (h + 1) * S // 32)) for h in range(2)]
-        blocks = [slice(k * P, (k + 1) * P) for k in range(S // P)]
-        strip_first = keep.tile([P, 3 * half], F32, name="strip_first")
-        strip_third = keep.tile([P, 5 * half], F32, name="strip_third")
-        strip = keep.tile([P, 2816], F32, name="strip")
-        step_second = strip[:, 0:2176].rearrange("p (k c) -> p k c", k=2)[:, :, 0:half]
-        step_third = (strip[:, 1216:1472], strip[:, 1408:1664])
-        square_last = strip[:, 1280:2816].rearrange("p (k c) -> p k c", k=2)[:, :, 0:half]
-        step = {a: strip_first[:, 0:S], d: strip[:, 1536:2048]}
-        moment = {t: keep.tile([P, S], F32, name="moment%d" % t)[:] for t in (a, b, c)}
-        moment[d] = strip_first[:, half : 3 * half]
-        rate = {b: keep.tile([P, S], F32, name="rate_second")[:]}
-        rate[a] = strip_third[:, half : 3 * half]
-        vmax_neg = {t: keep.tile([P, S], F32, name="vmax_neg%d" % t)[:] for t in PLANE_ORDER}
-        rate[c] = keep.tile([P, S], F32, name="rate_third")[:]
-        new, vmax_turned = {}, {}
-        clipped = {t: keep.tile([P, S], F32, name="clipped%d" % t)[:] for t in (a, b, c)}
-        clipped[d] = gap
-        excess, largest = {}, {}
-
-        def turn(bank, values, start, stop):
-            for k, block in enumerate(blocks):
-                nc.tensor.matmul(
-                    bank[:, block],
-                    values[:, block],
-                    identity[:],
-                    start=start and k == 0,
-                    stop=stop and k == len(blocks) - 1,
-                    is_transpose=True,
-                )
-
-        def add_to_excess(t, values, tag):
-            first = t not in excess
-            if first:
-                excess[t] = psum.tile([P, S], F32, name="excess%d" % t, tag=tag)
-            turn(excess[t], values, first, not first)
-
-        def gather_vmax(t):
-            nc.vector.tensor_scalar(vmax_neg[t], vmax_sb[t][:].indirect(ent_sb[:]), -1.0 / 0.875, 0.0, ALU.mult, ALU.add)
-
-        def gather_sec_half(t, h, squares):
-            cols, part = halves[h]
-            nc.vector.tensor_tensor(moment[t][:, cols], sec_sb[t][:].indirect(ent_sb[:, part]), squares, ALU.add)
-
-        def turn_vmax(t, largest_tag):
-            largest[t] = psum.tile([P, S], F32, name="largest%d" % t, tag=largest_tag)
-            vmax_turned[t] = keep.tile([P, S], F32, name="vmax_turned%d" % t, tag="w_raw1" if t == a else "vmax_turned%d" % t)
-            turn(largest[t], vmax_neg[t], True, True)
-            nc.scalar.activation(vmax_turned[t][:], largest[t][:], ACT.Copy, scale=-1.0)
-
-        def gather_sec(t, excess_tag):
-            nc.vector.tensor_tensor(moment[t], sec_sb[t][:].indirect(ent_sb[:]), y_sq[t], ALU.add)
-            add_to_excess(t, moment[t], excess_tag)
-
-        def open_largest(t):
-            turn(largest[t], vmax_turned[t], True, False)
-
         def make_largest(t):
-            nc.scalar.activation(clipped[t], excess[t][:], ACT.Relu)
-            if t != a:
-                open_largest(t)
-            turn(largest[t], clipped[t], False, True)
+            largest[t] = place("largest%d" % t, [P, S], F32)
+            nc.vector.tensor_tensor(largest[t][:], moment[t][:], vmax_at[t], ALU.max)
 
-        def make_rate(t):
-            nc.scalar.activation(rate[t], largest[t][:], ACT.Abs_reciprocal_sqrt, scale=4.0 * 0.875)
+        def make_rate(t, into):
+            rate[t] = into
+            nc.scalar.activation(into, largest[t][:], ACT.Abs_reciprocal_sqrt, scale=4.0 * 0.875)
 
         def make_step(t):
-            nc.gpsimd.tensor_tensor(step[t], y_sb[t], rate[t], ALU.mult)
-
-        def gather_par(t, h):
-            cols, part = halves[h]
-            nc.vector.tensor_tensor(new[t][:, cols], par_sb[t][:].indirect(ent_sb[:, part]), step[t][:, cols], ALU.add)
+            step[t] = place("step%d" % t, [P, S], F32, tag="step")
+            nc.vector.scalar_tensor_tensor(step[t][:], y[t][:], -1.0, rate[t], ALU.mult, ALU.mult)
 
         def scatter(t):
-            nc.vector.tensor_copy(par_sb[t][:].indirect(ent_sb[:]), new[t])
-            nc.sync.dma_start(out_rows[:, t, :], par_sb[t][:])
+            par_at[t] = fetch("par", t, 1.0, "largest%d" % d if t == d else "moment%d" % a)
+            nc.vector.tensor_tensor(table["par", t][:].indirect(ent_sb[:]), par_at[t], step[t][:], ALU.add)
+            nc.sync.dma_start(out_rows[:, t, :], table["par", t][:])
 
-        def round_first(t):
-            both = par_sb[t][:].rearrange("p (h c) -> p h c", h=2)
-            for i in range(4):
-                cols = slice(i * P, (i + 1) * P)
-                nc.scalar.copy(grouped_both[:, :, cols, t], both[:, :, cols])
-
-        def round_plane(t):
-            for h in range(2):
-                nc.scalar.copy(grouped_t[h][:, :, t], par_sb[t][:, h * U // 2 : (h + 1) * U // 2])
-
-        gather_vmax(a)
-        turn_vmax(a, "bank1")
-        add_to_excess(a, vmax_neg[a], "bank0")
-        open_largest(a)
         for t in (a, b):
-            square(t, keep.tile([P, S], F32, name="y_sq%d" % t)[:])
-        gather_vmax(b)
-        turn_vmax(b, "bank2")
-        gather_sec(a, "bank0")
-        make_largest(a)
-        make_rate(a)
-        negate(b, clipped[a])
-        square(c, step[a])
-        nc.scalar.activation(
-            square_last, y[d][:].rearrange("p (k c) -> p k c", k=2), ACT.Square, scale=math.sqrt(0.125 / 0.875)
-        )
-        negate(d, keep.tile([P, S], F32, name="y_last")[:])
-        gather_sec(b, "bank0")
-        add_to_excess(b, vmax_neg[b], "bank0")
-        make_largest(b)
-        make_rate(b)
-        gather_vmax(c)
-        turn_vmax(c, "bank3")
-        add_to_excess(c, vmax_neg[c], "bank1")
-        gather_vmax(d)
-        gather_sec_half(d, 1, square_last[:, 1, :])
-        for h in (1, 0):
-            gather_sec_half(c, h, y_sq[c][:, halves[h][0]])
-        add_to_excess(c, moment[c], "bank1")
-        for h in (1, 0):
-            cols = halves[h][0]
-            nc.vector.scalar_tensor_tensor(step[a][:, cols], y[a][:, cols], -1.0, rate[a][:, cols], ALU.mult, ALU.mult)
-        negate(c, strip_third[:, S : 2 * S])
-        make_largest(c)
-        make_rate(c)
-        turn_vmax(d, "bank2")
-        add_to_excess(d, vmax_neg[d], "bank0")
-        new[a] = keep.tile([P, S], F32, name="new_first")[:]
-        new[b] = strip_third[:, 3 * half : 5 * half]
-        gather_par(a, 1)
-        gather_par(a, 0)
-        gather_sec_half(d, 0, square_last[:, 0, :])
-        add_to_excess(d, moment[d], "bank0")
-        nc.gpsimd.tensor_tensor(
-            step_second, y_sb[b].rearrange("p (k c) -> p k c", k=2), rate[b].rearrange("p (k c) -> p k c", k=2), ALU.mult
-        )
-        nc.gpsimd.tensor_tensor(step_third[1], y_sb[c][:, halves[1][0]], rate[c][:, halves[1][0]], ALU.mult)
-        rate[d] = strip[:, 256:768]
-        make_largest(d)
-        make_rate(d)
+            vmax_at[t] = fetch("vmax", t, 1.0 / 0.875, "vmax_first" if t == a else "vmax_at")
+            make_square(t, place("square%d" % t, [P, S], F32)[:])
+            moment[t] = place("moment%d" % t, [P, S], F32)
+            nc.vector.tensor_tensor(moment[t][:], table["sec", t][:].indirect(ent_sb[:]), square[t], ALU.add)
+            if t == b:
+                make_step(a)
+            make_largest(t)
+            if t == a:
+                make_rate(a, place("rate_first", [P, S], F32)[:])
         scatter(a)
-        for h in (1, 0):
-            cols, part = halves[h]
-            nc.vector.tensor_tensor(new[b][:, cols], par_sb[b][:].indirect(ent_sb[:, part]), step_second[:, h, :], ALU.add)
-        round_first(a)
-        new[c] = strip[:, 640:1152]
-        nc.vector.tensor_tensor(new[c][:, halves[1][0]], par_sb[c][:].indirect(ent_sb[:, halves[1][1]]), step_third[1], ALU.add)
-        nc.gpsimd.tensor_tensor(step_third[0], y_sb[c][:, halves[0][0]], rate[c][:, halves[0][0]], ALU.mult)
-        make_step(d)
-        scatter(b)
-        round_plane(b)
-        nc.vector.tensor_tensor(new[c][:, halves[0][0]], par_sb[c][:].indirect(ent_sb[:, halves[0][1]]), step_third[0], ALU.add)
-        new[d] = gap
-        nc.vector.tensor_tensor(new[d], par_sb[d][:].indirect(ent_sb[:]), step[d], ALU.add)
-        scatter(c)
-        round_plane(c)
-        scatter(d)
+        for before, t in ((b, c), (c, d)):
+            sec_at = fetch("sec", t, 1.0, "rate_first")
+            freed = place("freed%d" % t, [P, 2, S], F32, tag="sec%d" % t)
+            make_square(t, freed[:, 0, :])
+            make_rate(before, freed[:, 1, :])
+            moment[t] = place("moment%d" % t, [P, S], F32)
+            nc.vector.tensor_tensor(moment[t][:], sec_at, square[t], ALU.add)
+            make_step(before)
+            vmax_at[t] = fetch("vmax", t, 1.0 / 0.875, "vmax_at")
+            make_largest(t)
+            scatter(before)
 
-        out_codes = keep.tile([P, U], U32, name="out_codes", align_bytes=64)
-        out_scales = keep.tile([P, U], U8, name="out_scales", align_bytes=64)
         chunks = [slice(i * CHUNK, (i + 1) * CHUNK) for i in range(U // CHUNK)]
-        for i, cols in enumerate(chunks):
-            into = grouped_t[i // 2][:, chunks[i % 2], d]
-            if i < 2:
-                nc.vector.tensor_copy(into, par_sb[d][:, cols])
-            else:
-                nc.scalar.copy(into, par_sb[d][:, cols])
+        pairs = [late.tile([P, 2, CHUNK, 2], BF16, name="pairs%d" % i, offset=2048 * i) for i in range(len(chunks))]
+
+        def round_plane(t, i, copy):
+            copy(pairs[i][:, t // 2, :, t % 2], table["par", t][:, chunks[i]])
+
+        make_rate(d, place("rate_last", [P, S], F32)[:])
+        round_plane(a, 0, nc.vector.tensor_copy)
+        make_step(d)
+        round_plane(a, 1, nc.vector.tensor_copy)
+        scatter(d)
+        for i in (2, 3):
+            round_plane(a, i, nc.scalar.copy)
+        for t in (b, c):
+            for i in range(len(chunks)):
+                round_plane(t, i, nc.scalar.copy)
+
+        out_codes = place("out_codes", [P, U], U32)
+        out_scales = place("out_scales", [P, U], U8)
+        grouped = [place("grouped%d" % i, [P, CHUNK * PACK], BF16) for i in range(len(chunks))]
+        movers = [(nc.vector.tensor_copy, I32)] * 2 + [(nc.scalar.copy, U32)] * 2
+        for i in (0, 1, 2):
+            round_plane(d, i, movers[i][0])
+        for i, (copy, word) in enumerate(movers):
+            if i == 3:
+                round_plane(d, i, copy)
+            copy(
+                grouped[i][:].bitcast(word).rearrange("p (c h) -> p c h", h=2),
+                pairs[i][:].rearrange("p h c e -> p h (c e)").bitcast(word).rearrange("p h c -> p c h"),
+            )
         words_out = out_1[0].rearrange("p c r -> p (c r)").bitcast(I32)
         for i, cols in enumerate(chunks):
-            nc.vector.quantize_mx(
-                out=out_codes[:, cols].bitcast(FP8X4),
-                scales=out_scales[:, cols],
-                in_=grouped[i // 2][:, (i % 2) * CHUNK * PACK : (i % 2 + 1) * CHUNK * PACK],
-            )
+            nc.vector.quantize_mx(out=out_codes[:, cols].bitcast(FP8X4), scales=out_scales[:, cols], in_=grouped[i][:])
             if i > 0:
                 ready = slice(0 if i == 1 else cols.start, cols.stop)
                 nc.sync.dma_start(words_out[:, ready], out_codes[:, ready].bitcast(I32))

@@ -2,6 +2,7 @@ import math
 from contextlib import ExitStack
 
 import concourse.mybir as mybir
+from concourse.masks import make_identity
 
 F32 = mybir.dt.float32
 BF16 = mybir.dt.bfloat16
@@ -32,15 +33,11 @@ def tile_picked_amsg8_none_po_kernel(
         psum = ctx.enter_context(tc.psum_pool(name="psum", bufs=1))
 
         def place(name, shape, dtype, tag=None):
-            if name == "moment3":
-                return late.tile(shape, dtype, name=name, offset=1024)
-            if tag == "vmax_at":
-                return late.tile(shape, dtype, name=name, tag=tag, offset=5120)
             return keep.tile(shape, dtype, name=name, tag=tag or name, align_bytes=64)
 
         offs_sb = lists.tile([P, S // 16], U16, name="offs_sb")
         ent_sb = lists.tile([P, S // 16], U16, name="ent_sb")
-        w_raw = [place("w_raw%d" % i, [P, 2, N], F32) for i in range(2)]
+        w_raw = place("w_raw", [P, PACK, N], F32)
         x_table = place("x_table", [P, T], I32)
         xs_table = place("xs_table", [P, T], U8)
         nc.gpsimd.memset(xs_table[:].bitcast(I32), 0)
@@ -49,68 +46,74 @@ def tile_picked_amsg8_none_po_kernel(
         nc.gpsimd.memset(one[:, 0:1], 1.0)
         nc.scalar.activation(one[:, 1:2], one[:, 0:1], ACT.Abs_reciprocal_sqrt)
 
+        identity = place("identity", [P, P], F32)
+        make_identity(nc, identity[:])
+
+        root_scale = late.tile([P, 16], F32, name="root_scale", offset=2048 - 32)
+        root_bias = late.tile([P, 16], F32, name="root_bias", offset=3 * 2048 - 32)
+        nc.gpsimd.memset(root_scale[:, 0:1], 4.0 * 0.875)
+        nc.gpsimd.memset(root_bias[:, 0:1], 0.0)
+
         rows = {name: ap.rearrange("(p t) u -> p t u", t=PACK) for name, ap in (("par", par), ("sec", sec), ("vmax", vmax))}
         out_rows = out_0.rearrange("(p t) u -> p t u", t=PACK)
         table = {(name, t): place("%s%d" % (name, t), [P, U], F32) for name in rows for t in range(PACK)}
 
         nc.sync.dma_start(offs_sb[:], offs)
-        w_halves = w1.rearrange("(p i j) c -> i p j c", i=2, j=2)
-        nc.sync.dma_start(w_raw[0][:], w_halves[0])
+        w_dealt = w1.rearrange("(p j) c -> p j c", j=PACK)
+        nc.sync.dma_start(w_raw[:, 0:2, :], w_dealt[:, 0:2, :])
         for q in range(4):
             nc.sync.dma_start(
                 xs_table[32 * q : 32 * q + 4, :].bitcast(I32),
                 x_scales[0, 4 * q : 4 * q + 4, :].bitcast(I32),
             )
+        nc.sync.dma_start(w_raw[:, 2:4, :], w_dealt[:, 2:4, :])
         nc.sync.dma_start(x_table[:], x_words[0].rearrange("p c r -> p (c r)").bitcast(I32))
-        nc.sync.dma_start(w_raw[1][:], w_halves[1])
         nc.sync.dma_start(ent_sb[:], ent)
         a, b, c, d = PLANE_ORDER
         order = [("vmax", a), ("sec", a), ("vmax", b), ("sec", b), ("par", a)]
-        for before, t in ((b, c), (c, d)):
-            order.extend([("sec", t), ("vmax", t), ("par", before)])
-        order.append(("par", d))
+        order.extend([("sec", c), ("vmax", c), ("par", b), ("vmax", d), ("par", c), ("sec", d), ("par", d)])
         for name, t in order:
             nc.sync.dma_start(table[name, t][:], rows[name][:, t, :])
 
+        half = S // 2
+        halves = [(slice(h * half, (h + 1) * half), slice(h * half // 16, (h + 1) * half // 16)) for h in range(2)]
         x_picked = place("x_picked", [P, S], U32)
         xs_picked = place("xs_picked", [P, S], U8)
-        w_codes = place("w_codes", [P, N], U32)
-        w_scales = place("w_scales", [P, N], U8)
-        w_rows = [raw[:].rearrange("p j (m t) -> p m j t", t=PACK) for raw in w_raw]
-        rounded = [place("w_rounded%d" % h, [P, 2 * N], BF16) for h in range(2)]
-        dealt = [r[:].rearrange("p (t m j) -> p m j t", t=2, j=PACK) for r in rounded]
-
-        def quantise_w(t):
-            cols = slice(t * P, (t + 1) * P)
-            nc.vector.quantize_mx(
-                out=w_codes[:, cols].bitcast(FP8X4), scales=w_scales[:, cols], in_=rounded[t // 2][:, (t % 2) * N : (t % 2 + 1) * N]
-            )
-
-        nc.vector.tensor_copy(dealt[1][:, :, 0:2, :], w_rows[0][:, :, :, 2:4])
-        nc.scalar.copy(dealt[0][:, :, 0:2, :], w_rows[0][:, :, :, 0:2])
         nc.vector.tensor_copy(xs_picked[:], xs_table[:].indirect(offs_sb[:]))
-        nc.vector.tensor_copy(x_picked[:], x_table[:].bitcast(U32).indirect(offs_sb[:]))
-        nc.vector.tensor_copy(dealt[1][:, :, 2:4, 0:1], w_rows[1][:, :, :, 2:3])
-        nc.scalar.copy(dealt[0][:, :, 2:4, 0:1], w_rows[1][:, :, :, 0:1])
-        quantise_w(a)
-        nc.vector.tensor_copy(dealt[1][:, :, 2:4, 1:2], w_rows[1][:, :, :, 3:4])
-        nc.vector.tensor_copy(dealt[0][:, :, 2:4, 1:2], w_rows[1][:, :, :, 1:2])
-        for t in (b, d, c):
-            quantise_w(t)
+        w_codes = {t: place("w_codes%d" % t, [P, P], U32) for t in PLANE_ORDER}
+        w_scales = place("w_scales", [P, N], U8)
+        w_rows = w_raw[:].rearrange("p j (m t) -> p m j t", t=PACK)
+        for i, round_w in ((1, nc.vector.tensor_copy), (0, nc.scalar.copy)):
+            rounded = place("w_rounded%d" % i, [P, 2 * N], BF16)
+            round_w(rounded[:].rearrange("p (t m j) -> p m j t", t=2, j=PACK), w_rows[:, :, :, 2 * i : 2 * i + 2])
+            for t in (2 * i, 2 * i + 1):
+                nc.vector.quantize_mx(
+                    out=w_codes[t][:].bitcast(FP8X4),
+                    scales=w_scales[:, t * P : (t + 1) * P],
+                    in_=rounded[:, (t % 2) * N : (t % 2 + 1) * N],
+                )
 
-        y = {}
-        for t in PLANE_ORDER:
-            y[t] = psum.tile([P, S], F32, name="y%d" % t, tag="y%d" % t)
+        def product(bank, t, tokens):
             cols = slice(t * P, (t + 1) * P)
             nc.tensor.matmul_mx(
-                out=y[t][:],
-                lhsT=w_codes[:, cols].bitcast(FP8X4),
+                out=bank,
+                lhsT=w_codes[t][:].bitcast(FP8X4),
                 lhsT_scale=w_scales[:, cols],
-                rhs=x_picked[:].bitcast(FP8X4),
-                rhs_scale=xs_picked[:],
+                rhs=x_picked[:, tokens].bitcast(FP8X4),
+                rhs_scale=xs_picked[:, tokens],
                 start=True,
                 stop=True,
             )
+
+        y_first = []
+        for h, (tokens, part) in enumerate(halves):
+            nc.vector.tensor_copy(x_picked[:, tokens], x_table[:].bitcast(U32).indirect(offs_sb[:, part]))
+            y_first.append(psum.tile([P, half], F32, name="y_first%d" % h, tag="y_first%d" % h))
+            product(y_first[h][:], a, tokens)
+        y = {}
+        for t in (b, c, d):
+            y[t] = psum.tile([P, S], F32, name="y%d" % t, tag="y%d" % t)
+            product(y[t][:], t, slice(0, S))
 
         square, moment, largest, rate, vmax_at, par_at, step = {}, {}, {}, {}, {}, {}, {}
 
@@ -136,32 +139,57 @@ def tile_picked_amsg8_none_po_kernel(
             nc.vector.scalar_tensor_tensor(step[t][:], y[t][:], -1.0, rate[t], ALU.mult, ALU.mult)
 
         def scatter(t):
-            par_at[t] = fetch("par", t, 1.0, "largest%d" % d if t == d else "moment%d" % a)
             nc.vector.tensor_tensor(table["par", t][:].indirect(ent_sb[:]), par_at[t], step[t][:], ALU.add)
             nc.sync.dma_start(out_rows[:, t, :], table["par", t][:])
 
-        for t in (a, b):
-            vmax_at[t] = fetch("vmax", t, 1.0 / 0.875, "vmax_first" if t == a else "vmax_at")
-            make_square(t, place("square%d" % t, [P, S], F32)[:])
-            moment[t] = place("moment%d" % t, [P, S], F32)
-            nc.vector.tensor_tensor(moment[t][:], table["sec", t][:].indirect(ent_sb[:]), square[t], ALU.add)
-            if t == b:
-                make_step(a)
-            make_largest(t)
-            if t == a:
-                make_rate(a, place("rate_first", [P, S], F32)[:])
+        square[a] = place("square_first", [P, S], F32)
+        moment[a] = place("moment%d" % a, [P, S], F32)
+        largest[a] = place("largest%d" % a, [P, S], F32)
+        vmax_first = place("vmax_first", [P, S], F32)
+        nc.vector.tensor_scalar(vmax_first[:], table["vmax", a][:].indirect(ent_sb[:]), 1.0 / 0.875, 0.0, ALU.mult, ALU.add)
+        for h, (cols, part) in enumerate(halves):
+            nc.scalar.activation(square[a][:, cols], y_first[h][:], ACT.Square, scale=math.sqrt(0.125 / 0.875))
+            nc.vector.tensor_tensor(moment[a][:, cols], table["sec", a][:].indirect(ent_sb[:, part]), square[a][:, cols], ALU.add)
+        for h, (cols, part) in enumerate(halves):
+            nc.vector.tensor_tensor(largest[a][:, cols], moment[a][:, cols], vmax_first[:, cols], ALU.max)
+        make_square(b, place("square_second", [P, S], F32)[:])
+        make_square(c, place("square_third", [P, S], F32)[:])
+        vmax_at[b] = fetch("vmax", b, 1.0 / 0.875, "w_codes%d" % b)
+        make_rate(a, place("rate_first", [P, S], F32)[:])
+        moment[b] = place("moment%d" % b, [P, S], F32)
+        nc.vector.tensor_tensor(moment[b][:], table["sec", b][:].indirect(ent_sb[:]), square[b], ALU.add)
+        step[a] = place("step_first", [P, S], F32, tag="step")
+        for h, (cols, part) in enumerate(halves):
+            nc.vector.scalar_tensor_tensor(step[a][:, cols], y_first[h][:], -1.0, rate[a][:, cols], ALU.mult, ALU.mult)
+        make_largest(b)
+        par_at[a] = fetch("par", a, 1.0, "sec%d" % b)
         scatter(a)
-        for before, t in ((b, c), (c, d)):
-            sec_at = fetch("sec", t, 1.0, "rate_first")
-            freed = place("freed%d" % t, [P, 2, S], F32, tag="sec%d" % t)
-            make_square(t, freed[:, 0, :])
-            make_rate(before, freed[:, 1, :])
-            moment[t] = place("moment%d" % t, [P, S], F32)
-            nc.vector.tensor_tensor(moment[t][:], sec_at, square[t], ALU.add)
-            make_step(before)
-            vmax_at[t] = fetch("vmax", t, 1.0 / 0.875, "vmax_at")
-            make_largest(t)
-            scatter(before)
+
+        terms = place("terms%d" % c, [P, 2, S], F32, tag="rate_first")
+        nc.scalar.activation(terms[:, 0, :], table["sec", c][:].indirect(ent_sb[:]), ACT.Copy)
+        make_square(d, terms[:, 1, :])
+        make_rate(b, place("rate_second", [P, S], F32, tag="sec%d" % c)[:])
+        moment[c] = place("moment%d" % c, [P, S], F32)
+        nc.vector.tensor_tensor(moment[c][:], terms[:, 0, :], square[c], ALU.add)
+        make_step(b)
+        vmax_at[c] = fetch("vmax", c, 1.0 / 0.875, "moment%d" % b)
+        make_largest(c)
+        par_at[b] = fetch("par", b, 1.0, "sec%d" % b)
+        scatter(b)
+
+        blocks = [slice(k * P, (k + 1) * P) for k in range(S // P)]
+
+        def turn(bank, terms):
+            for i, values in enumerate(terms):
+                for k, block in enumerate(blocks):
+                    nc.tensor.matmul(
+                        bank[:, block],
+                        values[:, block],
+                        identity[:],
+                        start=i == 0 and k == 0,
+                        stop=i == len(terms) - 1 and k == len(blocks) - 1,
+                        is_transpose=True,
+                    )
 
         chunks = [slice(i * CHUNK, (i + 1) * CHUNK) for i in range(U // CHUNK)]
         pairs = [late.tile([P, 2, CHUNK, 2], BF16, name="pairs%d" % i, offset=2048 * i) for i in range(len(chunks))]
@@ -169,7 +197,25 @@ def tile_picked_amsg8_none_po_kernel(
         def round_plane(t, i, copy):
             copy(pairs[i][:, t // 2, :, t % 2], table["par", t][:, chunks[i]])
 
-        make_rate(d, place("rate_last", [P, S], F32)[:])
+        vmax_neg = fetch("vmax", d, -1.0 / 0.875, "square_third")
+        make_rate(c, place("rate_third", [P, S], F32)[:])
+        par_at[c] = fetch("par", c, 1.0, "moment%d" % c)
+        sec_last = fetch("sec", d, 1.0, "largest%d" % c)
+        make_step(c)
+        scatter(c)
+        neg_turned = psum.tile([P, S], F32, name="neg_turned", tag="neg_turned")
+        excess = psum.tile([P, S], F32, name="excess", tag="excess")
+        largest[d] = psum.tile([P, S], F32, name="largest_last", tag="largest_last")
+        turn(neg_turned, [vmax_neg])
+        turn(excess, [vmax_neg, square[d], sec_last])
+        vmax_turned = place("vmax_turned", [P, S], F32, tag="sec%d" % d)
+        nc.scalar.activation(vmax_turned[:], neg_turned[:], ACT.Copy, scale=-1.0)
+        clipped = place("clipped", [P, S], F32)
+        nc.scalar.activation(clipped[:], excess[:], ACT.Relu)
+        turn(largest[d], [vmax_turned[:], clipped[:]])
+        par_at[d] = fetch("par", d, 1.0, "sec%d" % d)
+        rate[d] = place("rate_last", [P, S], F32)[:]
+        nc.scalar.activation(rate[d], largest[d][:], ACT.Abs_reciprocal_sqrt, scale=root_scale[:, 0:1], bias=root_bias[:, 0:1])
         round_plane(a, 0, nc.vector.tensor_copy)
         make_step(d)
         round_plane(a, 1, nc.vector.tensor_copy)

@@ -70,7 +70,7 @@ def tile_picked_amsg8_none_po_kernel(
         nc.sync.dma_start(x_table[:], x_words[0].rearrange("p c r -> p (c r)").bitcast(I32))
         nc.sync.dma_start(ent_sb[:], ent)
         a, b, c, d = PLANE_ORDER
-        order = [("vmax", a), ("sec", a), ("vmax", b), ("sec", b), ("par", a)]
+        order = [("vmax", a), ("sec", a), ("sec", b), ("par", a), ("vmax", b)]
         order.extend([("sec", c), ("vmax", c), ("par", b), ("vmax", d), ("par", c), ("sec", d), ("par", d)])
         for name, t in order:
             nc.sync.dma_start(table[name, t][:], rows[name][:, t, :])
@@ -135,7 +135,7 @@ def tile_picked_amsg8_none_po_kernel(
             nc.scalar.activation(into, largest[t][:], ACT.Abs_reciprocal_sqrt, scale=4.0 * 0.875)
 
         def make_step(t):
-            step[t] = place("step%d" % t, [P, S], F32, tag="step")
+            step[t] = place("step%d" % t, [P, S], F32, tag="step_late" if t in (c, d) else None)
             nc.vector.scalar_tensor_tensor(step[t][:], y[t][:], -1.0, rate[t], ALU.mult, ALU.mult)
 
         def scatter(t):
@@ -152,29 +152,27 @@ def tile_picked_amsg8_none_po_kernel(
             nc.vector.tensor_tensor(moment[a][:, cols], table["sec", a][:].indirect(ent_sb[:, part]), square[a][:, cols], ALU.add)
         for h, (cols, part) in enumerate(halves):
             nc.vector.tensor_tensor(largest[a][:, cols], moment[a][:, cols], vmax_first[:, cols], ALU.max)
-        make_square(b, place("square_second", [P, S], F32)[:])
-        make_square(c, place("square_third", [P, S], F32)[:])
-        vmax_at[b] = fetch("vmax", b, 1.0 / 0.875, "w_codes%d" % b)
+        for t in (b, c, d):
+            make_square(t, place("square%d" % t, [P, S], F32)[:])
         make_rate(a, place("rate_first", [P, S], F32)[:])
         moment[b] = place("moment%d" % b, [P, S], F32)
         nc.vector.tensor_tensor(moment[b][:], table["sec", b][:].indirect(ent_sb[:]), square[b], ALU.add)
-        step[a] = place("step_first", [P, S], F32, tag="step")
+        step[a] = place("step_first", [P, S], F32)
         for h, (cols, part) in enumerate(halves):
             nc.vector.scalar_tensor_tensor(step[a][:, cols], y_first[h][:], -1.0, rate[a][:, cols], ALU.mult, ALU.mult)
-        make_largest(b)
-        par_at[a] = fetch("par", a, 1.0, "sec%d" % b)
+        par_at[a] = fetch("par", a, 1.0, "moment%d" % a)
         scatter(a)
 
-        terms = place("terms%d" % c, [P, 2, S], F32, tag="rate_first")
-        nc.scalar.activation(terms[:, 0, :], table["sec", c][:].indirect(ent_sb[:]), ACT.Copy)
-        make_square(d, terms[:, 1, :])
-        make_rate(b, place("rate_second", [P, S], F32, tag="sec%d" % c)[:])
+        vmax_at[b] = fetch("vmax", b, 1.0 / 0.875, "sec%d" % b)
+        sec_third = fetch("sec", c, 1.0, "rate_first")
+        vmax_at[c] = fetch("vmax", c, 1.0 / 0.875, "largest%d" % a)
+        make_largest(b)
+        make_rate(b, place("rate_second", [P, S], F32, tag="vmax%d" % c)[:])
         moment[c] = place("moment%d" % c, [P, S], F32)
-        nc.vector.tensor_tensor(moment[c][:], terms[:, 0, :], square[c], ALU.add)
+        nc.vector.tensor_tensor(moment[c][:], sec_third, square[c], ALU.add)
         make_step(b)
-        vmax_at[c] = fetch("vmax", c, 1.0 / 0.875, "moment%d" % b)
         make_largest(c)
-        par_at[b] = fetch("par", b, 1.0, "sec%d" % b)
+        par_at[b] = fetch("par", b, 1.0, "moment%d" % a)
         scatter(b)
 
         blocks = [slice(k * P, (k + 1) * P) for k in range(S // P)]
@@ -197,8 +195,8 @@ def tile_picked_amsg8_none_po_kernel(
         def round_plane(t, i, copy):
             copy(pairs[i][:, t // 2, :, t % 2], table["par", t][:, chunks[i]])
 
-        vmax_neg = fetch("vmax", d, -1.0 / 0.875, "square_third")
-        make_rate(c, place("rate_third", [P, S], F32)[:])
+        vmax_neg = fetch("vmax", d, -1.0 / 0.875, "square%d" % c)
+        make_rate(c, place("rate_third", [P, S], F32, tag="vmax%d" % d)[:])
         par_at[c] = fetch("par", c, 1.0, "moment%d" % c)
         sec_last = fetch("sec", d, 1.0, "largest%d" % c)
         make_step(c)

@@ -71,7 +71,7 @@ def tile_picked_amsg8_none_po_kernel(
         nc.sync.dma_start(ent_sb[:], ent)
         a, b, c, d = PLANE_ORDER
         order = [("vmax", a), ("sec", a), ("sec", b), ("par", a), ("vmax", b)]
-        order.extend([("sec", c), ("vmax", c), ("par", b), ("vmax", d), ("par", c), ("sec", d), ("par", d)])
+        order.extend([("par", b), ("vmax", c), ("sec", c), ("vmax", d), ("par", c), ("sec", d), ("par", d)])
         for name, t in order:
             nc.sync.dma_start(table[name, t][:], rows[name][:, t, :])
 
@@ -164,15 +164,14 @@ def tile_picked_amsg8_none_po_kernel(
         scatter(a)
 
         vmax_at[b] = fetch("vmax", b, 1.0 / 0.875, "sec%d" % b)
-        sec_third = fetch("sec", c, 1.0, "rate_first")
+        par_at[b] = fetch("par", b, 1.0, "rate_first")
         vmax_at[c] = fetch("vmax", c, 1.0 / 0.875, "largest%d" % a)
         make_largest(b)
         make_rate(b, place("rate_second", [P, S], F32, tag="vmax%d" % c)[:])
-        moment[c] = place("moment%d" % c, [P, S], F32)
-        nc.vector.tensor_tensor(moment[c][:], sec_third, square[c], ALU.add)
+        moment[c] = place("moment%d" % c, [P, S], F32, tag="step_first")
+        nc.vector.tensor_tensor(moment[c][:], table["sec", c][:].indirect(ent_sb[:]), square[c], ALU.add)
         make_step(b)
         make_largest(c)
-        par_at[b] = fetch("par", b, 1.0, "moment%d" % a)
         scatter(b)
 
         blocks = [slice(k * P, (k + 1) * P) for k in range(S // P)]
@@ -197,7 +196,7 @@ def tile_picked_amsg8_none_po_kernel(
 
         vmax_neg = fetch("vmax", d, -1.0 / 0.875, "square%d" % c)
         make_rate(c, place("rate_third", [P, S], F32, tag="vmax%d" % d)[:])
-        par_at[c] = fetch("par", c, 1.0, "moment%d" % c)
+        par_at[c] = fetch("par", c, 1.0, "step_first")
         sec_last = fetch("sec", d, 1.0, "largest%d" % c)
         make_step(c)
         scatter(c)

@@ -49,10 +49,13 @@ def tile_picked_amsg8_none_po_kernel(
         identity = place("identity", [P, P], F32)
         make_identity(nc, identity[:])
 
-        root_scale = late.tile([P, 16], F32, name="root_scale", offset=2048 - 32)
-        root_bias = late.tile([P, 16], F32, name="root_bias", offset=3 * 2048 - 32)
-        nc.gpsimd.memset(root_scale[:, 0:1], 4.0 * 0.875)
-        nc.gpsimd.memset(root_bias[:, 0:1], 0.0)
+        first_pairs = place("pairs0", [P, 2, CHUNK, 2], BF16)
+        first_words = first_pairs[:].rearrange("p h c e -> p (h c e)").bitcast(F32)
+        last_scale, third_scale = first_words[:, 0:1], first_words[:, CHUNK : CHUNK + 1]
+        root_bias = late.tile([P, 1, 2048 // 4 + 16], F32, name="root_bias", offset=2048 - 32)
+        nc.gpsimd.memset(last_scale, 4.0 * 0.875)
+        nc.gpsimd.memset(third_scale, 4.0 * 0.875)
+        nc.gpsimd.memset(root_bias[:, 0, 0:1], 0.0)
 
         rows = {name: ap.rearrange("(p t) u -> p t u", t=PACK) for name, ap in (("par", par), ("sec", sec), ("vmax", vmax))}
         out_rows = out_0.rearrange("(p t) u -> p t u", t=PACK)
@@ -128,14 +131,14 @@ def tile_picked_amsg8_none_po_kernel(
 
         def make_largest(t):
             largest[t] = place("largest%d" % t, [P, S], F32)
-            nc.vector.tensor_tensor(largest[t][:], moment[t][:], vmax_at[t], ALU.max)
+            nc.vector.tensor_tensor(largest[t][:], moment[t], vmax_at[t], ALU.max)
 
         def make_rate(t, into):
             rate[t] = into
             nc.scalar.activation(into, largest[t][:], ACT.Abs_reciprocal_sqrt, scale=4.0 * 0.875)
 
         def make_step(t):
-            step[t] = place("step%d" % t, [P, S], F32, tag="step_late" if t in (c, d) else None)
+            step[t] = place("step%d" % t, [P, S], F32)
             nc.vector.scalar_tensor_tensor(step[t][:], y[t][:], -1.0, rate[t], ALU.mult, ALU.mult)
 
         def scatter(t):
@@ -154,22 +157,30 @@ def tile_picked_amsg8_none_po_kernel(
             nc.vector.tensor_tensor(largest[a][:, cols], moment[a][:, cols], vmax_first[:, cols], ALU.max)
         for t in (b, c, d):
             make_square(t, place("square%d" % t, [P, S], F32)[:])
-        make_rate(a, place("rate_first", [P, S], F32)[:])
-        moment[b] = place("moment%d" % b, [P, S], F32)
-        nc.vector.tensor_tensor(moment[b][:], table["sec", b][:].indirect(ent_sb[:]), square[b], ALU.add)
+        strip = place("rate_first", [P, 3 * half], F32)
+        rate[a], moment[b] = strip[:, half : 3 * half], strip[:, 0:S]
+        for cols, part in halves:
+            nc.scalar.activation(rate[a][:, cols], largest[a][:, cols], ACT.Abs_reciprocal_sqrt, scale=4.0 * 0.875)
         step[a] = place("step_first", [P, S], F32)
+
+        def second_moment(h):
+            cols, part = halves[h]
+            nc.vector.tensor_tensor(moment[b][:, cols], table["sec", b][:].indirect(ent_sb[:, part]), square[b][:, cols], ALU.add)
+
+        second_moment(0)
         for h, (cols, part) in enumerate(halves):
             nc.vector.scalar_tensor_tensor(step[a][:, cols], y_first[h][:], -1.0, rate[a][:, cols], ALU.mult, ALU.mult)
+        second_moment(1)
         par_at[a] = fetch("par", a, 1.0, "moment%d" % a)
         scatter(a)
 
-        vmax_at[b] = fetch("vmax", b, 1.0 / 0.875, "sec%d" % b)
-        par_at[b] = fetch("par", b, 1.0, "rate_first")
+        vmax_at[b] = fetch("vmax", b, 1.0 / 0.875, "vmax_first")
+        par_at[b] = fetch("par", b, 1.0, "square%d" % b)
         vmax_at[c] = fetch("vmax", c, 1.0 / 0.875, "largest%d" % a)
         make_largest(b)
         make_rate(b, place("rate_second", [P, S], F32, tag="vmax%d" % c)[:])
-        moment[c] = place("moment%d" % c, [P, S], F32, tag="step_first")
-        nc.vector.tensor_tensor(moment[c][:], table["sec", c][:].indirect(ent_sb[:]), square[c], ALU.add)
+        moment[c] = place("moment%d" % c, [P, S], F32, tag="step_first")[:]
+        nc.vector.tensor_tensor(moment[c], table["sec", c][:].indirect(ent_sb[:]), square[c], ALU.add)
         make_step(b)
         make_largest(c)
         scatter(b)
@@ -189,16 +200,18 @@ def tile_picked_amsg8_none_po_kernel(
                     )
 
         chunks = [slice(i * CHUNK, (i + 1) * CHUNK) for i in range(U // CHUNK)]
-        pairs = [late.tile([P, 2, CHUNK, 2], BF16, name="pairs%d" % i, offset=2048 * i) for i in range(len(chunks))]
+        pairs = [first_pairs] + [late.tile([P, 2, CHUNK, 2], BF16, name="pairs%d" % i, offset=2048 * (i - 1)) for i in (1, 2, 3)]
 
         def round_plane(t, i, copy):
             copy(pairs[i][:, t // 2, :, t % 2], table["par", t][:, chunks[i]])
 
         vmax_neg = fetch("vmax", d, -1.0 / 0.875, "square%d" % c)
-        make_rate(c, place("rate_third", [P, S], F32, tag="vmax%d" % d)[:])
+        rate[c] = place("rate_third", [P, S], F32, tag="vmax%d" % d)[:]
+        nc.scalar.activation(rate[c], largest[c][:], ACT.Abs_reciprocal_sqrt, scale=third_scale)
         par_at[c] = fetch("par", c, 1.0, "step_first")
         sec_last = fetch("sec", d, 1.0, "largest%d" % c)
         make_step(c)
+        round_plane(a, 0, nc.vector.tensor_copy)
         scatter(c)
         neg_turned = psum.tile([P, S], F32, name="neg_turned", tag="neg_turned")
         excess = psum.tile([P, S], F32, name="excess", tag="excess")
@@ -212,8 +225,7 @@ def tile_picked_amsg8_none_po_kernel(
         turn(largest[d], [vmax_turned[:], clipped[:]])
         par_at[d] = fetch("par", d, 1.0, "sec%d" % d)
         rate[d] = place("rate_last", [P, S], F32)[:]
-        nc.scalar.activation(rate[d], largest[d][:], ACT.Abs_reciprocal_sqrt, scale=root_scale[:, 0:1], bias=root_bias[:, 0:1])
-        round_plane(a, 0, nc.vector.tensor_copy)
+        nc.scalar.activation(rate[d], largest[d][:], ACT.Abs_reciprocal_sqrt, scale=last_scale, bias=root_bias[:, 0, 0:1])
         make_step(d)
         round_plane(a, 1, nc.vector.tensor_copy)
         scatter(d)

@@ -155,7 +155,7 @@ def tile_picked_amsg8_none_po_kernel(
             nc.vector.tensor_tensor(moment[a][:, cols], table["sec", a][:].indirect(ent_sb[:, part]), square[a][:, cols], ALU.add)
         for h, (cols, part) in enumerate(halves):
             nc.vector.tensor_tensor(largest[a][:, cols], moment[a][:, cols], vmax_first[:, cols], ALU.max)
-        for t in (b, c, d):
+        for t in (b, c):
             make_square(t, place("square%d" % t, [P, S], F32)[:])
         strip = place("rate_first", [P, 3 * half], F32)
         rate[a], moment[b] = strip[:, half : 3 * half], strip[:, 0:S]
@@ -179,6 +179,7 @@ def tile_picked_amsg8_none_po_kernel(
         vmax_at[c] = fetch("vmax", c, 1.0 / 0.875, "largest%d" % a)
         make_largest(b)
         make_rate(b, place("rate_second", [P, S], F32, tag="vmax%d" % c)[:])
+        make_square(d, place("square%d" % d, [P, S], F32, tag="largest%d" % b)[:])
         moment[c] = place("moment%d" % c, [P, S], F32, tag="step_first")[:]
         nc.vector.tensor_tensor(moment[c], table["sec", c][:].indirect(ent_sb[:]), square[c], ALU.add)
         make_step(b)
@@ -205,8 +206,8 @@ def tile_picked_amsg8_none_po_kernel(
         def round_plane(t, i, copy):
             copy(pairs[i][:, t // 2, :, t % 2], table["par", t][:, chunks[i]])
 
-        vmax_neg = fetch("vmax", d, -1.0 / 0.875, "square%d" % c)
-        rate[c] = place("rate_third", [P, S], F32, tag="vmax%d" % d)[:]
+        vmax_neg = fetch("vmax", d, -1.0 / 0.875, "vmax_first")
+        rate[c] = place("rate_third", [P, S], F32)[:]
         nc.scalar.activation(rate[c], largest[c][:], ACT.Abs_reciprocal_sqrt, scale=third_scale)
         par_at[c] = fetch("par", c, 1.0, "step_first")
         sec_last = fetch("sec", d, 1.0, "largest%d" % c)

@@ -2,7 +2,6 @@ import math
 from contextlib import ExitStack
 
 import concourse.mybir as mybir
-from concourse.masks import make_identity
 
 F32 = mybir.dt.float32
 BF16 = mybir.dt.bfloat16
@@ -19,7 +18,6 @@ PACK = 4
 K, T, S, N, U = 512, 2048, 512, 512, 1024
 FLOPS = 2 * K * S * N
 CHUNK = 256
-PLANE_ORDER = (2, 0, 1, 3)
 
 
 def tile_picked_amsg8_none_po_kernel(
@@ -46,17 +44,6 @@ def tile_picked_amsg8_none_po_kernel(
         nc.gpsimd.memset(one[:, 0:1], 1.0)
         nc.scalar.activation(one[:, 1:2], one[:, 0:1], ACT.Abs_reciprocal_sqrt)
 
-        identity = place("identity", [P, P], F32)
-        make_identity(nc, identity[:])
-
-        first_pairs = place("pairs0", [P, 2, CHUNK, 2], BF16)
-        first_words = first_pairs[:].rearrange("p h c e -> p (h c e)").bitcast(F32)
-        last_scale, third_scale = first_words[:, 0:1], first_words[:, CHUNK : CHUNK + 1]
-        root_bias = late.tile([P, 1, 2048 // 4 + 16], F32, name="root_bias", offset=2048 - 32)
-        nc.gpsimd.memset(last_scale, 4.0 * 0.875)
-        nc.gpsimd.memset(third_scale, 4.0 * 0.875)
-        nc.gpsimd.memset(root_bias[:, 0, 0:1], 0.0)
-
         rows = {name: ap.rearrange("(p t) u -> p t u", t=PACK) for name, ap in (("par", par), ("sec", sec), ("vmax", vmax))}
         out_rows = out_0.rearrange("(p t) u -> p t u", t=PACK)
         table = {(name, t): place("%s%d" % (name, t), [P, U], F32) for name in rows for t in range(PACK)}
@@ -72,21 +59,22 @@ def tile_picked_amsg8_none_po_kernel(
         nc.sync.dma_start(w_raw[:, 2:4, :], w_dealt[:, 2:4, :])
         nc.sync.dma_start(x_table[:], x_words[0].rearrange("p c r -> p (c r)").bitcast(I32))
         nc.sync.dma_start(ent_sb[:], ent)
-        a, b, c, d = PLANE_ORDER
-        order = [("vmax", a), ("sec", a), ("sec", b), ("par", a), ("vmax", b)]
-        order.extend([("par", b), ("vmax", c), ("sec", c), ("vmax", d), ("par", c), ("sec", d), ("par", d)])
+        a, b, c, d = range(PACK)
+        order = [("vmax", a), ("sec", a), ("vmax", b), ("sec", b), ("vmax", c), ("par", a)]
+        order.extend([("sec", c), ("vmax", d), ("par", b), ("sec", d), ("par", c), ("par", d)])
         for name, t in order:
             nc.sync.dma_start(table[name, t][:], rows[name][:, t, :])
 
         half = S // 2
         halves = [(slice(h * half, (h + 1) * half), slice(h * half // 16, (h + 1) * half // 16)) for h in range(2)]
+        whole = [(slice(0, S), slice(0, S // 16))]
         x_picked = place("x_picked", [P, S], U32)
         xs_picked = place("xs_picked", [P, S], U8)
         nc.vector.tensor_copy(xs_picked[:], xs_table[:].indirect(offs_sb[:]))
-        w_codes = {t: place("w_codes%d" % t, [P, P], U32) for t in PLANE_ORDER}
+        w_codes = {t: place("w_codes%d" % t, [P, P], U32) for t in range(PACK)}
         w_scales = place("w_scales", [P, N], U8)
         w_rows = w_raw[:].rearrange("p j (m t) -> p m j t", t=PACK)
-        for i, round_w in ((1, nc.vector.tensor_copy), (0, nc.scalar.copy)):
+        for i, round_w in ((0, nc.vector.tensor_copy), (1, nc.scalar.copy)):
             rounded = place("w_rounded%d" % i, [P, 2 * N], BF16)
             round_w(rounded[:].rearrange("p (t m j) -> p m j t", t=2, j=PACK), w_rows[:, :, :, 2 * i : 2 * i + 2])
             for t in (2 * i, 2 * i + 1):
@@ -118,133 +106,106 @@ def tile_picked_amsg8_none_po_kernel(
             y[t] = psum.tile([P, S], F32, name="y%d" % t, tag="y%d" % t)
             product(y[t][:], t, slice(0, S))
 
-        square, moment, largest, rate, vmax_at, par_at, step = {}, {}, {}, {}, {}, {}, {}
+        square, moment, largest, rate, vmax_at, step, new = {}, {}, {}, {}, {}, {}, {}
+        held = late.tile([P, PACK, S], F32, name="held", offset=0)
 
-        def fetch(name, t, scale, tag):
-            picked = place("%s_at%d" % (name, t), [P, S], F32, tag=tag)
-            nc.scalar.activation(picked[:], table[name, t][:].indirect(ent_sb[:]), ACT.Copy, scale=scale)
-            return picked[:]
+        def values(name, t, tag=None):
+            return place("%s%d" % (name, t), [P, S], F32, tag=tag)[:]
 
         def make_square(t, into):
             square[t] = into
             nc.scalar.activation(into, y[t][:], ACT.Square, scale=math.sqrt(0.125 / 0.875))
 
-        def make_largest(t):
-            largest[t] = place("largest%d" % t, [P, S], F32)
-            nc.vector.tensor_tensor(largest[t][:], moment[t], vmax_at[t], ALU.max)
+        def fetch_vmax(t):
+            vmax_at[t] = values("vmax_at", t)
+            nc.scalar.activation(vmax_at[t], table["vmax", t][:].indirect(ent_sb[:]), ACT.Copy, scale=1.0 / 0.875)
+
+        def make_moment(t, parts):
+            moment[t] = values("moment", t)
+            for cols, part in parts:
+                nc.vector.tensor_tensor(moment[t][:, cols], table["sec", t][:].indirect(ent_sb[:, part]), square[t][:, cols], ALU.add)
+
+        def make_largest(t, parts):
+            largest[t] = values("largest", t)
+            for cols, part in parts:
+                nc.vector.tensor_tensor(largest[t][:, cols], moment[t][:, cols], vmax_at[t][:, cols], ALU.max)
 
         def make_rate(t, into):
             rate[t] = into
-            nc.scalar.activation(into, largest[t][:], ACT.Abs_reciprocal_sqrt, scale=4.0 * 0.875)
+            nc.scalar.activation(into, largest[t], ACT.Abs_reciprocal_sqrt, scale=4.0 * 0.875)
 
-        def make_step(t):
-            step[t] = place("step%d" % t, [P, S], F32)
-            nc.vector.scalar_tensor_tensor(step[t][:], y[t][:], -1.0, rate[t], ALU.mult, ALU.mult)
+        def make_step(t, into):
+            step[t] = into
+            nc.vector.tensor_tensor(into, y[t][:], rate[t], ALU.mult)
 
-        def scatter(t):
-            nc.vector.tensor_tensor(table["par", t][:].indirect(ent_sb[:]), par_at[t], step[t][:], ALU.add)
+        def make_new(t, parts):
+            for cols, part in parts:
+                nc.vector.tensor_tensor(new[t][:, cols], table["par", t][:].indirect(ent_sb[:, part]), step[t][:, cols], ALU.subtract)
+
+        def scatter(t, on_scalar):
+            window = table["par", t][:].indirect(ent_sb[:])
+            if on_scalar:
+                nc.scalar.activation(window, new[t], ACT.Copy)
+            else:
+                nc.vector.tensor_copy(window, new[t])
             nc.sync.dma_start(out_rows[:, t, :], table["par", t][:])
 
-        square[a] = place("square_first", [P, S], F32)
-        moment[a] = place("moment%d" % a, [P, S], F32)
-        largest[a] = place("largest%d" % a, [P, S], F32)
-        vmax_first = place("vmax_first", [P, S], F32)
-        nc.vector.tensor_scalar(vmax_first[:], table["vmax", a][:].indirect(ent_sb[:]), 1.0 / 0.875, 0.0, ALU.mult, ALU.add)
+        vmax_at[a] = values("vmax_at", a)
+        nc.vector.tensor_scalar(vmax_at[a], table["vmax", a][:].indirect(ent_sb[:]), 1.0 / 0.875, 0.0, ALU.mult, ALU.add)
+        square[a] = values("square", a)
         for h, (cols, part) in enumerate(halves):
             nc.scalar.activation(square[a][:, cols], y_first[h][:], ACT.Square, scale=math.sqrt(0.125 / 0.875))
-            nc.vector.tensor_tensor(moment[a][:, cols], table["sec", a][:].indirect(ent_sb[:, part]), square[a][:, cols], ALU.add)
-        for h, (cols, part) in enumerate(halves):
-            nc.vector.tensor_tensor(largest[a][:, cols], moment[a][:, cols], vmax_first[:, cols], ALU.max)
         for t in (b, c):
-            make_square(t, place("square%d" % t, [P, S], F32)[:])
-        strip = place("rate_first", [P, 3 * half], F32)
-        rate[a], moment[b] = strip[:, half : 3 * half], strip[:, 0:S]
-        for cols, part in halves:
-            nc.scalar.activation(rate[a][:, cols], largest[a][:, cols], ACT.Abs_reciprocal_sqrt, scale=4.0 * 0.875)
-        step[a] = place("step_first", [P, S], F32)
-
-        def second_moment(h):
-            cols, part = halves[h]
-            nc.vector.tensor_tensor(moment[b][:, cols], table["sec", b][:].indirect(ent_sb[:, part]), square[b][:, cols], ALU.add)
-
-        second_moment(0)
+            make_square(t, values("square", t))
+        make_moment(a, halves)
+        make_largest(a, halves)
+        fetch_vmax(b)
+        make_rate(a, values("rate", a))
+        strip = place("strip", [P, 3 * half], F32, tag="moment%d" % a)
+        new[b] = strip[:, 0:S]
+        make_square(d, strip[:, half : 3 * half])
+        make_moment(b, whole)
+        step[a] = held[:, 0, :]
         for h, (cols, part) in enumerate(halves):
-            nc.vector.scalar_tensor_tensor(step[a][:, cols], y_first[h][:], -1.0, rate[a][:, cols], ALU.mult, ALU.mult)
-        second_moment(1)
-        par_at[a] = fetch("par", a, 1.0, "moment%d" % a)
-        scatter(a)
-
-        vmax_at[b] = fetch("vmax", b, 1.0 / 0.875, "vmax_first")
-        par_at[b] = fetch("par", b, 1.0, "square%d" % b)
-        vmax_at[c] = fetch("vmax", c, 1.0 / 0.875, "largest%d" % a)
-        make_largest(b)
-        make_rate(b, place("rate_second", [P, S], F32, tag="vmax%d" % c)[:])
-        make_square(d, place("square%d" % d, [P, S], F32, tag="largest%d" % b)[:])
-        moment[c] = place("moment%d" % c, [P, S], F32, tag="step_first")[:]
-        nc.vector.tensor_tensor(moment[c], table["sec", c][:].indirect(ent_sb[:]), square[c], ALU.add)
-        make_step(b)
-        make_largest(c)
-        scatter(b)
-
-        blocks = [slice(k * P, (k + 1) * P) for k in range(S // P)]
-
-        def turn(bank, terms):
-            for i, values in enumerate(terms):
-                for k, block in enumerate(blocks):
-                    nc.tensor.matmul(
-                        bank[:, block],
-                        values[:, block],
-                        identity[:],
-                        start=i == 0 and k == 0,
-                        stop=i == len(terms) - 1 and k == len(blocks) - 1,
-                        is_transpose=True,
-                    )
+            nc.vector.tensor_tensor(step[a][:, cols], y_first[h][:], rate[a][:, cols], ALU.mult)
+        make_largest(b, whole)
+        fetch_vmax(c)
+        make_rate(b, values("rate", b))
+        new[a] = values("new", a)
+        make_new(a, whole)
+        scatter(a, True)
+        make_step(b, held[:, 1, :])
+        make_moment(c, halves)
+        make_largest(c, halves)
+        make_new(b, halves[:1])
+        fetch_vmax(d)
+        make_rate(c, values("rate", c))
+        make_moment(d, whole)
+        make_largest(d, whole)
+        make_new(b, halves[1:])
+        make_rate(d, held[:, 2, :])
+        scatter(b, True)
+        make_step(c, values("step", c, tag="sec%d" % d))
+        make_step(d, held[:, 3, :])
+        for t in (c, d):
+            new[t] = values("new", t)
+            make_new(t, whole)
+        scatter(d, False)
+        scatter(c, True)
 
         chunks = [slice(i * CHUNK, (i + 1) * CHUNK) for i in range(U // CHUNK)]
-        pairs = [first_pairs] + [late.tile([P, 2, CHUNK, 2], BF16, name="pairs%d" % i, offset=2048 * (i - 1)) for i in (1, 2, 3)]
-
-        def round_plane(t, i, copy):
-            copy(pairs[i][:, t // 2, :, t % 2], table["par", t][:, chunks[i]])
-
-        vmax_neg = fetch("vmax", d, -1.0 / 0.875, "vmax_first")
-        rate[c] = place("rate_third", [P, S], F32)[:]
-        nc.scalar.activation(rate[c], largest[c][:], ACT.Abs_reciprocal_sqrt, scale=third_scale)
-        par_at[c] = fetch("par", c, 1.0, "step_first")
-        sec_last = fetch("sec", d, 1.0, "largest%d" % c)
-        make_step(c)
-        round_plane(a, 0, nc.vector.tensor_copy)
-        scatter(c)
-        neg_turned = psum.tile([P, S], F32, name="neg_turned", tag="neg_turned")
-        excess = psum.tile([P, S], F32, name="excess", tag="excess")
-        largest[d] = psum.tile([P, S], F32, name="largest_last", tag="largest_last")
-        turn(neg_turned, [vmax_neg])
-        turn(excess, [vmax_neg, square[d], sec_last])
-        vmax_turned = place("vmax_turned", [P, S], F32, tag="sec%d" % d)
-        nc.scalar.activation(vmax_turned[:], neg_turned[:], ACT.Copy, scale=-1.0)
-        clipped = place("clipped", [P, S], F32)
-        nc.scalar.activation(clipped[:], excess[:], ACT.Relu)
-        turn(largest[d], [vmax_turned[:], clipped[:]])
-        par_at[d] = fetch("par", d, 1.0, "sec%d" % d)
-        rate[d] = place("rate_last", [P, S], F32)[:]
-        nc.scalar.activation(rate[d], largest[d][:], ACT.Abs_reciprocal_sqrt, scale=last_scale, bias=root_bias[:, 0, 0:1])
-        make_step(d)
-        round_plane(a, 1, nc.vector.tensor_copy)
-        scatter(d)
-        for i in (2, 3):
-            round_plane(a, i, nc.scalar.copy)
-        for t in (b, c):
-            for i in range(len(chunks)):
-                round_plane(t, i, nc.scalar.copy)
+        pairs = [late.tile([P, 2, CHUNK, 2], BF16, name="pairs%d" % i, offset=2048 * i) for i in range(len(chunks))]
+        for i, cols in enumerate(chunks):
+            for t in (a, b):
+                nc.gpsimd.tensor_scalar(pairs[i][:, 0, :, t], table["par", t][:, cols], 1.0, -0.0, ALU.mult, ALU.add)
 
         out_codes = place("out_codes", [P, U], U32)
         out_scales = place("out_scales", [P, U], U8)
         grouped = [place("grouped%d" % i, [P, CHUNK * PACK], BF16) for i in range(len(chunks))]
         movers = [(nc.vector.tensor_copy, I32)] * 2 + [(nc.scalar.copy, U32)] * 2
-        for i in (0, 1, 2):
-            round_plane(d, i, movers[i][0])
         for i, (copy, word) in enumerate(movers):
-            if i == 3:
-                round_plane(d, i, copy)
+            for t in (d, c):
+                copy(pairs[i][:, 1, :, t % 2], table["par", t][:, chunks[i]])
             copy(
                 grouped[i][:].bitcast(word).rearrange("p (c h) -> p c h", h=2),
                 pairs[i][:].rearrange("p h c e -> p h (c e)").bitcast(word).rearrange("p h c -> p c h"),

@@ -31,7 +31,7 @@ def tile_picked_amsg8_none_po_kernel(
         psum = ctx.enter_context(tc.psum_pool(name="psum", bufs=1))
 
         def place(name, shape, dtype, tag=None):
-            return keep.tile(shape, dtype, name=name, tag=tag or name, align_bytes=64)
+            return keep.tile(shape, dtype, name=name, tag=tag or name, align_bytes=256)
 
         offs_sb = lists.tile([P, S // 16], U16, name="offs_sb")
         ent_sb = lists.tile([P, S // 16], U16, name="ent_sb")
@@ -60,8 +60,8 @@ def tile_picked_amsg8_none_po_kernel(
         nc.sync.dma_start(x_table[:], x_words[0].rearrange("p c r -> p (c r)").bitcast(I32))
         nc.sync.dma_start(ent_sb[:], ent)
         a, b, c, d = range(PACK)
-        order = [("vmax", a), ("sec", a), ("vmax", b), ("sec", b), ("vmax", c), ("par", a)]
-        order.extend([("sec", c), ("vmax", d), ("par", b), ("sec", d), ("par", c), ("par", d)])
+        order = [("vmax", a), ("sec", a), ("sec", b), ("sec", c), ("vmax", b), ("vmax", c), ("vmax", d)]
+        order.extend([("par", a), ("sec", d), ("par", b), ("par", c), ("par", d)])
         for name, t in order:
             nc.sync.dma_start(table[name, t][:], rows[name][:, t, :])
 
@@ -107,7 +107,7 @@ def tile_picked_amsg8_none_po_kernel(
             product(y[t][:], t, slice(0, S))
 
         square, moment, largest, rate, vmax_at, step, new = {}, {}, {}, {}, {}, {}, {}
-        held = late.tile([P, PACK, S], F32, name="held", offset=0)
+        held = late.tile([P, PACK * S], F32, name="held", offset=0)
 
         def values(name, t, tag=None):
             return place("%s%d" % (name, t), [P, S], F32, tag=tag)[:]
@@ -157,39 +157,37 @@ def tile_picked_amsg8_none_po_kernel(
             nc.scalar.activation(square[a][:, cols], y_first[h][:], ACT.Square, scale=math.sqrt(0.125 / 0.875))
         for t in (b, c):
             make_square(t, values("square", t))
+        make_square(d, held[:, half : 3 * half])
         make_moment(a, halves)
         make_largest(a, halves)
-        fetch_vmax(b)
         make_rate(a, values("rate", a))
-        strip = place("strip", [P, 3 * half], F32, tag="moment%d" % a)
-        new[b] = strip[:, 0:S]
-        make_square(d, strip[:, half : 3 * half])
         make_moment(b, whole)
-        step[a] = held[:, 0, :]
+        step[a] = held[:, 3 * S : 4 * S]
         for h, (cols, part) in enumerate(halves):
             nc.vector.tensor_tensor(step[a][:, cols], y_first[h][:], rate[a][:, cols], ALU.mult)
+        make_moment(c, whole)
+        fetch_vmax(b)
         make_largest(b, whole)
         fetch_vmax(c)
-        make_rate(b, values("rate", b))
-        new[a] = values("new", a)
+        make_largest(c, whole)
+        fetch_vmax(d)
+        make_rate(b, values("rate", b, tag="moment%d" % c))
+        make_rate(c, values("rate", c))
+        for t in range(PACK):
+            new[t] = values("new", t)
         make_new(a, whole)
         scatter(a, True)
-        make_step(b, held[:, 1, :])
-        make_moment(c, halves)
-        make_largest(c, halves)
-        make_new(b, halves[:1])
-        fetch_vmax(d)
-        make_rate(c, values("rate", c))
-        make_moment(d, whole)
+        make_moment(d, halves)
+        make_step(b, held[:, 0:S])
         make_largest(d, whole)
-        make_new(b, halves[1:])
-        make_rate(d, held[:, 2, :])
+        make_rate(d, values("rate", d))
+        make_new(b, whole)
         scatter(b, True)
-        make_step(c, values("step", c, tag="sec%d" % d))
-        make_step(d, held[:, 3, :])
-        for t in (c, d):
-            new[t] = values("new", t)
-            make_new(t, whole)
+        make_step(c, held[:, S : 2 * S])
+        make_step(d, held[:, 2 * S : 3 * S])
+        make_new(c, halves[:1])
+        make_new(d, whole)
+        make_new(c, halves[1:])
         scatter(d, False)
         scatter(c, True)
 

@@ -60,8 +60,8 @@ def tile_picked_amsg8_none_po_kernel(
         nc.sync.dma_start(x_table[:], x_words[0].rearrange("p c r -> p (c r)").bitcast(I32))
         nc.sync.dma_start(ent_sb[:], ent)
         a, b, c, d = range(PACK)
-        order = [("vmax", a), ("sec", a), ("sec", b), ("sec", c), ("vmax", b), ("vmax", c), ("vmax", d)]
-        order.extend([("par", a), ("sec", d), ("par", b), ("par", c), ("par", d)])
+        order = [("vmax", a), ("sec", a), ("vmax", b), ("sec", b), ("vmax", c), ("par", a)]
+        order.extend([("sec", c), ("vmax", d), ("sec", d), ("par", b), ("par", c), ("par", d)])
         for name, t in order:
             nc.sync.dma_start(table[name, t][:], rows[name][:, t, :])
 
@@ -97,13 +97,13 @@ def tile_picked_amsg8_none_po_kernel(
             )
 
         y_first = []
+        y = {t: psum.tile([P, S], F32, name="y%d" % t, tag="y%d" % t) for t in (b, c, d)}
         for h, (tokens, part) in enumerate(halves):
             nc.vector.tensor_copy(x_picked[:, tokens], x_table[:].bitcast(U32).indirect(offs_sb[:, part]))
             y_first.append(psum.tile([P, half], F32, name="y_first%d" % h, tag="y_first%d" % h))
             product(y_first[h][:], a, tokens)
-        y = {}
-        for t in (b, c, d):
-            y[t] = psum.tile([P, S], F32, name="y%d" % t, tag="y%d" % t)
+            product(y[b][:, tokens], b, tokens)
+        for t in (c, d):
             product(y[t][:], t, slice(0, S))
 
         square, moment, largest, rate, vmax_at, step, new = {}, {}, {}, {}, {}, {}, {}
@@ -116,17 +116,17 @@ def tile_picked_amsg8_none_po_kernel(
             square[t] = into
             nc.scalar.activation(into, y[t][:], ACT.Square, scale=math.sqrt(0.125 / 0.875))
 
-        def fetch_vmax(t):
-            vmax_at[t] = values("vmax_at", t)
+        def fetch_vmax(t, into):
+            vmax_at[t] = into
             nc.scalar.activation(vmax_at[t], table["vmax", t][:].indirect(ent_sb[:]), ACT.Copy, scale=1.0 / 0.875)
 
-        def make_moment(t, parts):
-            moment[t] = values("moment", t)
+        def make_moment(t, parts, into):
+            moment[t] = into
             for cols, part in parts:
                 nc.vector.tensor_tensor(moment[t][:, cols], table["sec", t][:].indirect(ent_sb[:, part]), square[t][:, cols], ALU.add)
 
-        def make_largest(t, parts):
-            largest[t] = values("largest", t)
+        def make_largest(t, parts, into):
+            largest[t] = into
             for cols, part in parts:
                 nc.vector.tensor_tensor(largest[t][:, cols], moment[t][:, cols], vmax_at[t][:, cols], ALU.max)
 
@@ -142,12 +142,11 @@ def tile_picked_amsg8_none_po_kernel(
             for cols, part in parts:
                 nc.vector.tensor_tensor(new[t][:, cols], table["par", t][:].indirect(ent_sb[:, part]), step[t][:, cols], ALU.subtract)
 
-        def scatter(t, on_scalar):
-            window = table["par", t][:].indirect(ent_sb[:])
-            if on_scalar:
-                nc.scalar.activation(window, new[t], ACT.Copy)
-            else:
-                nc.vector.tensor_copy(window, new[t])
+        def scatter_on_scalar(t, parts):
+            for cols, part in parts:
+                nc.scalar.activation(table["par", t][:].indirect(ent_sb[:, part]), new[t][:, cols], ACT.Copy)
+
+        def store(t):
             nc.sync.dma_start(out_rows[:, t, :], table["par", t][:])
 
         vmax_at[a] = values("vmax_at", a)
@@ -157,56 +156,68 @@ def tile_picked_amsg8_none_po_kernel(
             nc.scalar.activation(square[a][:, cols], y_first[h][:], ACT.Square, scale=math.sqrt(0.125 / 0.875))
         for t in (b, c):
             make_square(t, values("square", t))
-        make_square(d, held[:, half : 3 * half])
-        make_moment(a, halves)
-        make_largest(a, halves)
+        make_moment(a, halves, held[:, half : 3 * half])
+        make_largest(a, halves, values("largest", a))
+        fetch_vmax(b, values("vmax_at", b))
         make_rate(a, values("rate", a))
-        make_moment(b, whole)
-        step[a] = held[:, 3 * S : 4 * S]
+        make_square(d, held[:, half : 3 * half])
+        make_moment(b, whole, values("moment", b))
+        step[a] = values("step", a)
         for h, (cols, part) in enumerate(halves):
             nc.vector.tensor_tensor(step[a][:, cols], y_first[h][:], rate[a][:, cols], ALU.mult)
-        make_moment(c, whole)
-        fetch_vmax(b)
-        make_largest(b, whole)
-        fetch_vmax(c)
-        make_largest(c, whole)
-        fetch_vmax(d)
-        make_rate(b, values("rate", b, tag="moment%d" % c))
-        make_rate(c, values("rate", c))
-        for t in range(PACK):
+        make_largest(b, whole, values("largest", b))
+        strip = place("strip", [P, 3 * half], F32)
+        fetch_vmax(c, strip[:, half : 3 * half])
+        make_rate(b, values("rate", b))
+        new[a] = strip[:, 0:S]
+        for t in (b, c, d):
             new[t] = values("new", t)
-        make_new(a, whole)
-        scatter(a, True)
-        make_moment(d, halves)
-        make_step(b, held[:, 0:S])
-        make_largest(d, whole)
+        make_new(a, halves[:1])
+        scatter_on_scalar(a, halves[:1])
+        make_step(b, values("step", b))
+        make_moment(c, halves, values("moment", c))
+        make_largest(c, halves, values("largest", c))
+        make_new(a, halves[1:])
+        fetch_vmax(d, values("vmax_at", d))
+        make_rate(c, values("rate", c))
+        scatter_on_scalar(a, halves[1:])
+        store(a)
+        make_moment(d, halves, values("moment", d))
+        make_largest(d, halves, held[:, 3 * S : 4 * S])
         make_rate(d, values("rate", d))
         make_new(b, whole)
-        scatter(b, True)
-        make_step(c, held[:, S : 2 * S])
+        scatter_on_scalar(b, whole)
+        store(b)
+        make_step(c, held[:, 3 * S : 4 * S])
         make_step(d, held[:, 2 * S : 3 * S])
         make_new(c, halves[:1])
         make_new(d, whole)
         make_new(c, halves[1:])
-        scatter(d, False)
-        scatter(c, True)
+        nc.vector.tensor_copy(table["par", d][:].indirect(ent_sb[:]), new[d])
+        store(d)
+        scatter_on_scalar(c, whole)
+        store(c)
 
         chunks = [slice(i * CHUNK, (i + 1) * CHUNK) for i in range(U // CHUNK)]
-        pairs = [late.tile([P, 2, CHUNK, 2], BF16, name="pairs%d" % i, offset=2048 * i) for i in range(len(chunks))]
-        for i, cols in enumerate(chunks):
-            for t in (a, b):
-                nc.gpsimd.tensor_scalar(pairs[i][:, 0, :, t], table["par", t][:, cols], 1.0, -0.0, ALU.mult, ALU.add)
+        paired = late.tile([P, PACK * U], BF16, name="paired", offset=0)
+        pairs = paired[:].rearrange("p (i h c e) -> p i h c e", h=2, c=CHUNK, e=2)
+        for t in (a, b):
+            plane = table["par", t][:].rearrange("p (i c) -> p i c", c=CHUNK)
+            nc.gpsimd.tensor_scalar(pairs[:, :, 0, :, t], plane, 1.0, -0.0, ALU.mult, ALU.add)
 
         out_codes = place("out_codes", [P, U], U32)
         out_scales = place("out_scales", [P, U], U8)
         grouped = [place("grouped%d" % i, [P, CHUNK * PACK], BF16) for i in range(len(chunks))]
         movers = [(nc.vector.tensor_copy, I32)] * 2 + [(nc.scalar.copy, U32)] * 2
+        third = table["par", c][:].rearrange("p (i c) -> p i c", c=CHUNK)
+        for i in (0, 2):
+            movers[i][0](pairs[:, i : i + 2, 1, :, c % 2], third[:, i : i + 2, :])
         for i, (copy, word) in enumerate(movers):
-            for t in (d, c):
-                copy(pairs[i][:, 1, :, t % 2], table["par", t][:, chunks[i]])
+            copy(pairs[:, i, 1, :, d % 2], table["par", d][:, chunks[i]])
+        for i, (copy, word) in enumerate(movers):
             copy(
                 grouped[i][:].bitcast(word).rearrange("p (c h) -> p c h", h=2),
-                pairs[i][:].rearrange("p h c e -> p h (c e)").bitcast(word).rearrange("p h c -> p c h"),
+                paired[:, i * PACK * CHUNK : (i + 1) * PACK * CHUNK].bitcast(word).rearrange("p (h c) -> p c h", h=2),
             )
         words_out = out_1[0].rearrange("p c r -> p (c r)").bitcast(I32)
         for i, cols in enumerate(chunks):

@@ -27,7 +27,6 @@ def tile_picked_amsg8_none_po_kernel(
     with ExitStack() as ctx:
         lists = ctx.enter_context(tc.tile_pool(name="lists", bufs=1))
         keep = ctx.enter_context(tc.tile_pool(name="keep", bufs=1))
-        late = ctx.enter_context(tc.tile_pool(name="late", bufs=1))
         psum = ctx.enter_context(tc.psum_pool(name="psum", bufs=1))
 
         def place(name, shape, dtype, tag=None):
@@ -107,7 +106,8 @@ def tile_picked_amsg8_none_po_kernel(
             product(y[t][:], t, slice(0, S))
 
         square, moment, largest, rate, vmax_at, step, new = {}, {}, {}, {}, {}, {}, {}
-        held = late.tile([P, PACK * S], F32, name="held", offset=0)
+        paired = place("paired", [P, PACK * U], BF16)
+        held = paired[:].bitcast(F32)
 
         def values(name, t, tag=None):
             return place("%s%d" % (name, t), [P, S], F32, tag=tag)[:]
@@ -156,11 +156,11 @@ def tile_picked_amsg8_none_po_kernel(
             nc.scalar.activation(square[a][:, cols], y_first[h][:], ACT.Square, scale=math.sqrt(0.125 / 0.875))
         for t in (b, c):
             make_square(t, values("square", t))
-        make_moment(a, halves, held[:, half : 3 * half])
+        make_moment(a, halves, values("moment", a))
         make_largest(a, halves, values("largest", a))
         fetch_vmax(b, values("vmax_at", b))
         make_rate(a, values("rate", a))
-        make_square(d, held[:, half : 3 * half])
+        make_square(d, values("square", d, tag="moment%d" % a))
         make_moment(b, whole, values("moment", b))
         step[a] = values("step", a)
         for h, (cols, part) in enumerate(halves):
@@ -174,7 +174,7 @@ def tile_picked_amsg8_none_po_kernel(
             new[t] = values("new", t)
         make_new(a, halves[:1])
         scatter_on_scalar(a, halves[:1])
-        make_step(b, values("step", b))
+        make_step(b, held[:, 0:S])
         make_moment(c, halves, values("moment", c))
         make_largest(c, halves, values("largest", c))
         make_new(a, halves[1:])
@@ -183,13 +183,13 @@ def tile_picked_amsg8_none_po_kernel(
         scatter_on_scalar(a, halves[1:])
         store(a)
         make_moment(d, halves, values("moment", d))
-        make_largest(d, halves, held[:, 3 * S : 4 * S])
+        make_largest(d, halves, held[:, 5 * half : 7 * half])
         make_rate(d, values("rate", d))
         make_new(b, whole)
         scatter_on_scalar(b, whole)
         store(b)
-        make_step(c, held[:, 3 * S : 4 * S])
-        make_step(d, held[:, 2 * S : 3 * S])
+        make_step(c, held[:, 5 * half : 7 * half])
+        make_step(d, held[:, 3 * half : 5 * half])
         make_new(c, halves[:1])
         make_new(d, whole)
         make_new(c, halves[1:])
@@ -199,11 +199,10 @@ def tile_picked_amsg8_none_po_kernel(
         store(c)
 
         chunks = [slice(i * CHUNK, (i + 1) * CHUNK) for i in range(U // CHUNK)]
-        paired = late.tile([P, PACK * U], BF16, name="paired", offset=0)
         pairs = paired[:].rearrange("p (i h c e) -> p i h c e", h=2, c=CHUNK, e=2)
-        for t in (a, b):
+        for t, some in ((a, slice(0, 2)), (a, slice(2, 4)), (b, slice(0, 4))):
             plane = table["par", t][:].rearrange("p (i c) -> p i c", c=CHUNK)
-            nc.gpsimd.tensor_scalar(pairs[:, :, 0, :, t], plane, 1.0, -0.0, ALU.mult, ALU.add)
+            nc.gpsimd.tensor_scalar(pairs[:, some, 0, :, t], plane[:, some, :], 1.0, -0.0, ALU.mult, ALU.add)
 
         out_codes = place("out_codes", [P, U], U32)
         out_scales = place("out_scales", [P, U], U8)

@@ -205,28 +205,40 @@ def tile_picked_amsg8_none_po_kernel(
             nc.gpsimd.tensor_scalar(pairs[:, some, 0, :, t], plane[:, some, :], 1.0, -0.0, ALU.mult, ALU.add)
 
         out_codes = place("out_codes", [P, U], U32)
-        out_scales = place("out_scales", [P, U], U8)
-        grouped = [place("grouped%d" % i, [P, CHUNK * PACK], BF16) for i in range(len(chunks))]
-        movers = [(nc.vector.tensor_copy, I32)] * 2 + [(nc.scalar.copy, U32)] * 2
-        third = table["par", c][:].rearrange("p (i c) -> p i c", c=CHUNK)
-        for i in (0, 2):
-            movers[i][0](pairs[:, i : i + 2, 1, :, c % 2], third[:, i : i + 2, :])
-        for i, (copy, word) in enumerate(movers):
-            copy(pairs[:, i, 1, :, d % 2], table["par", d][:, chunks[i]])
-        for i, (copy, word) in enumerate(movers):
+        out_scales = place("out_scales", [P, U // 2], U8)
+        grouped_tile = place("grouped", [P, U * PACK], BF16)
+        grouped = [grouped_tile[:, PACK * cols.start : PACK * cols.stop] for cols in chunks]
+        words_out = out_1[0].rearrange("p c r -> p (c r)").bitcast(I32)
+
+        def join(i, copy, word):
             copy(
-                grouped[i][:].bitcast(word).rearrange("p (c h) -> p c h", h=2),
+                grouped[i].bitcast(word).rearrange("p (c h) -> p c h", h=2),
                 paired[:, i * PACK * CHUNK : (i + 1) * PACK * CHUNK].bitcast(word).rearrange("p (h c) -> p c h", h=2),
             )
-        words_out = out_1[0].rearrange("p c r -> p (c r)").bitcast(I32)
-        for i, cols in enumerate(chunks):
-            nc.vector.quantize_mx(out=out_codes[:, cols].bitcast(FP8X4), scales=out_scales[:, cols], in_=grouped[i][:])
-            if i > 0:
-                ready = slice(0 if i == 1 else cols.start, cols.stop)
-                nc.sync.dma_start(words_out[:, ready], out_codes[:, ready].bitcast(I32))
+
+        def quantise(cols):
+            side = cols.start // (U // 2)
+            nc.vector.quantize_mx(
+                out=out_codes[:, cols].bitcast(FP8X4),
+                scales=out_scales[4 * side : P, cols.start - side * U // 2 : cols.stop - side * U // 2],
+                in_=grouped_tile[:, PACK * cols.start : PACK * cols.stop],
+            )
+            nc.sync.dma_start(words_out[:, cols], out_codes[:, cols].bitcast(I32))
+
+        third = table["par", c][:].rearrange("p (i c) -> p i c", c=CHUNK)
+        for copy, first, some in ((nc.vector.tensor_copy, 0, (0, 1)), (nc.scalar.copy, 2, (3, 2))):
+            copy(pairs[:, first : first + 2, 1, :, c % 2], third[:, first : first + 2, :])
+            for i in some:
+                copy(pairs[:, i, 1, :, d % 2], table["par", d][:, chunks[i]])
+        for i in (0, 1):
+            join(i, nc.vector.tensor_copy, I32)
+        join(2, nc.scalar.copy, U32)
+        join(3, nc.vector.tensor_copy, I32)
+        for cols in (slice(0, U // 2), chunks[3], chunks[2]):
+            quantise(cols)
         for q in range(4):
             queue = nc.scalar if q % 2 == 0 else nc.sync
             queue.dma_start(
-                out_2[0, 4 * q : 4 * q + 4, :].bitcast(I32),
-                out_scales[32 * q : 32 * q + 4, :].bitcast(I32),
+                out_2[0, 4 * q : 4 * q + 4, :].bitcast(I32).rearrange("r (j c) -> j r c", j=2),
+                out_scales[32 * q : 32 * q + 8, :].bitcast(I32),
             )

@@ -47,9 +47,9 @@ def tile_picked_amsg8_none_po_kernel(
         out_rows = out_0.rearrange("(p t) u -> p t u", t=PACK)
         table = {(name, t): place("%s%d" % (name, t), [P, U], F32) for name in rows for t in range(PACK)}
 
-        nc.sync.dma_start(offs_sb[:], offs)
         w_dealt = w1.rearrange("(p j) c -> p j c", j=PACK)
         nc.sync.dma_start(w_raw[:, 0:2, :], w_dealt[:, 0:2, :])
+        nc.sync.dma_start(offs_sb[:], offs)
         for q in range(4):
             nc.sync.dma_start(
                 xs_table[32 * q : 32 * q + 4, :].bitcast(I32),

@@ -223,19 +223,25 @@ def tile_picked_amsg8_none_po_kernel(
                 scales=out_scales[4 * side : P, cols.start - side * U // 2 : cols.stop - side * U // 2],
                 in_=grouped_tile[:, PACK * cols.start : PACK * cols.stop],
             )
+
+        def store_words(cols):
             nc.sync.dma_start(words_out[:, cols], out_codes[:, cols].bitcast(I32))
 
         third = table["par", c][:].rearrange("p (i c) -> p i c", c=CHUNK)
-        for copy, first, some in ((nc.vector.tensor_copy, 0, (0, 1)), (nc.scalar.copy, 2, (3, 2))):
+        for copy, first, some in ((nc.vector.tensor_copy, 0, (0, 1)), (nc.scalar.copy, 2, (2, 3))):
             copy(pairs[:, first : first + 2, 1, :, c % 2], third[:, first : first + 2, :])
             for i in some:
                 copy(pairs[:, i, 1, :, d % 2], table["par", d][:, chunks[i]])
         for i in (0, 1):
             join(i, nc.vector.tensor_copy, I32)
         join(2, nc.scalar.copy, U32)
+        for i in (0, 1):
+            quantise(chunks[i])
+        store_words(slice(0, U // 2))
         join(3, nc.vector.tensor_copy, I32)
-        for cols in (slice(0, U // 2), chunks[3], chunks[2]):
-            quantise(cols)
+        for i in (2, 3):
+            quantise(chunks[i])
+            store_words(chunks[i])
         for q in range(4):
             queue = nc.scalar if q % 2 == 0 else nc.sync
             queue.dma_start(

import math
from contextlib import ExitStack

import concourse.mybir as mybir

F32 = mybir.dt.float32
BF16 = mybir.dt.bfloat16
I32 = mybir.dt.int32
U32 = mybir.dt.uint32
U16 = mybir.dt.uint16
U8 = mybir.dt.uint8
FP8X4 = mybir.dt.float8_e4m3fn_x4
ALU = mybir.AluOpType
ACT = mybir.ActivationFunctionType

P = 128
PACK = 4
K, T, S, N, U = 512, 2048, 512, 512, 1024
FLOPS = 2 * K * S * N
CHUNK = 256


def tile_picked_amsg8_none_po_kernel(
    tc, x_words, x_scales, w1, par, sec, vmax, offs, ent, out_0, out_1, out_2
):
    nc = tc.nc
    with ExitStack() as ctx:
        lists = ctx.enter_context(tc.tile_pool(name="lists", bufs=1))
        keep = ctx.enter_context(tc.tile_pool(name="keep", bufs=1))
        psum = ctx.enter_context(tc.psum_pool(name="psum", bufs=1))

        def place(name, shape, dtype, tag=None):
            return keep.tile(shape, dtype, name=name, tag=tag or name, align_bytes=256)

        offs_sb = lists.tile([P, S // 16], U16, name="offs_sb")
        ent_sb = lists.tile([P, S // 16], U16, name="ent_sb")
        w_raw = place("w_raw", [P, PACK, N], F32)
        x_table = place("x_table", [P, T], I32)
        xs_table = place("xs_table", [P, T], U8)
        nc.gpsimd.memset(xs_table[:].bitcast(I32), 0)

        one = place("one", [P, 2], F32)
        nc.gpsimd.memset(one[:, 0:1], 1.0)
        nc.scalar.activation(one[:, 1:2], one[:, 0:1], ACT.Abs_reciprocal_sqrt)

        rows = {name: ap.rearrange("(p t) u -> p t u", t=PACK) for name, ap in (("par", par), ("sec", sec), ("vmax", vmax))}
        out_rows = out_0.rearrange("(p t) u -> p t u", t=PACK)
        table = {(name, t): place("%s%d" % (name, t), [P, U], F32) for name in rows for t in range(PACK)}

        w_dealt = w1.rearrange("(p j) c -> p j c", j=PACK)
        nc.sync.dma_start(w_raw[:, 0:2, :], w_dealt[:, 0:2, :])
        nc.sync.dma_start(offs_sb[:], offs)
        for q in range(4):
            nc.sync.dma_start(
                xs_table[32 * q : 32 * q + 4, :].bitcast(I32),
                x_scales[0, 4 * q : 4 * q + 4, :].bitcast(I32),
            )
        nc.sync.dma_start(w_raw[:, 2:4, :], w_dealt[:, 2:4, :])
        nc.sync.dma_start(x_table[:], x_words[0].rearrange("p c r -> p (c r)").bitcast(I32))
        nc.sync.dma_start(ent_sb[:], ent)
        a, b, c, d = range(PACK)
        order = [("vmax", a), ("sec", a), ("vmax", b), ("sec", b), ("vmax", c), ("par", a)]
        order.extend([("sec", c), ("vmax", d), ("sec", d), ("par", b), ("par", c), ("par", d)])
        for name, t in order:
            nc.sync.dma_start(table[name, t][:], rows[name][:, t, :])

        half = S // 2
        halves = [(slice(h * half, (h + 1) * half), slice(h * half // 16, (h + 1) * half // 16)) for h in range(2)]
        whole = [(slice(0, S), slice(0, S // 16))]
        x_picked = place("x_picked", [P, S], U32)
        xs_picked = place("xs_picked", [P, S], U8)
        nc.vector.tensor_copy(xs_picked[:], xs_table[:].indirect(offs_sb[:]))
        w_codes = {t: place("w_codes%d" % t, [P, P], U32) for t in range(PACK)}
        w_scales = place("w_scales", [P, N], U8)
        w_rows = w_raw[:].rearrange("p j (m t) -> p m j t", t=PACK)
        for i, round_w in ((0, nc.vector.tensor_copy), (1, nc.scalar.copy)):
            rounded = place("w_rounded%d" % i, [P, 2 * N], BF16)
            round_w(rounded[:].rearrange("p (t m j) -> p m j t", t=2, j=PACK), w_rows[:, :, :, 2 * i : 2 * i + 2])
            for t in (2 * i, 2 * i + 1):
                nc.vector.quantize_mx(
                    out=w_codes[t][:].bitcast(FP8X4),
                    scales=w_scales[:, t * P : (t + 1) * P],
                    in_=rounded[:, (t % 2) * N : (t % 2 + 1) * N],
                )

        def product(bank, t, tokens):
            cols = slice(t * P, (t + 1) * P)
            nc.tensor.matmul_mx(
                out=bank,
                lhsT=w_codes[t][:].bitcast(FP8X4),
                lhsT_scale=w_scales[:, cols],
                rhs=x_picked[:, tokens].bitcast(FP8X4),
                rhs_scale=xs_picked[:, tokens],
                start=True,
                stop=True,
            )

        y_first = []
        y = {t: psum.tile([P, S], F32, name="y%d" % t, tag="y%d" % t) for t in (b, c, d)}
        for h, (tokens, part) in enumerate(halves):
            nc.vector.tensor_copy(x_picked[:, tokens], x_table[:].bitcast(U32).indirect(offs_sb[:, part]))
            y_first.append(psum.tile([P, half], F32, name="y_first%d" % h, tag="y_first%d" % h))
            product(y_first[h][:], a, tokens)
            product(y[b][:, tokens], b, tokens)
        for t in (c, d):
            product(y[t][:], t, slice(0, S))

        square, moment, largest, rate, vmax_at, step, new = {}, {}, {}, {}, {}, {}, {}
        paired = place("paired", [P, PACK * U], BF16)
        held = paired[:].bitcast(F32)

        def values(name, t, tag=None):
            return place("%s%d" % (name, t), [P, S], F32, tag=tag)[:]

        def make_square(t, into):
            square[t] = into
            nc.scalar.activation(into, y[t][:], ACT.Square, scale=math.sqrt(0.125 / 0.875))

        def fetch_vmax(t, into):
            vmax_at[t] = into
            nc.scalar.activation(vmax_at[t], table["vmax", t][:].indirect(ent_sb[:]), ACT.Copy, scale=1.0 / 0.875)

        def make_moment(t, parts, into):
            moment[t] = into
            for cols, part in parts:
                nc.vector.tensor_tensor(moment[t][:, cols], table["sec", t][:].indirect(ent_sb[:, part]), square[t][:, cols], ALU.add)

        def make_largest(t, parts, into):
            largest[t] = into
            for cols, part in parts:
                nc.vector.tensor_tensor(largest[t][:, cols], moment[t][:, cols], vmax_at[t][:, cols], ALU.max)

        def make_rate(t, into):
            rate[t] = into
            nc.scalar.activation(into, largest[t], ACT.Abs_reciprocal_sqrt, scale=4.0 * 0.875)

        def make_step(t, into):
            step[t] = into
            nc.vector.tensor_tensor(into, y[t][:], rate[t], ALU.mult)

        def make_new(t, parts):
            for cols, part in parts:
                nc.vector.tensor_tensor(new[t][:, cols], table["par", t][:].indirect(ent_sb[:, part]), step[t][:, cols], ALU.subtract)

        def scatter_on_scalar(t, parts):
            for cols, part in parts:
                nc.scalar.activation(table["par", t][:].indirect(ent_sb[:, part]), new[t][:, cols], ACT.Copy)

        def store(t):
            nc.sync.dma_start(out_rows[:, t, :], table["par", t][:])

        vmax_at[a] = values("vmax_at", a)
        nc.vector.tensor_scalar(vmax_at[a], table["vmax", a][:].indirect(ent_sb[:]), 1.0 / 0.875, 0.0, ALU.mult, ALU.add)
        square[a] = values("square", a)
        for h, (cols, part) in enumerate(halves):
            nc.scalar.activation(square[a][:, cols], y_first[h][:], ACT.Square, scale=math.sqrt(0.125 / 0.875))
        for t in (b, c):
            make_square(t, values("square", t))
        make_moment(a, halves, values("moment", a))
        make_largest(a, halves, values("largest", a))
        fetch_vmax(b, values("vmax_at", b))
        make_rate(a, values("rate", a))
        make_square(d, values("square", d, tag="moment%d" % a))
        make_moment(b, whole, values("moment", b))
        step[a] = values("step", a)
        for h, (cols, part) in enumerate(halves):
            nc.vector.tensor_tensor(step[a][:, cols], y_first[h][:], rate[a][:, cols], ALU.mult)
        make_largest(b, whole, values("largest", b))
        strip = place("strip", [P, 3 * half], F32)
        fetch_vmax(c, strip[:, half : 3 * half])
        make_rate(b, values("rate", b))
        new[a] = strip[:, 0:S]
        for t in (b, c, d):
            new[t] = values("new", t)
        make_new(a, halves[:1])
        scatter_on_scalar(a, halves[:1])
        make_step(b, held[:, 0:S])
        make_moment(c, halves, values("moment", c))
        make_largest(c, halves, values("largest", c))
        make_new(a, halves[1:])
        fetch_vmax(d, values("vmax_at", d))
        make_rate(c, values("rate", c))
        scatter_on_scalar(a, halves[1:])
        store(a)
        make_moment(d, halves, values("moment", d))
        make_largest(d, halves, held[:, 5 * half : 7 * half])
        make_rate(d, values("rate", d))
        make_new(b, whole)
        scatter_on_scalar(b, whole)
        store(b)
        make_step(c, held[:, 5 * half : 7 * half])
        make_step(d, held[:, 3 * half : 5 * half])
        make_new(c, halves[:1])
        make_new(d, whole)
        make_new(c, halves[1:])
        nc.vector.tensor_copy(table["par", d][:].indirect(ent_sb[:]), new[d])
        store(d)
        scatter_on_scalar(c, whole)
        store(c)

        chunks = [slice(i * CHUNK, (i + 1) * CHUNK) for i in range(U // CHUNK)]
        pairs = paired[:].rearrange("p (i h c e) -> p i h c e", h=2, c=CHUNK, e=2)
        for t, some in ((a, slice(0, 2)), (a, slice(2, 4)), (b, slice(0, 4))):
            plane = table["par", t][:].rearrange("p (i c) -> p i c", c=CHUNK)
            nc.gpsimd.tensor_scalar(pairs[:, some, 0, :, t], plane[:, some, :], 1.0, -0.0, ALU.mult, ALU.add)

        out_codes = place("out_codes", [P, U], U32)
        out_scales = place("out_scales", [P, U // 2], U8)
        grouped_tile = place("grouped", [P, U * PACK], BF16)
        grouped = [grouped_tile[:, PACK * cols.start : PACK * cols.stop] for cols in chunks]
        words_out = out_1[0].rearrange("p c r -> p (c r)").bitcast(I32)

        def join(i, copy, word):
            copy(
                grouped[i].bitcast(word).rearrange("p (c h) -> p c h", h=2),
                paired[:, i * PACK * CHUNK : (i + 1) * PACK * CHUNK].bitcast(word).rearrange("p (h c) -> p c h", h=2),
            )

        def quantise(cols):
            side = cols.start // (U // 2)
            nc.vector.quantize_mx(
                out=out_codes[:, cols].bitcast(FP8X4),
                scales=out_scales[4 * side : P, cols.start - side * U // 2 : cols.stop - side * U // 2],
                in_=grouped_tile[:, PACK * cols.start : PACK * cols.stop],
            )

        def store_words(cols):
            nc.sync.dma_start(words_out[:, cols], out_codes[:, cols].bitcast(I32))

        third = table["par", c][:].rearrange("p (i c) -> p i c", c=CHUNK)
        for copy, first, some in ((nc.vector.tensor_copy, 0, (0, 1)), (nc.scalar.copy, 2, (2, 3))):
            copy(pairs[:, first : first + 2, 1, :, c % 2], third[:, first : first + 2, :])
            for i in some:
                copy(pairs[:, i, 1, :, d % 2], table["par", d][:, chunks[i]])
        for i in (0, 1):
            join(i, nc.vector.tensor_copy, I32)
        join(2, nc.scalar.copy, U32)
        for i in (0, 1):
            quantise(chunks[i])
        store_words(slice(0, U // 2))
        join(3, nc.vector.tensor_copy, I32)
        for i in (2, 3):
            quantise(chunks[i])
            store_words(chunks[i])
        for q in range(4):
            queue = nc.scalar if q % 2 == 0 else nc.sync
            queue.dma_start(
                out_2[0, 4 * q : 4 * q + 4, :].bitcast(I32).rearrange("r (j c) -> j r c", j=2),
                out_scales[32 * q : 32 * q + 8, :].bitcast(I32),
            )
